import numpy as np
import ml_dtypes


def mxq(x, axis, fmt="e4m3"):
    dtype, down = {"e4m3": (ml_dtypes.float8_e4m3fn, 7), "e5m2": (ml_dtypes.float8_e5m2, 14)}[fmt]
    v = np.moveaxis(np.asarray(x, np.float32).astype(ml_dtypes.bfloat16).astype(np.float64), axis, -1)
    blocks = v.reshape(v.shape[:-1] + (-1, 32))
    amax = np.abs(blocks).max(-1, keepdims=True)
    byte = np.maximum(np.where(amax > 0, np.frexp(amax)[1] - 1 + 127, 0) - down, 1)
    scale = np.exp2(byte - 127.0)
    codes = (blocks / scale).astype(np.float32).astype(dtype).astype(np.float64)
    return np.moveaxis((codes * scale).reshape(v.shape), -1, axis)


WIDE = False


def mx_kscale(k):
    if not WIDE:
        return np.ones(k)
    levels = np.array([10, -10, 5, -5, 0])
    if k % 512:
        return np.exp2(np.random.permutation(np.resize(levels, k // 32))).repeat(32)
    a = np.empty((k // 512, 16))
    for p in range(k // 512):
        a[p, :8] = np.random.permutation(np.resize(levels, 8))
        for g in range(8):
            far = levels[np.abs(levels - a[p, g]) >= 10]
            a[p, g + 8] = far[np.random.randint(len(far))]
    return np.exp2(a.ravel()).repeat(32)


def f64(x):
    return np.asarray(x).astype(np.float64)


def striped(idx):
    return np.tile(idx.reshape(-1, 16).T, (8, 1)).astype(np.uint16)


def unstriped(offs):
    return offs[:16].T.reshape(-1).astype(np.int64)


E2M1 = np.array([0.0, 0.5, 1.0, 1.5, 2.0, 3.0, 4.0, 6.0, -0.0, -0.5, -1.0, -1.5, -2.0, -3.0, -4.0, -6.0])


def pack_weight(w, fmt):
    k, n = w.shape
    w = f64(np.asarray(w, np.float32).astype(ml_dtypes.bfloat16)).reshape(k // 32, 32, n)
    amax = np.abs(w).max(1)
    if fmt == "e4m3":
        byte = np.frexp(amax)[1] - 1 + 127 - 7
    else:
        mant, ex = np.frexp(amax / 6.0)
        byte = np.where(mant > 0.5, ex, ex - 1) + 127
    byte = np.clip(np.where(amax > 0, byte, 1), 1, 254)
    scaled = (w * np.exp2(127.0 - byte)[:, None, :]).reshape(k, n).astype(np.float32)
    by_word = np.ascontiguousarray(scaled.reshape(k // 512, 128, 4, n).transpose(0, 1, 3, 2))
    if fmt == "e4m3":
        words = by_word.astype(ml_dtypes.float8_e4m3fn).view(np.uint8)
    else:
        c = by_word.astype(ml_dtypes.float4_e2m1fn).view(np.uint8) & 0xF
        words = (c[..., 0::2] | (c[..., 1::2] << 4)).reshape(k // 512, 128, 2 * n)
    return np.ascontiguousarray(words), np.ascontiguousarray(byte.astype(np.uint8).reshape(k // 512, 16, n))


def unpack_weight(words, scales, fmt):
    g, _, n = scales.shape
    words = np.ascontiguousarray(words).reshape(g, 128, n, -1)
    if fmt == "e4m3":
        vals = words.view(ml_dtypes.float8_e4m3fn).astype(np.float64)
    else:
        nib = np.empty((g, 128, n, 4), np.uint8)
        nib[..., 0::2] = words & 0xF
        nib[..., 1::2] = words >> 4
        vals = E2M1[nib]
    vals = vals * np.repeat(np.exp2(scales.astype(np.float64) - 127.0), 8, axis=1)[..., None]
    return vals.transpose(0, 1, 3, 2).reshape(g * 512, n)


def gelu(v):
    return 0.5 * v * (1.0 + np.tanh(np.sqrt(2.0 / np.pi) * (v + 0.044715 * v**3)))


K, K2, H, N, T, S = 1024, 512, 1024, 512, 4096, 1024

def setup_inputs():
    n = np.random.standard_normal
    s = mx_kscale(K)[:, None]
    s2 = mx_kscale(K2)[:, None]
    u = mx_kscale(H)[:, None]
    tab_words, tab_scales = pack_weight(n((K, T)) * s, "e4m3")
    w2_words, w2_scales = pack_weight(0.23 * n((K2, H)) / np.sqrt(K2) / s2, "e2m1")
    w3_words, w3_scales = pack_weight(n((H, N)) / np.sqrt(H) / u, "e4m3")
    return {
        "tab_words": tab_words, "tab_scales": tab_scales,
        "offs": striped(np.random.permutation(T)[:S]),
        "w1": (0.28 * n((K, H)) / np.sqrt(K) / s).astype(np.float32),
        "stress": (n((K2, S)) * s2).astype(np.float32),
        "w2_words": w2_words, "w2_scales": w2_scales,
        "phase": np.random.uniform(0.4, 0.9, H).astype(np.float32),
        "gain": (np.random.uniform(0.5, 1.5, H) * u[:, 0]).astype(np.float32),
        "w3_words": w3_words, "w3_scales": w3_scales,
        "offs2": striped(np.random.permutation(S)),
        "wgo": np.exp(0.3 * n((128, S))).astype(np.float32),
        "x0": n((N, S)).astype(np.float32),
    }

def reference(tab_words, tab_scales, offs, w1, stress, w2_words, w2_scales, phase, gain,
              w3_words, w3_scales, offs2, wgo, x0):
    v = unpack_weight(tab_words, tab_scales, "e4m3")[:, unstriped(offs)]
    w2 = unpack_weight(w2_words, w2_scales, "e2m1")
    w3 = unpack_weight(w3_words, w3_scales, "e4m3")
    arg = mxq(f64(w1), 0, "e4m3").T @ v + w2.T @ mxq(f64(stress), 0, "e4m3")
    h = np.cos(arg + f64(phase)[:, None]) * f64(gain)[:, None]
    y = w3.T @ mxq(h, 0, "e4m3")
    page = np.zeros((N, S))
    page[:, unstriped(offs2)] = np.tile(f64(wgo), (N // 128, 1)) * y
    return np.abs(page - f64(x0))

@@ -1,0 +1,292 @@
+import math
+from contextlib import ExitStack
+
+import concourse.mybir as mybir
+
+K, K2, H, N, T, S = 1024, 512, 1024, 512, 4096, 1024
+FLOPS = 2 * (K + K2) * H * S + 2 * H * N * S
+
+F32 = mybir.dt.float32
+BF16 = mybir.dt.bfloat16
+I32 = mybir.dt.int32
+U32 = mybir.dt.uint32
+U16 = mybir.dt.uint16
+U8 = mybir.dt.uint8
+FP8X4 = mybir.dt.float8_e4m3fn_x4
+FP4X4 = mybir.dt.float4_e2m1fn_x4
+ALU = mybir.AluOpType
+ACT = mybir.ActivationFunctionType
+
+P = 128
+W = 256
+CH = S // W
+TWO_PI = 2.0 * math.pi
+TURN_OFFSET = 1.0
+V_K_UNITS = 3
+V_GAIN_UNITS = 3
+V_IL_UNITS = 8
+
+
+def tile_list_morton_grain_corrections_kernel(
+    tc, tab_words, tab_scales, offs, w1, stress, w2_words, w2_scales, phase, gain,
+    w3_words, w3_scales, offs2, wgo, x0, out,
+):
+    nc = tc.nc
+    with ExitStack() as ctx:
+        keep = ctx.enter_context(tc.tile_pool(name="keep", bufs=1))
+        ring = ctx.enter_context(tc.tile_pool(name="ring", bufs=3))
+        psum = ctx.enter_context(tc.psum_pool(name="psum", bufs=1))
+
+        def kt(name, shape, dt):
+            return keep.tile(shape, dt, name=name, align_bytes=64)
+
+        offs_t = kt("offs_t", [P, S // 16], U16)
+        offs2_t = kt("offs2_t", [P, S // 16], U16)
+        tab_w = [kt("tab_w%d" % a, [P, T], U32) for a in range(2)]
+        tab_s = kt("tab_s", [P, T], U8)
+        w2_raw = kt("w2_raw", [P, 2 * H], U8)
+        w2s_raw = kt("w2s_raw", [P, H], U8)
+        w2_c = kt("w2_c", [P, 2 * H], U8)
+        w2_s = kt("w2_s", [P, H], U8)
+        w3_c = kt("w3_c", [P, 2, N], U32)
+        w3_s = kt("w3_s", [P, N], U8)
+        ph_raw = kt("ph_raw", [P, 2, 4], F32)
+        ph = kt("ph", [P, 2, 4], F32)
+        gn = kt("gn", [P, 2, 4], F32)
+        wgo_t = kt("wgo_t", [P, S], F32)
+        x0_t = [kt("x0_t%d" % n, [P, S], F32) for n in range(4)]
+        w1_raw = {(a, g): kt("w1_raw%d%d" % (a, g), [P, 4, 512], F32) for a in range(2) for g in range(2)}
+        st_raw = [kt("st_raw%d" % c, [P, 4, W], F32) for c in range(CH)]
+        zero = kt("zero", [P, 1], F32)
+        zero_b = kt("zero_b", [P, 1], F32)
+
+        nc.vector.memset(zero[:], 0.0)
+        nc.scalar.activation(zero_b[:], zero[:], ACT.Sin)
+        nc.vector.memset(w2s_raw[:].bitcast(I32), 0)
+        nc.vector.memset(tab_s[:].bitcast(I32), 0)
+        nc.vector.memset(w3_s[:].bitcast(I32), 0)
+
+        def load_w1(a, g):
+            nc.sync.dma_start(out=w1_raw[a, g][:], in_=w1[512 * g : 512 * (g + 1), 512 * a : 512 * (a + 1)].rearrange("(p j) c -> p j c", j=4))
+
+        def load_tab(g):
+            nc.sync.dma_start(out=tab_w[g][:].bitcast(I32), in_=tab_words[g].rearrange("p n t -> p (n t)").bitcast(I32))
+
+        def load_stress(c):
+            nc.sync.dma_start(out=st_raw[c][:], in_=stress[:, W * c : W * (c + 1)].rearrange("(p j) c -> p j c", j=4))
+
+        def load_tab_s(g, q):
+            nc.sync.dma_start(out=tab_s[32 * q + 4 * g : 32 * q + 4 * g + 4, :].bitcast(I32), in_=tab_scales[g, 4 * q : 4 * q + 4, :].bitcast(I32))
+
+        nc.sync.dma_start(out=w2_raw[:].bitcast(I32), in_=w2_words[0].bitcast(I32))
+        nc.sync.dma_start(offs_t[:], offs)
+        load_w1(0, 0)
+        for q in range(4):
+            nc.sync.dma_start(out=w2s_raw[32 * q : 32 * q + 4, :].bitcast(I32), in_=w2_scales[0, 4 * q : 4 * q + 4, :].bitcast(I32))
+        load_tab(0)
+        load_w1(0, 1)
+        for q in range(4):
+            load_tab_s(0, q)
+        load_tab_s(1, 0)
+        load_tab_s(1, 1)
+        load_stress(0)
+        load_tab_s(1, 2)
+        load_tab_s(1, 3)
+        load_tab(1)
+        nc.sync.dma_start(out=ph_raw[:], in_=phase.rearrange("(a p t) -> p a t", a=2, t=4))
+        nc.sync.dma_start(out=gn[:], in_=gain.rearrange("(a p t) -> p a t", a=2, t=4))
+        load_w1(1, 0)
+        load_w1(1, 1)
+        load_stress(1)
+        nc.sync.dma_start(out=w3_c[:].bitcast(I32), in_=w3_words.rearrange("a p n t -> p a (n t)").bitcast(I32))
+        for q in range(4):
+            nc.sync.dma_start(out=w3_s[32 * q : 32 * q + 8, :].bitcast(I32), in_=w3_scales[:, 4 * q : 4 * q + 4, :].bitcast(I32))
+        nc.sync.dma_start(offs2_t[:], offs2)
+        nc.sync.dma_start(out=wgo_t[:], in_=wgo)
+        load_stress(2)
+        load_stress(3)
+        for n in range(4):
+            nc.sync.dma_start(out=x0_t[n][:], in_=x0[P * n : P * (n + 1), :])
+
+        nc.vector.tensor_copy(
+            out=w2_c[:].rearrange("p (a t m b) -> p a t m b", a=2, t=4, b=2),
+            in_=w2_raw[:].rearrange("p (a m t b) -> p a t m b", a=2, t=4, b=2),
+        )
+        nc.vector.tensor_copy(
+            out=w2_s[:].rearrange("p (a t m) -> p a t m", a=2, t=4),
+            in_=w2s_raw[:].rearrange("p (a m t) -> p a t m", a=2, t=4),
+        )
+
+        w1_c, w1_s = {}, {}
+
+        def cast(eng, o, i):
+            if eng == "v":
+                nc.vector.tensor_copy(out=o, in_=i)
+            else:
+                nc.scalar.copy(out=o, in_=i)
+
+        def prep_w1(a, g, eng):
+            grouped = ring.tile([P, 2048], BF16, name="w1_b", align_bytes=64, bufs=2)
+            cast(eng, grouped[:].rearrange("p (t m j) -> p m j t", t=4, j=4), w1_raw[a, g][:].rearrange("p j (m t) -> p m j t", t=4))
+            w1_c[a, g] = kt("w1_c%d%d" % (a, g), [P, 512], U32)
+            w1_s[a, g] = kt("w1_s%d%d" % (a, g), [P, 512], U8)
+            nc.vector.quantize_mx(out=w1_c[a, g][:].bitcast(FP8X4), scales=w1_s[a, g][:], in_=grouped[:])
+
+        st_c, st_s = {}, {}
+
+        def prep_stress(c, eng):
+            grouped = ring.tile([P, 4 * W], BF16, name="st_b", align_bytes=64, bufs=2)
+            cast(eng, grouped[:].rearrange("p (c i j) -> p c j i", i=4, j=4), st_raw[c][:].rearrange("p j (c i) -> p c j i", i=4))
+            st_c[c] = kt("st_c%d" % c, [P, W], U32)
+            st_s[c] = kt("st_s%d" % c, [P, W], U8)
+            nc.vector.quantize_mx(out=st_c[c][:].bitcast(FP8X4), scales=st_s[c][:], in_=grouped[:])
+
+        g_w, g_s = {}, {}
+
+        def gather_words(g, half):
+            g_w[g, half] = kt("g_w%d%d" % (g, half), [P, 512], U32)
+            nc.vector.tensor_copy(g_w[g, half][:], tab_w[g][:].indirect(offs_t[:, 32 * half : 32 * (half + 1)]))
+
+        def gather_scales(half):
+            g_s[half] = kt("g_s%d" % half, [P, 512], U8)
+            nc.vector.tensor_copy(g_s[half][:], tab_s[:].indirect(offs_t[:, 32 * half : 32 * (half + 1)]))
+
+        prep_w1(0, 0, "s")
+        gather_words(0, 0)
+        gather_words(0, 1)
+        prep_w1(0, 1, "s")
+        gather_scales(0)
+        prep_stress(0, "s")
+        gather_words(1, 0)
+        nc.vector.tensor_scalar(ph[:], ph_raw[:], 1.0 / TWO_PI, TURN_OFFSET, ALU.mult, ALU.add)
+
+        h_c, h_s, u_t, k_t, hb_t = {}, {}, {}, {}, {}
+        y_t = [kt("y_t%d" % n, [P, S], F32) for n in range(4)]
+        page = [kt("page%d" % n, [P, S], F32) for n in range(4)]
+        units = [(c, a) for c in range(CH) for a in range(2)]
+
+        def unit_mm(i):
+            c, a = units[i]
+            half, cols = c // 2, slice(W * (c % 2), W * (c % 2 + 1))
+            u_t[i] = ring.tile([P, 4, W], F32, name="u")
+            for pair in range(2):
+                bank = psum.tile([P, 2, W], F32, name="s1_%d" % pair, bufs=3)
+                for tt in range(2):
+                    t = 2 * pair + tt
+                    m = slice(P * t, P * (t + 1))
+                    nc.tensor.matmul_mx(
+                        out=bank[:, tt, :], lhsT=w1_c[a, 0][:, m].bitcast(FP8X4), lhsT_scale=w1_s[a, 0][:, m],
+                        rhs=g_w[0, half][:, cols].bitcast(FP8X4), rhs_scale=g_s[half][:, cols], start=True, stop=False)
+                    col0 = 512 * a + P * t
+                    for e in range(W // P):
+                        nc.tensor.matmul_mx(
+                            out=bank[:, tt, P * e : P * (e + 1)], lhsT=w2_c[:, 2 * col0 : 2 * (col0 + P)].bitcast(FP4X4),
+                            lhsT_scale=w2_s[:, col0 : col0 + P],
+                            rhs=st_c[c][:, P * e : P * (e + 1)].bitcast(FP8X4), rhs_scale=st_s[c][:, P * e : P * (e + 1)],
+                            start=False, stop=False)
+                    nc.tensor.matmul_mx(
+                        out=bank[:, tt, :], lhsT=w1_c[a, 1][:, m].bitcast(FP8X4), lhsT_scale=w1_s[a, 1][:, m],
+                        rhs=g_w[1, half][:, cols].bitcast(FP8X4), rhs_scale=g_s[half][4:P, cols], start=False, stop=True)
+                for tt in range(2):
+                    t = 2 * pair + tt
+                    nc.scalar.activation(u_t[i][:, t, :], bank[:, tt, :], ACT.Abs, bias=ph[:, a, t : t + 1], scale=1.0 / TWO_PI)
+
+        def unit_k(i):
+            u = u_t[i][:].rearrange("p t n -> p (t n)")
+            k_t[i] = ring.tile([P, 4 * W], I32, name="k", bufs=2)
+            if i < V_K_UNITS:
+                nc.vector.tensor_scalar(k_t[i][:], u, -0.25, None, ALU.add)
+            else:
+                nc.scalar.activation(k_t[i][:].bitcast(U32), u, ACT.Copy, bias=-0.25)
+
+        def unit_f(i):
+            u = u_t[i][:].rearrange("p t n -> p (t n)")
+            nc.vector.tensor_tensor(u, u, k_t[i][:], ALU.subtract)
+
+        def unit_sin(i):
+            c, a = units[i]
+            u = u_t[i][:].rearrange("p t n -> p (t n)")
+            nc.scalar.activation(u, u, ACT.Sin, bias=math.pi / 2, scale=-TWO_PI)
+            hb_t[i] = ring.tile([P, 4, W], BF16, name="hb", bufs=2)
+            for t in range(4):
+                if i < V_GAIN_UNITS:
+                    nc.vector.tensor_scalar(hb_t[i][:, t, :], u_t[i][:, t, :], gn[:, a, t : t + 1], None, ALU.mult)
+                else:
+                    nc.scalar.activation(hb_t[i][:, t, :], u_t[i][:, t, :], ACT.Copy, scale=gn[:, a, t : t + 1])
+
+        def unit_q(i):
+            c, a = units[i]
+            grouped = ring.tile([P, 4 * W], BF16, name="h_b", align_bytes=64, bufs=2)
+            cast("v" if i < V_IL_UNITS else "s", grouped[:].rearrange("p (c i t) -> p c t i", i=4, t=4), hb_t[i][:].rearrange("p t (c i) -> p c t i", i=4))
+            h_c[c, a] = ring.tile([P, W], U32, name="h_c", align_bytes=64, bufs=4)
+            h_s[c, a] = ring.tile([P, W], U8, name="h_s", align_bytes=64, bufs=4)
+            nc.vector.quantize_mx(out=h_c[c, a][:].bitcast(FP8X4), scales=h_s[c, a][:], in_=grouped[:])
+
+        y_bank = {}
+
+        def stage2(c):
+            for pair in range(2):
+                y_bank[c, pair] = psum.tile([P, 2, W], F32, name="s2_%d" % pair)
+                for nn in range(2):
+                    n = 2 * pair + nn
+                    m = slice(P * n, P * (n + 1))
+                    for a in range(2):
+                        nc.tensor.matmul_mx(
+                            out=y_bank[c, pair][:, nn, :], lhsT=w3_c[:, a, m].bitcast(FP8X4), lhsT_scale=w3_s[4 * a : P, m],
+                            rhs=h_c[c, a][:].bitcast(FP8X4), rhs_scale=h_s[c, a][:], start=(a == 0), stop=(a == 1))
+
+        def y_out(c, n):
+            nc.scalar.copy(out=y_t[n][:, W * c : W * (c + 1)], in_=y_bank[c, n // 2][:, n % 2, :])
+
+        def scatter(c0, c1, n):
+            cols = slice(W * c0, W * c1)
+            nc.vector.tensor_tensor(page[n][:].indirect(offs2_t[:, W * c0 // 16 : W * c1 // 16]), y_t[n][:, cols], wgo_t[:, cols], ALU.mult)
+
+        def finish(n):
+            for half in range(2):
+                cols = slice(512 * half, 512 * (half + 1))
+                nc.vector.tensor_tensor(x0_t[n][:, cols], page[n][:, cols], x0_t[n][:, cols], ALU.subtract)
+                nc.scalar.activation(x0_t[n][:, cols], x0_t[n][:, cols], ACT.Abs, bias=zero_b[:])
+                nc.sync.dma_start(out=out[P * n : P * (n + 1), cols], in_=x0_t[n][:, cols])
+
+
+        unit_mm(0)
+        unit_k(0)
+        unit_f(0)
+        prep_w1(1, 0, "s")
+        unit_sin(0)
+        unit_q(0)
+        prep_w1(1, 1, "v")
+        gather_words(1, 1)
+        gather_scales(1)
+        unit_mm(1)
+        prep_stress(1, "s")
+        unit_k(1)
+        unit_f(1)
+        unit_mm(2)
+        unit_sin(1)
+        unit_q(1)
+        stage2(0)
+        pend = [(c, n) for c in range(3) for n in range(4)]
+        for i in range(2, 8):
+            c, a = units[i]
+            unit_k(i)
+            unit_f(i)
+            cc, n = pend[2 * (i - 2)]
+            y_out(cc, n)
+            scatter(cc, cc + 1, n)
+            if i + 1 < 8:
+                if a == 1:
+                    prep_stress(c + 1, "s")
+                unit_mm(i + 1)
+            unit_sin(i)
+            unit_q(i)
+            cc, n = pend[2 * (i - 2) + 1]
+            y_out(cc, n)
+            scatter(cc, cc + 1, n)
+            if a == 1:
+                stage2(c)
+        for n in range(4):
+            y_out(3, n)
+            scatter(3, 4, n)
+            finish(n)

@@ -2,6 +2,7 @@ import math
 from contextlib import ExitStack
 
 import concourse.mybir as mybir
+from concourse.masks import make_identity
 
 K, K2, H, N, T, S = 1024, 512, 1024, 512, 4096, 1024
 FLOPS = 2 * (K + K2) * H * S + 2 * H * N * S
@@ -18,13 +19,21 @@ ALU = mybir.AluOpType
 ACT = mybir.ActivationFunctionType
 
 P = 128
+PACK = 4
+PASS = P * PACK
+BANK = 512
+LIST = 16
 W = 256
-CH = S // W
+CHUNKS = S // W
+TILES = N // P
+UNITS = [(c, a) for c in range(CHUNKS) for a in range(H // PASS)]
 TWO_PI = 2.0 * math.pi
-TURN_OFFSET = 1.0
-V_K_UNITS = 3
-V_GAIN_UNITS = 3
-V_IL_UNITS = 8
+
+TURNS_ON_VECTOR = 4
+GAIN_ON_VECTOR = 5
+WEAVE_ON_SCALAR_FROM = 6
+FIRST_SCATTER_PLACE = 7
+EARLY_TILES = 2
 
 
 def tile_list_morton_grain_corrections_kernel(
@@ -34,259 +43,340 @@ def tile_list_morton_grain_corrections_kernel(
     nc = tc.nc
     with ExitStack() as ctx:
         keep = ctx.enter_context(tc.tile_pool(name="keep", bufs=1))
-        ring = ctx.enter_context(tc.tile_pool(name="ring", bufs=3))
+        ring = ctx.enter_context(tc.tile_pool(name="ring", bufs=2))
         psum = ctx.enter_context(tc.psum_pool(name="psum", bufs=1))
 
-        def kt(name, shape, dt):
-            return keep.tile(shape, dt, name=name, align_bytes=64)
+        def held(name, shape, dtype):
+            return keep.tile(shape, dtype, name=name, align_bytes=64)
 
-        offs_t = kt("offs_t", [P, S // 16], U16)
-        offs2_t = kt("offs2_t", [P, S // 16], U16)
-        tab_w = [kt("tab_w%d" % a, [P, T], U32) for a in range(2)]
-        tab_s = kt("tab_s", [P, T], U8)
-        w2_raw = kt("w2_raw", [P, 2 * H], U8)
-        w2s_raw = kt("w2s_raw", [P, H], U8)
-        w2_c = kt("w2_c", [P, 2 * H], U8)
-        w2_s = kt("w2_s", [P, H], U8)
-        w3_c = kt("w3_c", [P, 2, N], U32)
-        w3_s = kt("w3_s", [P, N], U8)
-        ph_raw = kt("ph_raw", [P, 2, 4], F32)
-        ph = kt("ph", [P, 2, 4], F32)
-        gn = kt("gn", [P, 2, 4], F32)
-        wgo_t = kt("wgo_t", [P, S], F32)
-        x0_t = [kt("x0_t%d" % n, [P, S], F32) for n in range(4)]
-        w1_raw = {(a, g): kt("w1_raw%d%d" % (a, g), [P, 4, 512], F32) for a in range(2) for g in range(2)}
-        st_raw = [kt("st_raw%d" % c, [P, 4, W], F32) for c in range(CH)]
-        zero = kt("zero", [P, 1], F32)
-        zero_b = kt("zero_b", [P, 1], F32)
+        def arg_bank(shape):
+            return psum.tile(shape, F32, name="arg_bank", bufs=6)
+
+        def cast(on_vector, dst, src):
+            if on_vector:
+                nc.vector.tensor_copy(out=dst, in_=src)
+            else:
+                nc.scalar.copy(out=dst, in_=src)
+
+        offs_t = held("offs_t", [P, S // LIST], U16)
+        offs2_t = held("offs2_t", [P, S // LIST], U16)
+        tab_w = [held("tab_w%d" % g, [P, T], U32) for g in range(2)]
+        tab_s = held("tab_s", [P, T], U8)
+        picked_rows = held("picked_rows", [P, S], U8)
+        v_s = held("v_s", [P, 2 * S], U8)
+        w2_raw = held("w2_raw", [P, 2 * H], U8)
+        w2s_raw = held("w2s_raw", [P, H], U8)
+        w2_c = held("w2_c", [P, 2 * H], U8)
+        w2_s = held("w2_s", [P, H], U8)
+        w3_c = held("w3_c", [P, 2, N], U32)
+        w3_s = held("w3_s", [P, N], U8)
+        phase_t = held("phase_t", [P, 2, PACK], F32)
+        phase_turns = held("phase_turns", [P, 2, PACK], F32)
+        gain_t = held("gain_t", [P, 2, PACK], F32)
+        wgo_t = held("wgo_t", [P, S], F32)
+        w1_raw = [held("w1_raw%d" % g, [P, PACK, H], F32) for g in range(2)]
+        st_raw = [held("st_raw%d" % c, [P, PACK, W], F32) for c in range(CHUNKS)]
+        zero = held("zero", [P, 1], F32)
+        zero_bias = held("zero_bias", [P, 1], F32)
+        ident = held("ident", [P, P], F32)
 
         nc.vector.memset(zero[:], 0.0)
-        nc.scalar.activation(zero_b[:], zero[:], ACT.Sin)
-        nc.vector.memset(w2s_raw[:].bitcast(I32), 0)
-        nc.vector.memset(tab_s[:].bitcast(I32), 0)
-        nc.vector.memset(w3_s[:].bitcast(I32), 0)
+        nc.scalar.activation(zero_bias[:], zero[:], ACT.Sin)
 
-        def load_w1(a, g):
-            nc.sync.dma_start(out=w1_raw[a, g][:], in_=w1[512 * g : 512 * (g + 1), 512 * a : 512 * (a + 1)].rearrange("(p j) c -> p j c", j=4))
+        nc.sync.dma_start(out=tab_s[0:32, :].bitcast(I32), in_=tab_scales.rearrange("g q n -> q g n").bitcast(I32))
+        nc.vector.memset(tab_s[32:64, :].bitcast(I32), 0)
+        nc.vector.memset(tab_s[64:128, :].bitcast(I32), 0)
+        nc.gpsimd.memset(w2s_raw[:].bitcast(I32), 0)
+        nc.gpsimd.memset(v_s[:].bitcast(I32), 0)
+        nc.gpsimd.memset(w3_s[:].bitcast(I32), 0)
+
+        def load_w1(g):
+            rows = w1[PASS * g : PASS * (g + 1), :]
+            nc.sync.dma_start(out=w1_raw[g][:], in_=rows.rearrange("(p i) r -> p i r", i=PACK))
 
         def load_tab(g):
-            nc.sync.dma_start(out=tab_w[g][:].bitcast(I32), in_=tab_words[g].rearrange("p n t -> p (n t)").bitcast(I32))
+            words = tab_words[g].rearrange("p n i -> p (n i)")
+            nc.sync.dma_start(out=tab_w[g][:].bitcast(I32), in_=words.bitcast(I32))
 
         def load_stress(c):
-            nc.sync.dma_start(out=st_raw[c][:], in_=stress[:, W * c : W * (c + 1)].rearrange("(p j) c -> p j c", j=4))
+            columns = stress[:, W * c : W * (c + 1)]
+            nc.sync.dma_start(out=st_raw[c][:], in_=columns.rearrange("(p i) j -> p i j", i=PACK))
 
-        def load_tab_s(g, q):
-            nc.sync.dma_start(out=tab_s[32 * q + 4 * g : 32 * q + 4 * g + 4, :].bitcast(I32), in_=tab_scales[g, 4 * q : 4 * q + 4, :].bitcast(I32))
-
-        nc.sync.dma_start(out=w2_raw[:].bitcast(I32), in_=w2_words[0].bitcast(I32))
         nc.sync.dma_start(offs_t[:], offs)
-        load_w1(0, 0)
-        for q in range(4):
-            nc.sync.dma_start(out=w2s_raw[32 * q : 32 * q + 4, :].bitcast(I32), in_=w2_scales[0, 4 * q : 4 * q + 4, :].bitcast(I32))
+        nc.sync.dma_start(out=w2_raw[:].bitcast(I32), in_=w2_words[0].bitcast(I32))
+        load_w1(0)
         load_tab(0)
-        load_w1(0, 1)
-        for q in range(4):
-            load_tab_s(0, q)
-        load_tab_s(1, 0)
-        load_tab_s(1, 1)
+        for quad in range(4):
+            nc.sync.dma_start(
+                out=w2s_raw[32 * quad : 32 * quad + 4, :].bitcast(I32),
+                in_=w2_scales[0, 4 * quad : 4 * quad + 4, :].bitcast(I32),
+            )
+        load_w1(1)
         load_stress(0)
-        load_tab_s(1, 2)
-        load_tab_s(1, 3)
+
+        nc.vector.tensor_copy(picked_rows[:], tab_s[:].indirect(offs_t[:]))
+        for quad in range(4):
+            nc.sync.dma_start(
+                out=v_s[32 * quad : 32 * quad + 4, :].bitcast(I32),
+                in_=picked_rows[8 * quad : 8 * quad + 8, :].bitcast(I32),
+            )
+
         load_tab(1)
-        nc.sync.dma_start(out=ph_raw[:], in_=phase.rearrange("(a p t) -> p a t", a=2, t=4))
-        nc.sync.dma_start(out=gn[:], in_=gain.rearrange("(a p t) -> p a t", a=2, t=4))
-        load_w1(1, 0)
-        load_w1(1, 1)
+        nc.sync.dma_start(out=phase_t[:], in_=phase.rearrange("(a p t) -> p a t", a=2, t=PACK))
+        nc.sync.dma_start(out=gain_t[:], in_=gain.rearrange("(a p t) -> p a t", a=2, t=PACK))
         load_stress(1)
-        nc.sync.dma_start(out=w3_c[:].bitcast(I32), in_=w3_words.rearrange("a p n t -> p a (n t)").bitcast(I32))
-        for q in range(4):
-            nc.sync.dma_start(out=w3_s[32 * q : 32 * q + 8, :].bitcast(I32), in_=w3_scales[:, 4 * q : 4 * q + 4, :].bitcast(I32))
+        nc.sync.dma_start(out=w3_c[:].bitcast(I32), in_=w3_words.rearrange("a p n i -> p a (n i)").bitcast(I32))
+        for quad in range(4):
+            nc.sync.dma_start(
+                out=w3_s[32 * quad : 32 * quad + 8, :].bitcast(I32),
+                in_=w3_scales[:, 4 * quad : 4 * quad + 4, :].bitcast(I32),
+            )
         nc.sync.dma_start(offs2_t[:], offs2)
         nc.sync.dma_start(out=wgo_t[:], in_=wgo)
-        load_stress(2)
-        load_stress(3)
-        for n in range(4):
-            nc.sync.dma_start(out=x0_t[n][:], in_=x0[P * n : P * (n + 1), :])
+        for c in range(2, CHUNKS):
+            load_stress(c)
+
+        make_identity(nc, ident[:])
 
         nc.vector.tensor_copy(
-            out=w2_c[:].rearrange("p (a t m b) -> p a t m b", a=2, t=4, b=2),
-            in_=w2_raw[:].rearrange("p (a m t b) -> p a t m b", a=2, t=4, b=2),
+            out=w2_c[:].rearrange("p (a t m b) -> p a t m b", a=2, t=PACK, b=2),
+            in_=w2_raw[:].rearrange("p (a m t b) -> p a t m b", a=2, t=PACK, b=2),
         )
         nc.vector.tensor_copy(
-            out=w2_s[:].rearrange("p (a t m) -> p a t m", a=2, t=4),
-            in_=w2s_raw[:].rearrange("p (a m t) -> p a t m", a=2, t=4),
+            out=w2_s[:].rearrange("p (a t m) -> p a t m", a=2, t=PACK),
+            in_=w2s_raw[:].rearrange("p (a m t) -> p a t m", a=2, t=PACK),
         )
 
-        w1_c, w1_s = {}, {}
+        w1_c, w1_s, st_c, st_s, h_c, h_s = {}, {}, {}, {}, {}, {}
+        turns, cosine, y_place, x0_t, late_diff = {}, {}, {}, {}, {}
 
-        def cast(eng, o, i):
-            if eng == "v":
-                nc.vector.tensor_copy(out=o, in_=i)
-            else:
-                nc.scalar.copy(out=o, in_=i)
+        def quantise_w1(a, g, on_vector):
+            woven = ring.tile([P, PACK * PASS], BF16, name="w1_woven", align_bytes=64)
+            cast(
+                on_vector,
+                woven[:].rearrange("p (t m i) -> p m i t", t=PACK, i=PACK),
+                w1_raw[g][:, :, PASS * a : PASS * (a + 1)].rearrange("p i (m t) -> p m i t", t=PACK),
+            )
+            w1_c[a, g] = held("w1_c%d%d" % (a, g), [P, PASS], U32)
+            w1_s[a, g] = held("w1_s%d%d" % (a, g), [P, PASS], U8)
+            nc.vector.quantize_mx(out=w1_c[a, g][:].bitcast(FP8X4), scales=w1_s[a, g][:], in_=woven[:])
 
-        def prep_w1(a, g, eng):
-            grouped = ring.tile([P, 2048], BF16, name="w1_b", align_bytes=64, bufs=2)
-            cast(eng, grouped[:].rearrange("p (t m j) -> p m j t", t=4, j=4), w1_raw[a, g][:].rearrange("p j (m t) -> p m j t", t=4))
-            w1_c[a, g] = kt("w1_c%d%d" % (a, g), [P, 512], U32)
-            w1_s[a, g] = kt("w1_s%d%d" % (a, g), [P, 512], U8)
-            nc.vector.quantize_mx(out=w1_c[a, g][:].bitcast(FP8X4), scales=w1_s[a, g][:], in_=grouped[:])
+        def quantise_stress(c, on_vector):
+            woven = ring.tile([P, PACK * W], BF16, name="st_woven", align_bytes=64)
+            cast(
+                on_vector,
+                woven[:].rearrange("p (j e i) -> p j i e", e=4, i=PACK),
+                st_raw[c][:].rearrange("p i (j e) -> p j i e", e=4),
+            )
+            st_c[c] = held("st_c%d" % c, [P, W], U32)
+            st_s[c] = held("st_s%d" % c, [P, W], U8)
+            nc.vector.quantize_mx(out=st_c[c][:].bitcast(FP8X4), scales=st_s[c][:], in_=woven[:])
 
-        st_c, st_s = {}, {}
-
-        def prep_stress(c, eng):
-            grouped = ring.tile([P, 4 * W], BF16, name="st_b", align_bytes=64, bufs=2)
-            cast(eng, grouped[:].rearrange("p (c i j) -> p c j i", i=4, j=4), st_raw[c][:].rearrange("p j (c i) -> p c j i", i=4))
-            st_c[c] = kt("st_c%d" % c, [P, W], U32)
-            st_s[c] = kt("st_s%d" % c, [P, W], U8)
-            nc.vector.quantize_mx(out=st_c[c][:].bitcast(FP8X4), scales=st_s[c][:], in_=grouped[:])
-
-        g_w, g_s = {}, {}
+        v_c = [held("v_c%d" % g, [P, S], U32) for g in range(2)]
 
         def gather_words(g, half):
-            g_w[g, half] = kt("g_w%d%d" % (g, half), [P, 512], U32)
-            nc.vector.tensor_copy(g_w[g, half][:], tab_w[g][:].indirect(offs_t[:, 32 * half : 32 * (half + 1)]))
+            lo, hi = half * S // 2, (half + 1) * S // 2
+            nc.vector.tensor_copy(v_c[g][:, lo:hi], tab_w[g][:].indirect(offs_t[:, lo // LIST : hi // LIST]))
 
-        def gather_scales(half):
-            g_s[half] = kt("g_s%d" % half, [P, 512], U8)
-            nc.vector.tensor_copy(g_s[half][:], tab_s[:].indirect(offs_t[:, 32 * half : 32 * (half + 1)]))
+        y_neg = held("y_neg", [P, TILES, S], F32)
+        page_neg = [held("page_neg%d" % n, [P, S], F32) for n in range(TILES)]
 
-        prep_w1(0, 0, "s")
-        gather_words(0, 0)
-        gather_words(0, 1)
-        prep_w1(0, 1, "s")
-        gather_scales(0)
-        prep_stress(0, "s")
-        gather_words(1, 0)
-        nc.vector.tensor_scalar(ph[:], ph_raw[:], 1.0 / TWO_PI, TURN_OFFSET, ALU.mult, ALU.add)
-
-        h_c, h_s, u_t, k_t, hb_t = {}, {}, {}, {}, {}
-        y_t = [kt("y_t%d" % n, [P, S], F32) for n in range(4)]
-        page = [kt("page%d" % n, [P, S], F32) for n in range(4)]
-        units = [(c, a) for c in range(CH) for a in range(2)]
-
-        def unit_mm(i):
-            c, a = units[i]
-            half, cols = c // 2, slice(W * (c % 2), W * (c % 2 + 1))
-            u_t[i] = ring.tile([P, 4, W], F32, name="u")
+        def argument(i):
+            c, a = UNITS[i]
+            cols = slice(W * c, W * (c + 1))
+            turns[i] = ring.tile([P, PACK, W], F32, name="turns", bufs=3)
             for pair in range(2):
-                bank = psum.tile([P, 2, W], F32, name="s1_%d" % pair, bufs=3)
-                for tt in range(2):
-                    t = 2 * pair + tt
-                    m = slice(P * t, P * (t + 1))
+                bank = arg_bank([P, 2, W])
+                slices = [(e, 2 * pair + e) for e in range(2)]
+                for e, t in slices:
                     nc.tensor.matmul_mx(
-                        out=bank[:, tt, :], lhsT=w1_c[a, 0][:, m].bitcast(FP8X4), lhsT_scale=w1_s[a, 0][:, m],
-                        rhs=g_w[0, half][:, cols].bitcast(FP8X4), rhs_scale=g_s[half][:, cols], start=True, stop=False)
-                    col0 = 512 * a + P * t
-                    for e in range(W // P):
+                        out=bank[:, e, :],
+                        lhsT=w1_c[a, 0][:, P * t : P * (t + 1)].bitcast(FP8X4),
+                        lhsT_scale=w1_s[a, 0][:, P * t : P * (t + 1)],
+                        rhs=v_c[0][:, cols].bitcast(FP8X4),
+                        rhs_scale=v_s[:, cols],
+                        start=(e == 0),
+                        stop=False,
+                    )
+                for e, t in slices:
+                    first = PASS * a + P * t
+                    for lo in range(0, W, P):
                         nc.tensor.matmul_mx(
-                            out=bank[:, tt, P * e : P * (e + 1)], lhsT=w2_c[:, 2 * col0 : 2 * (col0 + P)].bitcast(FP4X4),
-                            lhsT_scale=w2_s[:, col0 : col0 + P],
-                            rhs=st_c[c][:, P * e : P * (e + 1)].bitcast(FP8X4), rhs_scale=st_s[c][:, P * e : P * (e + 1)],
-                            start=False, stop=False)
+                            out=bank[:, e, lo : lo + P],
+                            lhsT=w2_c[:, 2 * first : 2 * (first + P)].bitcast(FP4X4),
+                            lhsT_scale=w2_s[:, first : first + P],
+                            rhs=st_c[c][:, lo : lo + P].bitcast(FP8X4),
+                            rhs_scale=st_s[c][:, lo : lo + P],
+                            start=False,
+                            stop=False,
+                        )
+                for e, t in slices:
                     nc.tensor.matmul_mx(
-                        out=bank[:, tt, :], lhsT=w1_c[a, 1][:, m].bitcast(FP8X4), lhsT_scale=w1_s[a, 1][:, m],
-                        rhs=g_w[1, half][:, cols].bitcast(FP8X4), rhs_scale=g_s[half][4:P, cols], start=False, stop=True)
-                for tt in range(2):
-                    t = 2 * pair + tt
-                    nc.scalar.activation(u_t[i][:, t, :], bank[:, tt, :], ACT.Abs, bias=ph[:, a, t : t + 1], scale=1.0 / TWO_PI)
+                        out=bank[:, e, :],
+                        lhsT=w1_c[a, 1][:, P * t : P * (t + 1)].bitcast(FP8X4),
+                        lhsT_scale=w1_s[a, 1][:, P * t : P * (t + 1)],
+                        rhs=v_c[1][:, cols].bitcast(FP8X4),
+                        rhs_scale=v_s[:, S + W * c : S + W * (c + 1)],
+                        start=False,
+                        stop=(e == 1),
+                    )
+                for e, t in slices:
+                    nc.scalar.activation(
+                        turns[i][:, t, :], bank[:, e, :], ACT.Abs,
+                        bias=phase_turns[:, a, t : t + 1], scale=1.0 / TWO_PI,
+                    )
 
-        def unit_k(i):
-            u = u_t[i][:].rearrange("p t n -> p (t n)")
-            k_t[i] = ring.tile([P, 4 * W], I32, name="k", bufs=2)
-            if i < V_K_UNITS:
-                nc.vector.tensor_scalar(k_t[i][:], u, -0.25, None, ALU.add)
+        def reduce_turns(i):
+            flat = turns[i][:].rearrange("p t j -> p (t j)")
+            whole = ring.tile([P, PACK * W], I32, name="whole")
+            if i < TURNS_ON_VECTOR:
+                nc.vector.tensor_scalar(whole[:], flat, -0.25, None, ALU.add)
             else:
-                nc.scalar.activation(k_t[i][:].bitcast(U32), u, ACT.Copy, bias=-0.25)
+                nc.scalar.activation(whole[:].bitcast(U32), flat, ACT.Copy, bias=-0.25)
+            nc.vector.tensor_tensor(flat, flat, whole[:], ALU.subtract)
 
-        def unit_f(i):
-            u = u_t[i][:].rearrange("p t n -> p (t n)")
-            nc.vector.tensor_tensor(u, u, k_t[i][:], ALU.subtract)
+        def sine(i):
+            if i < GAIN_ON_VECTOR:
+                cosine[i] = ring.tile([P, PACK * W], F32, name="cosine")
+                dst = cosine[i][:].rearrange("p (j e t) -> p j t e", e=4, t=PACK)
+                src = turns[i][:].rearrange("p t (j e) -> p j t e", e=4)
+            else:
+                dst = src = turns[i][:].rearrange("p t j -> p (t j)")
+            nc.scalar.activation(dst, src, ACT.Sin, bias=math.pi / 2, scale=-TWO_PI)
 
-        def unit_sin(i):
-            c, a = units[i]
-            u = u_t[i][:].rearrange("p t n -> p (t n)")
-            nc.scalar.activation(u, u, ACT.Sin, bias=math.pi / 2, scale=-TWO_PI)
-            hb_t[i] = ring.tile([P, 4, W], BF16, name="hb", bufs=2)
-            for t in range(4):
-                if i < V_GAIN_UNITS:
-                    nc.vector.tensor_scalar(hb_t[i][:, t, :], u_t[i][:, t, :], gn[:, a, t : t + 1], None, ALU.mult)
-                else:
-                    nc.scalar.activation(hb_t[i][:, t, :], u_t[i][:, t, :], ACT.Copy, scale=gn[:, a, t : t + 1])
+        def second_product(parts):
+            bank = psum.tile([P, BANK], F32, name="y_bank", bufs=2)
+            for e, (c, n) in enumerate(parts):
+                y_place[c, n] = (bank, W * e)
+                for a in range(2):
+                    nc.tensor.matmul_mx(
+                        out=bank[:, W * e : W * (e + 1)],
+                        lhsT=w3_c[:, a, P * n : P * (n + 1)].bitcast(FP8X4),
+                        lhsT_scale=w3_s[4 * a : P, P * n : P * (n + 1)],
+                        rhs=h_c[c, a][:].bitcast(FP8X4),
+                        rhs_scale=h_s[c, a][:],
+                        start=(a == 0),
+                        stop=(a == 1),
+                    )
 
-        def unit_q(i):
-            c, a = units[i]
-            grouped = ring.tile([P, 4 * W], BF16, name="h_b", align_bytes=64, bufs=2)
-            cast("v" if i < V_IL_UNITS else "s", grouped[:].rearrange("p (c i t) -> p c t i", i=4, t=4), hb_t[i][:].rearrange("p t (c i) -> p c t i", i=4))
+        def own_tiles(c):
+            return list(range(TILES if c < CHUNKS - 2 else EARLY_TILES))
+
+        def quantise_h(i):
+            c, a = UNITS[i]
+            woven = ring.tile([P, PACK * W], BF16, name="h_woven", align_bytes=64)
+            if i < GAIN_ON_VECTOR:
+                nc.vector.tensor_tensor(
+                    woven[:].rearrange("p (j t) -> p j t", t=PACK),
+                    cosine[i][:].rearrange("p (j t) -> p j t", t=PACK),
+                    gain_t[:, a, :].unsqueeze(1).to_broadcast([P, W, PACK]),
+                    ALU.mult,
+                )
+            else:
+                h_slices = ring.tile([P, PACK, W], BF16, name="h_slices")
+                for t in range(PACK):
+                    nc.scalar.activation(
+                        h_slices[:, t, :], turns[i][:, t, :], ACT.Copy, scale=gain_t[:, a, t : t + 1]
+                    )
+                cast(
+                    i < WEAVE_ON_SCALAR_FROM,
+                    woven[:].rearrange("p (j e t) -> p j t e", e=4, t=PACK),
+                    h_slices[:].rearrange("p t (j e) -> p j t e", e=4),
+                )
             h_c[c, a] = ring.tile([P, W], U32, name="h_c", align_bytes=64, bufs=4)
             h_s[c, a] = ring.tile([P, W], U8, name="h_s", align_bytes=64, bufs=4)
-            nc.vector.quantize_mx(out=h_c[c, a][:].bitcast(FP8X4), scales=h_s[c, a][:], in_=grouped[:])
+            nc.vector.quantize_mx(out=h_c[c, a][:].bitcast(FP8X4), scales=h_s[c, a][:], in_=woven[:])
+            if a == 1:
+                tiles = own_tiles(c)
+                for lo in range(0, len(tiles), 2):
+                    second_product([(c, n) for n in tiles[lo : lo + 2]])
+                if c == CHUNKS - 1:
+                    for n in range(EARLY_TILES, TILES):
+                        second_product([(c - 1, n), (c, n)])
 
-        y_bank = {}
-
-        def stage2(c):
-            for pair in range(2):
-                y_bank[c, pair] = psum.tile([P, 2, W], F32, name="s2_%d" % pair)
-                for nn in range(2):
-                    n = 2 * pair + nn
-                    m = slice(P * n, P * (n + 1))
-                    for a in range(2):
-                        nc.tensor.matmul_mx(
-                            out=y_bank[c, pair][:, nn, :], lhsT=w3_c[:, a, m].bitcast(FP8X4), lhsT_scale=w3_s[4 * a : P, m],
-                            rhs=h_c[c, a][:].bitcast(FP8X4), rhs_scale=h_s[c, a][:], start=(a == 0), stop=(a == 1))
-
-        def y_out(c, n):
-            nc.scalar.copy(out=y_t[n][:, W * c : W * (c + 1)], in_=y_bank[c, n // 2][:, n % 2, :])
-
-        def scatter(c0, c1, n):
-            cols = slice(W * c0, W * c1)
-            nc.vector.tensor_tensor(page[n][:].indirect(offs2_t[:, W * c0 // 16 : W * c1 // 16]), y_t[n][:, cols], wgo_t[:, cols], ALU.mult)
+        def scatter(c, n, chunks=1):
+            bank, at = y_place[c, n]
+            lo, hi = W * c, W * (c + chunks)
+            nc.scalar.activation(y_neg[:, n, lo:hi], bank[:, at : at + hi - lo], ACT.Copy, scale=-1.0)
+            nc.vector.tensor_tensor(
+                page_neg[n][:].indirect(offs2_t[:, lo // LIST : hi // LIST]),
+                y_neg[:, n, lo:hi], wgo_t[:, lo:hi], ALU.mult,
+            )
 
         def finish(n):
             for half in range(2):
-                cols = slice(512 * half, 512 * (half + 1))
-                nc.vector.tensor_tensor(x0_t[n][:, cols], page[n][:, cols], x0_t[n][:, cols], ALU.subtract)
-                nc.scalar.activation(x0_t[n][:, cols], x0_t[n][:, cols], ACT.Abs, bias=zero_b[:])
-                nc.sync.dma_start(out=out[P * n : P * (n + 1), cols], in_=x0_t[n][:, cols])
+                cols = slice(BANK * half, BANK * (half + 1))
+                if n < EARLY_TILES:
+                    bank = arg_bank([P, 4, P])
+                    blocks = [(b, slice(BANK * half + P * b, BANK * half + P * (b + 1))) for b in range(4)]
+                    for b, blk in blocks:
+                        nc.tensor.matmul(
+                            bank[:, b, :], x0_t[n][:, blk], ident[:], start=(b == 0), stop=False, is_transpose=True
+                        )
+                    for b, blk in blocks:
+                        nc.tensor.matmul(
+                            bank[:, b, :], page_neg[n][:, blk], ident[:], start=False, stop=(b == 3), is_transpose=True
+                        )
+                    turned = held("turned%d%d" % (n, half), [P, 4, P], F32)
+                    nc.scalar.activation(turned[:], bank[:], ACT.Abs, bias=zero_bias[:])
+                    for b, blk in blocks:
+                        nc.tensor.transpose(bank[:, b, :], turned[:, b, :], ident[:])
+                    result = y_neg[:, n, cols]
+                    nc.scalar.copy(out=result, in_=bank[:].rearrange("p b j -> p (b j)"))
+                else:
+                    if half not in late_diff:
+                        name = "turned%d%d" % (EARLY_TILES - 1, half)
+                        late_diff[half] = held(name, [P, TILES - EARLY_TILES, BANK], F32)
+                    result = late_diff[half][:, n - EARLY_TILES, :]
+                    nc.vector.tensor_tensor(result, page_neg[n][:, cols], x0_t[n][:, cols], ALU.add)
+                    nc.scalar.activation(result, result, ACT.Abs, bias=zero_bias[:])
+                nc.sync.dma_start(out=out[P * n : P * (n + 1), cols], in_=result)
 
+        nc.vector.tensor_scalar(phase_turns[:], phase_t[:], 1.0 / TWO_PI, None, ALU.mult)
 
-        unit_mm(0)
-        unit_k(0)
-        unit_f(0)
-        prep_w1(1, 0, "s")
-        unit_sin(0)
-        unit_q(0)
-        prep_w1(1, 1, "v")
+        quantise_w1(0, 0, False)
+        quantise_w1(1, 0, False)
+        gather_words(0, 0)
+        gather_words(0, 1)
+        quantise_w1(0, 1, False)
+        quantise_w1(1, 1, True)
+        quantise_stress(0, False)
+        gather_words(1, 0)
+        argument(0)
+        argument(1)
+        reduce_turns(0)
         gather_words(1, 1)
-        gather_scales(1)
-        unit_mm(1)
-        prep_stress(1, "s")
-        unit_k(1)
-        unit_f(1)
-        unit_mm(2)
-        unit_sin(1)
-        unit_q(1)
-        stage2(0)
-        pend = [(c, n) for c in range(3) for n in range(4)]
-        for i in range(2, 8):
-            c, a = units[i]
-            unit_k(i)
-            unit_f(i)
-            cc, n = pend[2 * (i - 2)]
-            y_out(cc, n)
-            scatter(cc, cc + 1, n)
-            if i + 1 < 8:
-                if a == 1:
-                    prep_stress(c + 1, "s")
-                unit_mm(i + 1)
-            unit_sin(i)
-            unit_q(i)
-            cc, n = pend[2 * (i - 2) + 1]
-            y_out(cc, n)
-            scatter(cc, cc + 1, n)
-            if a == 1:
-                stage2(c)
-        for n in range(4):
-            y_out(3, n)
-            scatter(3, 4, n)
+        quantise_stress(1, True)
+
+        for g in range(2):
+            pair = held("w1_raw%d" % g, [P, 2, S], F32)
+            rows = x0[2 * P * g : 2 * P * (g + 1), :]
+            nc.sync.dma_start(out=pair[:], in_=rows.rearrange("(n p) j -> p n j", n=2))
+            x0_t[2 * g] = pair[:, 0, :]
+            x0_t[2 * g + 1] = pair[:, 1, :]
+
+        waiting = [(c, n) for c in range(CHUNKS - 1) for n in own_tiles(c)]
+        places = {FIRST_SCATTER_PLACE + e: pick for e, pick in enumerate(waiting)}
+        last = len(UNITS) - 1
+        for i, (c, a) in enumerate(UNITS):
+            if 0 < i < last:
+                argument(i + 1)
+            sine(i)
+            if 2 * i in places:
+                scatter(*places[2 * i])
+            if i < last:
+                reduce_turns(i + 1)
+            if a == 1 and c + 2 < CHUNKS:
+                quantise_stress(c + 2, False)
+            quantise_h(i)
+            if 2 * i + 1 in places:
+                scatter(*places[2 * i + 1])
+        for place in range(2 * len(UNITS), FIRST_SCATTER_PLACE + len(waiting)):
+            scatter(*places[place])
+
+        for n in range(TILES):
+            if n < EARLY_TILES:
+                scatter(CHUNKS - 1, n)
+            else:
+                scatter(CHUNKS - 2, n, chunks=2)
             finish(n)

@@ -121,9 +121,9 @@ def tile_list_morton_grain_corrections_kernel(
                 in_=picked_rows[8 * quad : 8 * quad + 8, :].bitcast(I32),
             )
 
+        nc.sync.dma_start(out=gain_t[:], in_=gain.rearrange("(a p t) -> p a t", a=2, t=PACK))
         load_tab(1)
         nc.sync.dma_start(out=phase_t[:], in_=phase.rearrange("(a p t) -> p a t", a=2, t=PACK))
-        nc.sync.dma_start(out=gain_t[:], in_=gain.rearrange("(a p t) -> p a t", a=2, t=PACK))
         load_stress(1)
         nc.sync.dma_start(out=w3_c[:].bitcast(I32), in_=w3_words.rearrange("a p n i -> p a (n i)").bitcast(I32))
         for quad in range(4):
@@ -267,10 +267,7 @@ def tile_list_morton_grain_corrections_kernel(
             woven = ring.tile([P, PACK * W], BF16, name="h_woven", align_bytes=64)
             if i < GAIN_ON_VECTOR:
                 nc.vector.tensor_tensor(
-                    woven[:].rearrange("p (j t) -> p j t", t=PACK),
-                    cosine[i][:].rearrange("p (j t) -> p j t", t=PACK),
-                    gain_t[:, a, :].unsqueeze(1).to_broadcast([P, W, PACK]),
-                    ALU.mult,
+                    woven[:], cosine[i][:], gain_wide[:, a].rearrange("p j t -> p (j t)"), ALU.mult
                 )
             else:
                 h_slices = ring.tile([P, PACK, W], BF16, name="h_slices")
@@ -341,6 +338,8 @@ def tile_list_morton_grain_corrections_kernel(
         quantise_w1(0, 1, False)
         quantise_w1(1, 1, True)
         quantise_stress(0, False)
+        gain_wide = held("gain_wide", [P, 2, W, PACK], F32)
+        nc.scalar.copy(out=gain_wide[:], in_=gain_t[:].unsqueeze(2).to_broadcast([P, 2, W, PACK]))
         gather_words(1, 0)
         argument(0)
         argument(1)

@@ -26,14 +26,16 @@ LIST = 16
 W = 256
 CHUNKS = S // W
 TILES = N // P
-UNITS = [(c, a) for c in range(CHUNKS) for a in range(H // PASS)]
+UNITS = [(0, 0), (1, 0), (0, 1), (1, 1)] + [(c, a) for c in range(2, CHUNKS) for a in range(H // PASS)]
 TWO_PI = 2.0 * math.pi
 
 TURNS_ON_VECTOR = 4
-GAIN_ON_VECTOR = 5
-WEAVE_ON_SCALAR_FROM = 6
-FIRST_SCATTER_PLACE = 7
-EARLY_TILES = 2
+GAIN_ON_VECTOR = 4
+WEAVE_ON_SCALAR_FROM = 4
+SPREAD = 32
+FIRST_SCATTER_PLACE = 11
+MERGED_FROM = 4
+TENSOR_TILES = 2
 
 
 def tile_list_morton_grain_corrections_kernel(
@@ -43,7 +45,6 @@ def tile_list_morton_grain_corrections_kernel(
     nc = tc.nc
     with ExitStack() as ctx:
         keep = ctx.enter_context(tc.tile_pool(name="keep", bufs=1))
-        ring = ctx.enter_context(tc.tile_pool(name="ring", bufs=2))
         psum = ctx.enter_context(tc.psum_pool(name="psum", bufs=1))
 
         def held(name, shape, dtype):
@@ -74,7 +75,7 @@ def tile_list_morton_grain_corrections_kernel(
         phase_turns = held("phase_turns", [P, 2, PACK], F32)
         gain_t = held("gain_t", [P, 2, PACK], F32)
         wgo_t = held("wgo_t", [P, S], F32)
-        w1_raw = [held("w1_raw%d" % g, [P, PACK, H], F32) for g in range(2)]
+        w1_raw = {(a, g): held("w1_raw%d%d" % (a, g), [P, PACK, PASS], F32) for a in range(2) for g in range(2)}
         st_raw = [held("st_raw%d" % c, [P, PACK, W], F32) for c in range(CHUNKS)]
         zero = held("zero", [P, 1], F32)
         zero_bias = held("zero_bias", [P, 1], F32)
@@ -83,16 +84,16 @@ def tile_list_morton_grain_corrections_kernel(
         nc.vector.memset(zero[:], 0.0)
         nc.scalar.activation(zero_bias[:], zero[:], ACT.Sin)
 
+        nc.vector.memset(w2s_raw[:].bitcast(I32), 0)
         nc.sync.dma_start(out=tab_s[0:32, :].bitcast(I32), in_=tab_scales.rearrange("g q n -> q g n").bitcast(I32))
         nc.vector.memset(tab_s[32:64, :].bitcast(I32), 0)
         nc.vector.memset(tab_s[64:128, :].bitcast(I32), 0)
-        nc.gpsimd.memset(w2s_raw[:].bitcast(I32), 0)
         nc.gpsimd.memset(v_s[:].bitcast(I32), 0)
         nc.gpsimd.memset(w3_s[:].bitcast(I32), 0)
 
-        def load_w1(g):
-            rows = w1[PASS * g : PASS * (g + 1), :]
-            nc.sync.dma_start(out=w1_raw[g][:], in_=rows.rearrange("(p i) r -> p i r", i=PACK))
+        def load_w1(a, g):
+            block = w1[PASS * g : PASS * (g + 1), PASS * a : PASS * (a + 1)]
+            nc.sync.dma_start(out=w1_raw[a, g][:], in_=block.rearrange("(p i) r -> p i r", i=PACK))
 
         def load_tab(g):
             words = tab_words[g].rearrange("p n i -> p (n i)")
@@ -103,28 +104,28 @@ def tile_list_morton_grain_corrections_kernel(
             nc.sync.dma_start(out=st_raw[c][:], in_=columns.rearrange("(p i) j -> p i j", i=PACK))
 
         nc.sync.dma_start(offs_t[:], offs)
-        nc.sync.dma_start(out=w2_raw[:].bitcast(I32), in_=w2_words[0].bitcast(I32))
-        load_w1(0)
         load_tab(0)
         for quad in range(4):
             nc.sync.dma_start(
                 out=w2s_raw[32 * quad : 32 * quad + 4, :].bitcast(I32),
                 in_=w2_scales[0, 4 * quad : 4 * quad + 4, :].bitcast(I32),
             )
-        load_w1(1)
+        load_tab(1)
+        nc.sync.dma_start(out=w2_raw[:].bitcast(I32), in_=w2_words[0].bitcast(I32))
+        nc.sync.dma_start(out=phase_t[:], in_=phase.rearrange("(a p t) -> p a t", a=2, t=PACK))
         load_stress(0)
-
+        load_w1(0, 0)
+        nc.sync.dma_start(out=gain_t[:], in_=gain.rearrange("(a p t) -> p a t", a=2, t=PACK))
         nc.vector.tensor_copy(picked_rows[:], tab_s[:].indirect(offs_t[:]))
         for quad in range(4):
             nc.sync.dma_start(
                 out=v_s[32 * quad : 32 * quad + 4, :].bitcast(I32),
                 in_=picked_rows[8 * quad : 8 * quad + 8, :].bitcast(I32),
             )
-
-        nc.sync.dma_start(out=gain_t[:], in_=gain.rearrange("(a p t) -> p a t", a=2, t=PACK))
-        load_tab(1)
-        nc.sync.dma_start(out=phase_t[:], in_=phase.rearrange("(a p t) -> p a t", a=2, t=PACK))
+        load_w1(0, 1)
         load_stress(1)
+        load_w1(1, 0)
+        load_w1(1, 1)
         nc.sync.dma_start(out=w3_c[:].bitcast(I32), in_=w3_words.rearrange("a p n i -> p a (n i)").bitcast(I32))
         for quad in range(4):
             nc.sync.dma_start(
@@ -132,9 +133,9 @@ def tile_list_morton_grain_corrections_kernel(
                 in_=w3_scales[:, 4 * quad : 4 * quad + 4, :].bitcast(I32),
             )
         nc.sync.dma_start(offs2_t[:], offs2)
+        load_stress(2)
         nc.sync.dma_start(out=wgo_t[:], in_=wgo)
-        for c in range(2, CHUNKS):
-            load_stress(c)
+        load_stress(3)
 
         make_identity(nc, ident[:])
 
@@ -147,22 +148,39 @@ def tile_list_morton_grain_corrections_kernel(
             in_=w2s_raw[:].rearrange("p (a m t) -> p a t m", a=2, t=PACK),
         )
 
-        w1_c, w1_s, st_c, st_s, h_c, h_s = {}, {}, {}, {}, {}, {}
-        turns, cosine, y_place, x0_t, late_diff = {}, {}, {}, {}, {}
+        def buffers(name, count, shape, dtype):
+            return [held("%s%d" % (name, e), shape, dtype) for e in range(count)]
 
-        def quantise_w1(a, g, on_vector):
-            woven = ring.tile([P, PACK * PASS], BF16, name="w1_woven", align_bytes=64)
-            cast(
-                on_vector,
-                woven[:].rearrange("p (t m i) -> p m i t", t=PACK, i=PACK),
-                w1_raw[g][:, :, PASS * a : PASS * (a + 1)].rearrange("p i (m t) -> p m i t", t=PACK),
-            )
+        w1_woven = held("w1_woven", [P, PACK * PASS], BF16)
+        woven_bufs = buffers("woven", 2, [P, PACK * W], BF16)
+        turns_bufs = buffers("turns", 3, [P, PACK, W], F32)
+        whole_bufs = buffers("whole", 2, [P, PACK * W], I32)
+        cosine_bufs = buffers("cosine", 2, [P, PACK * W], F32)
+        slices_bufs = buffers("h_slices", 2, [P, PACK, W], BF16)
+        turned_bufs = buffers("turned", 4, [P, 4, P], F32)
+        woven_uses = []
+
+        def next_woven():
+            woven_uses.append(woven_bufs[len(woven_uses) % 2])
+            return woven_uses[-1]
+
+        w1_c, w1_s, st_c, st_s, h_c, h_s = {}, {}, {}, {}, {}, {}
+        turns, cosine, y_place, y_rows, x0_bank = {}, {}, {}, {}, {}
+
+        def quantise_w1(a, g, vector_columns):
+            woven = w1_woven
+            dst = woven[:].rearrange("p (t m i) -> p m i t", t=PACK, i=PACK)
+            src = w1_raw[a, g][:].rearrange("p i (m t) -> p m i t", t=PACK)
+            if vector_columns > 0:
+                cast(True, dst[:, :vector_columns], src[:, :vector_columns])
+            if vector_columns < P:
+                cast(False, dst[:, vector_columns:], src[:, vector_columns:])
             w1_c[a, g] = held("w1_c%d%d" % (a, g), [P, PASS], U32)
             w1_s[a, g] = held("w1_s%d%d" % (a, g), [P, PASS], U8)
             nc.vector.quantize_mx(out=w1_c[a, g][:].bitcast(FP8X4), scales=w1_s[a, g][:], in_=woven[:])
 
         def quantise_stress(c, on_vector):
-            woven = ring.tile([P, PACK * W], BF16, name="st_woven", align_bytes=64)
+            woven = next_woven()
             cast(
                 on_vector,
                 woven[:].rearrange("p (j e i) -> p j i e", e=4, i=PACK),
@@ -173,31 +191,22 @@ def tile_list_morton_grain_corrections_kernel(
             nc.vector.quantize_mx(out=st_c[c][:].bitcast(FP8X4), scales=st_s[c][:], in_=woven[:])
 
         v_c = [held("v_c%d" % g, [P, S], U32) for g in range(2)]
+        for g in range(2):
+            nc.vector.tensor_copy(v_c[g][:], tab_w[g][:].indirect(offs_t[:]))
 
-        def gather_words(g, half):
-            lo, hi = half * S // 2, (half + 1) * S // 2
-            nc.vector.tensor_copy(v_c[g][:, lo:hi], tab_w[g][:].indirect(offs_t[:, lo // LIST : hi // LIST]))
-
-        y_neg = held("y_neg", [P, TILES, S], F32)
+        x0_t = held("tab_w0", [P, TILES, S], F32)
+        nc.sync.dma_start(out=x0_t[:, 0:2, :], in_=x0[0 : 2 * P, :].rearrange("(n p) j -> p n j", n=2))
+        nc.sync.dma_start(out=x0_t[:, 2:4, :], in_=x0[2 * P : 4 * P, :].rearrange("(n p) j -> p n j", n=2))
+        y_neg = held("tab_w1", [P, TILES * S], F32)
         page_neg = [held("page_neg%d" % n, [P, S], F32) for n in range(TILES)]
 
         def argument(i):
             c, a = UNITS[i]
             cols = slice(W * c, W * (c + 1))
-            turns[i] = ring.tile([P, PACK, W], F32, name="turns", bufs=3)
+            turns[i] = turns_bufs[i % len(turns_bufs)]
             for pair in range(2):
                 bank = arg_bank([P, 2, W])
                 slices = [(e, 2 * pair + e) for e in range(2)]
-                for e, t in slices:
-                    nc.tensor.matmul_mx(
-                        out=bank[:, e, :],
-                        lhsT=w1_c[a, 0][:, P * t : P * (t + 1)].bitcast(FP8X4),
-                        lhsT_scale=w1_s[a, 0][:, P * t : P * (t + 1)],
-                        rhs=v_c[0][:, cols].bitcast(FP8X4),
-                        rhs_scale=v_s[:, cols],
-                        start=(e == 0),
-                        stop=False,
-                    )
                 for e, t in slices:
                     first = PASS * a + P * t
                     for lo in range(0, W, P):
@@ -207,19 +216,20 @@ def tile_list_morton_grain_corrections_kernel(
                             lhsT_scale=w2_s[:, first : first + P],
                             rhs=st_c[c][:, lo : lo + P].bitcast(FP8X4),
                             rhs_scale=st_s[c][:, lo : lo + P],
-                            start=False,
+                            start=(e == 0 and lo == 0),
                             stop=False,
                         )
-                for e, t in slices:
-                    nc.tensor.matmul_mx(
-                        out=bank[:, e, :],
-                        lhsT=w1_c[a, 1][:, P * t : P * (t + 1)].bitcast(FP8X4),
-                        lhsT_scale=w1_s[a, 1][:, P * t : P * (t + 1)],
-                        rhs=v_c[1][:, cols].bitcast(FP8X4),
-                        rhs_scale=v_s[:, S + W * c : S + W * (c + 1)],
-                        start=False,
-                        stop=(e == 1),
-                    )
+                for g in range(2):
+                    for e, t in slices:
+                        nc.tensor.matmul_mx(
+                            out=bank[:, e, :],
+                            lhsT=w1_c[a, g][:, P * t : P * (t + 1)].bitcast(FP8X4),
+                            lhsT_scale=w1_s[a, g][:, P * t : P * (t + 1)],
+                            rhs=v_c[g][:, cols].bitcast(FP8X4),
+                            rhs_scale=v_s[:, S * g + W * c : S * g + W * (c + 1)],
+                            start=False,
+                            stop=(g == 1 and e == 1),
+                        )
                 for e, t in slices:
                     nc.scalar.activation(
                         turns[i][:, t, :], bank[:, e, :], ACT.Abs,
@@ -228,8 +238,8 @@ def tile_list_morton_grain_corrections_kernel(
 
         def reduce_turns(i):
             flat = turns[i][:].rearrange("p t j -> p (t j)")
-            whole = ring.tile([P, PACK * W], I32, name="whole")
-            if i < TURNS_ON_VECTOR:
+            whole = whole_bufs[i % 2]
+            if 2 <= i < TURNS_ON_VECTOR:
                 nc.vector.tensor_scalar(whole[:], flat, -0.25, None, ALU.add)
             else:
                 nc.scalar.activation(whole[:].bitcast(U32), flat, ACT.Copy, bias=-0.25)
@@ -237,7 +247,7 @@ def tile_list_morton_grain_corrections_kernel(
 
         def sine(i):
             if i < GAIN_ON_VECTOR:
-                cosine[i] = ring.tile([P, PACK * W], F32, name="cosine")
+                cosine[i] = cosine_bufs[i % 2]
                 dst = cosine[i][:].rearrange("p (j e t) -> p j t e", e=4, t=PACK)
                 src = turns[i][:].rearrange("p t (j e) -> p j t e", e=4)
             else:
@@ -260,121 +270,137 @@ def tile_list_morton_grain_corrections_kernel(
                     )
 
         def own_tiles(c):
-            return list(range(TILES if c < CHUNKS - 2 else EARLY_TILES))
+            return list(range(TILES if c < CHUNKS - 2 else MERGED_FROM))
+
+        def apply_gain(i):
+            if i >= GAIN_ON_VECTOR:
+                a = UNITS[i][1]
+                for t in range(PACK):
+                    nc.scalar.activation(
+                        slices_bufs[i % 2][:, t, :], turns[i][:, t, :], ACT.Copy, scale=gain_t[:, a, t : t + 1]
+                    )
 
         def quantise_h(i):
             c, a = UNITS[i]
-            woven = ring.tile([P, PACK * W], BF16, name="h_woven", align_bytes=64)
+            woven = next_woven()
             if i < GAIN_ON_VECTOR:
                 nc.vector.tensor_tensor(
-                    woven[:], cosine[i][:], gain_wide[:, a].rearrange("p j t -> p (j t)"), ALU.mult
+                    woven[:].rearrange("p (u x) -> p u x", x=SPREAD * PACK),
+                    cosine[i][:].rearrange("p (u x) -> p u x", x=SPREAD * PACK),
+                    gain_wide[:, a].rearrange("p j t -> p (j t)").unsqueeze(1).to_broadcast([P, W // SPREAD, SPREAD * PACK]),
+                    ALU.mult,
                 )
             else:
-                h_slices = ring.tile([P, PACK, W], BF16, name="h_slices")
-                for t in range(PACK):
-                    nc.scalar.activation(
-                        h_slices[:, t, :], turns[i][:, t, :], ACT.Copy, scale=gain_t[:, a, t : t + 1]
-                    )
                 cast(
                     i < WEAVE_ON_SCALAR_FROM,
                     woven[:].rearrange("p (j e t) -> p j t e", e=4, t=PACK),
-                    h_slices[:].rearrange("p t (j e) -> p j t e", e=4),
+                    slices_bufs[i % 2][:].rearrange("p t (j e) -> p j t e", e=4),
                 )
-            h_c[c, a] = ring.tile([P, W], U32, name="h_c", align_bytes=64, bufs=4)
-            h_s[c, a] = ring.tile([P, W], U8, name="h_s", align_bytes=64, bufs=4)
+            h_c[c, a] = held("h_c%d%d" % (c, a), [P, W], U32)
+            h_s[c, a] = held("h_s%d%d" % (c, a), [P, W], U8)
             nc.vector.quantize_mx(out=h_c[c, a][:].bitcast(FP8X4), scales=h_s[c, a][:], in_=woven[:])
-            if a == 1:
+            if (c, 0) in h_c and (c, 1) in h_c:
                 tiles = own_tiles(c)
                 for lo in range(0, len(tiles), 2):
                     second_product([(c, n) for n in tiles[lo : lo + 2]])
                 if c == CHUNKS - 1:
-                    for n in range(EARLY_TILES, TILES):
+                    for n in range(MERGED_FROM, TILES):
                         second_product([(c - 1, n), (c, n)])
 
         def scatter(c, n, chunks=1):
             bank, at = y_place[c, n]
             lo, hi = W * c, W * (c + chunks)
-            nc.scalar.activation(y_neg[:, n, lo:hi], bank[:, at : at + hi - lo], ACT.Copy, scale=-1.0)
+            rows = y_neg[:, S * n + lo : S * n + hi]
+            nc.scalar.activation(rows, bank[:, at : at + hi - lo], ACT.Copy, scale=-1.0)
             nc.vector.tensor_tensor(
-                page_neg[n][:].indirect(offs2_t[:, lo // LIST : hi // LIST]),
-                y_neg[:, n, lo:hi], wgo_t[:, lo:hi], ALU.mult,
+                page_neg[n][:].indirect(offs2_t[:, lo // LIST : hi // LIST]), rows, wgo_t[:, lo:hi], ALU.mult
             )
 
-        def finish(n):
+        def blocks_of(half):
+            return [(b, slice(BANK * half + P * b, BANK * half + P * (b + 1))) for b in range(4)]
+
+        def turn_x0(n):
             for half in range(2):
-                cols = slice(BANK * half, BANK * (half + 1))
-                if n < EARLY_TILES:
-                    bank = arg_bank([P, 4, P])
-                    blocks = [(b, slice(BANK * half + P * b, BANK * half + P * (b + 1))) for b in range(4)]
-                    for b, blk in blocks:
-                        nc.tensor.matmul(
-                            bank[:, b, :], x0_t[n][:, blk], ident[:], start=(b == 0), stop=False, is_transpose=True
-                        )
-                    for b, blk in blocks:
+                x0_bank[n, half] = arg_bank([P, 4, P])
+                for b, blk in blocks_of(half):
+                    nc.tensor.matmul(
+                        x0_bank[n, half][:, b, :], x0_t[:, n, blk], ident[:],
+                        start=(b == 0), stop=False, is_transpose=True,
+                    )
+
+        def finish(n):
+            if n < TENSOR_TILES:
+                turned = {}
+                for half in range(2):
+                    bank = x0_bank[n, half]
+                    for b, blk in blocks_of(half):
                         nc.tensor.matmul(
                             bank[:, b, :], page_neg[n][:, blk], ident[:], start=False, stop=(b == 3), is_transpose=True
                         )
-                    turned = held("turned%d%d" % (n, half), [P, 4, P], F32)
-                    nc.scalar.activation(turned[:], bank[:], ACT.Abs, bias=zero_bias[:])
-                    for b, blk in blocks:
-                        nc.tensor.transpose(bank[:, b, :], turned[:, b, :], ident[:])
-                    result = y_neg[:, n, cols]
-                    nc.scalar.copy(out=result, in_=bank[:].rearrange("p b j -> p (b j)"))
-                else:
-                    if half not in late_diff:
-                        name = "turned%d%d" % (EARLY_TILES - 1, half)
-                        late_diff[half] = held(name, [P, TILES - EARLY_TILES, BANK], F32)
-                    result = late_diff[half][:, n - EARLY_TILES, :]
-                    nc.vector.tensor_tensor(result, page_neg[n][:, cols], x0_t[n][:, cols], ALU.add)
+                    turned[half] = turned_bufs[2 * (n % 2) + half]
+                    nc.scalar.activation(turned[half][:], bank[:], ACT.Abs, bias=zero_bias[:])
+                for half in range(2):
+                    bank = x0_bank[n, half]
+                    cols = slice(BANK * half, BANK * (half + 1))
+                    for b, blk in blocks_of(half):
+                        nc.tensor.transpose(bank[:, b, :], turned[half][:, b, :], ident[:])
+                    nc.scalar.copy(out=x0_t[:, n, cols], in_=bank[:].rearrange("p b j -> p (b j)"))
+                    nc.sync.dma_start(out=out[P * n : P * (n + 1), cols], in_=x0_t[:, n, cols])
+            else:
+                for half in range(2):
+                    cols = slice(BANK * half, BANK * (half + 1))
+                    result = turned_bufs[2 * (n % 2) + half][:].rearrange("p b j -> p (b j)")
+                    nc.vector.tensor_tensor(result, page_neg[n][:, cols], x0_t[:, n, cols], ALU.add)
                     nc.scalar.activation(result, result, ACT.Abs, bias=zero_bias[:])
-                nc.sync.dma_start(out=out[P * n : P * (n + 1), cols], in_=result)
+                    nc.sync.dma_start(out=out[P * n : P * (n + 1), cols], in_=result)
 
         nc.vector.tensor_scalar(phase_turns[:], phase_t[:], 1.0 / TWO_PI, None, ALU.mult)
-
-        quantise_w1(0, 0, False)
-        quantise_w1(1, 0, False)
-        gather_words(0, 0)
-        gather_words(0, 1)
-        quantise_w1(0, 1, False)
-        quantise_w1(1, 1, True)
+        gain_wide = held("gain_wide", [P, 2, SPREAD, PACK], F32)
+        nc.scalar.copy(out=gain_wide[:], in_=gain_t[:].unsqueeze(2).to_broadcast([P, 2, SPREAD, PACK]))
         quantise_stress(0, False)
-        gain_wide = held("gain_wide", [P, 2, W, PACK], F32)
-        nc.scalar.copy(out=gain_wide[:], in_=gain_t[:].unsqueeze(2).to_broadcast([P, 2, W, PACK]))
-        gather_words(1, 0)
+        quantise_w1(0, 0, 0)
+        quantise_w1(0, 1, 80)
         argument(0)
-        argument(1)
+        quantise_stress(1, False)
+        quantise_w1(1, 0, 128)
         reduce_turns(0)
-        gather_words(1, 1)
-        quantise_stress(1, True)
+        quantise_w1(1, 1, 128)
+        argument(1)
 
-        for g in range(2):
-            pair = held("w1_raw%d" % g, [P, 2, S], F32)
-            rows = x0[2 * P * g : 2 * P * (g + 1), :]
-            nc.sync.dma_start(out=pair[:], in_=rows.rearrange("(n p) j -> p n j", n=2))
-            x0_t[2 * g] = pair[:, 0, :]
-            x0_t[2 * g + 1] = pair[:, 1, :]
-
-        waiting = [(c, n) for c in range(CHUNKS - 1) for n in own_tiles(c)]
-        places = {FIRST_SCATTER_PLACE + e: pick for e, pick in enumerate(waiting)}
+        places = {}
+        place = 0
+        for c in range(CHUNKS - 1):
+            place = max(place, 3 * (UNITS.index((c, 1)) + 1) + 1, 11 if c < CHUNKS - 2 else 21)
+            for n in own_tiles(c):
+                places[place] = (c, n)
+                place = place + 1
         last = len(UNITS) - 1
+
+        def use_place(place):
+            if place in places:
+                scatter(*places[place])
+
         for i, (c, a) in enumerate(UNITS):
             if 0 < i < last:
                 argument(i + 1)
+            if i == last - 1:
+                for n in range(TENSOR_TILES):
+                    turn_x0(n)
+            use_place(3 * i)
             sine(i)
-            if 2 * i in places:
-                scatter(*places[2 * i])
+            use_place(3 * i + 1)
             if i < last:
                 reduce_turns(i + 1)
-            if a == 1 and c + 2 < CHUNKS:
-                quantise_stress(c + 2, False)
+            apply_gain(i)
+            use_place(3 * i + 2)
             quantise_h(i)
-            if 2 * i + 1 in places:
-                scatter(*places[2 * i + 1])
-        for place in range(2 * len(UNITS), FIRST_SCATTER_PLACE + len(waiting)):
-            scatter(*places[place])
+            if i in (0, 2):
+                quantise_stress(2 if i == 0 else 3, True)
+        for place in range(3 * len(UNITS), max(places) + 1):
+            use_place(place)
 
         for n in range(TILES):
-            if n < EARLY_TILES:
+            if n < MERGED_FROM:
                 scatter(CHUNKS - 1, n)
             else:
                 scatter(CHUNKS - 2, n, chunks=2)

@@ -29,12 +29,12 @@ TILES = N // P
 UNITS = [(0, 0), (1, 0), (0, 1), (1, 1)] + [(c, a) for c in range(2, CHUNKS) for a in range(H // PASS)]
 TWO_PI = 2.0 * math.pi
 
-TURNS_ON_VECTOR = 4
+TURNS_ON_VECTOR = 2
 GAIN_ON_VECTOR = 4
 WEAVE_ON_SCALAR_FROM = 4
 SPREAD = 32
 FIRST_SCATTER_PLACE = 11
-MERGED_FROM = 4
+MERGED_FROM = 3
 TENSOR_TILES = 2
 
 
@@ -115,7 +115,6 @@ def tile_list_morton_grain_corrections_kernel(
         nc.sync.dma_start(out=phase_t[:], in_=phase.rearrange("(a p t) -> p a t", a=2, t=PACK))
         load_stress(0)
         load_w1(0, 0)
-        nc.sync.dma_start(out=gain_t[:], in_=gain.rearrange("(a p t) -> p a t", a=2, t=PACK))
         nc.vector.tensor_copy(picked_rows[:], tab_s[:].indirect(offs_t[:]))
         for quad in range(4):
             nc.sync.dma_start(
@@ -123,6 +122,7 @@ def tile_list_morton_grain_corrections_kernel(
                 in_=picked_rows[8 * quad : 8 * quad + 8, :].bitcast(I32),
             )
         load_w1(0, 1)
+        nc.sync.dma_start(out=gain_t[:], in_=gain.rearrange("(a p t) -> p a t", a=2, t=PACK))
         load_stress(1)
         load_w1(1, 0)
         load_w1(1, 1)
@@ -151,13 +151,14 @@ def tile_list_morton_grain_corrections_kernel(
         def buffers(name, count, shape, dtype):
             return [held("%s%d" % (name, e), shape, dtype) for e in range(count)]
 
-        w1_woven = held("w1_woven", [P, PACK * PASS], BF16)
+        w1_woven = buffers("w1_woven", 2, [P, PACK * PASS], BF16)
         woven_bufs = buffers("woven", 2, [P, PACK * W], BF16)
         turns_bufs = buffers("turns", 3, [P, PACK, W], F32)
         whole_bufs = buffers("whole", 2, [P, PACK * W], I32)
         cosine_bufs = buffers("cosine", 2, [P, PACK * W], F32)
         slices_bufs = buffers("h_slices", 2, [P, PACK, W], BF16)
-        turned_bufs = buffers("turned", 4, [P, 4, P], F32)
+        turned_bufs = buffers("turned", 2 * TENSOR_TILES, [P, 4, P], F32)
+        late_diff = held("late_diff", [P, 4, BANK], F32)
         woven_uses = []
 
         def next_woven():
@@ -167,8 +168,8 @@ def tile_list_morton_grain_corrections_kernel(
         w1_c, w1_s, st_c, st_s, h_c, h_s = {}, {}, {}, {}, {}, {}
         turns, cosine, y_place, y_rows, x0_bank = {}, {}, {}, {}, {}
 
-        def quantise_w1(a, g, vector_columns):
-            woven = w1_woven
+        def quantise_w1(a, g, vector_columns, pieces=1):
+            woven = w1_woven[max(a, g)]
             dst = woven[:].rearrange("p (t m i) -> p m i t", t=PACK, i=PACK)
             src = w1_raw[a, g][:].rearrange("p i (m t) -> p m i t", t=PACK)
             if vector_columns > 0:
@@ -177,7 +178,12 @@ def tile_list_morton_grain_corrections_kernel(
                 cast(False, dst[:, vector_columns:], src[:, vector_columns:])
             w1_c[a, g] = held("w1_c%d%d" % (a, g), [P, PASS], U32)
             w1_s[a, g] = held("w1_s%d%d" % (a, g), [P, PASS], U8)
-            nc.vector.quantize_mx(out=w1_c[a, g][:].bitcast(FP8X4), scales=w1_s[a, g][:], in_=woven[:])
+            for lo in range(0, PASS, PASS // pieces):
+                hi = lo + PASS // pieces
+                nc.vector.quantize_mx(
+                    out=w1_c[a, g][:, lo:hi].bitcast(FP8X4), scales=w1_s[a, g][:, lo:hi],
+                    in_=woven[:, PACK * lo : PACK * hi],
+                )
 
         def quantise_stress(c, on_vector):
             woven = next_woven()
@@ -337,8 +343,11 @@ def tile_list_morton_grain_corrections_kernel(
                         nc.tensor.matmul(
                             bank[:, b, :], page_neg[n][:, blk], ident[:], start=False, stop=(b == 3), is_transpose=True
                         )
-                    turned[half] = turned_bufs[2 * (n % 2) + half]
-                    nc.scalar.activation(turned[half][:], bank[:], ACT.Abs, bias=zero_bias[:])
+                    if 2 * n + half != 3:
+                        turned[half] = turned_bufs[2 * n + half][:]
+                    else:
+                        turned[half] = late_diff[:, :, 0:P]
+                    nc.scalar.activation(turned[half], bank[:], ACT.Abs, bias=zero_bias[:])
                 for half in range(2):
                     bank = x0_bank[n, half]
                     cols = slice(BANK * half, BANK * (half + 1))
@@ -349,28 +358,32 @@ def tile_list_morton_grain_corrections_kernel(
             else:
                 for half in range(2):
                     cols = slice(BANK * half, BANK * (half + 1))
-                    result = turned_bufs[2 * (n % 2) + half][:].rearrange("p b j -> p (b j)")
+                    result = late_diff[:, 2 * (n - TENSOR_TILES) + half, :]
                     nc.vector.tensor_tensor(result, page_neg[n][:, cols], x0_t[:, n, cols], ALU.add)
-                    nc.scalar.activation(result, result, ACT.Abs, bias=zero_bias[:])
+                    if 2 * n + half >= 8:
+                        nc.vector.scalar_tensor_tensor(x0_t[:, n, cols], result, -1.0, result, ALU.mult, ALU.max)
+                        result = x0_t[:, n, cols]
+                    else:
+                        nc.scalar.activation(result, result, ACT.Abs, bias=zero_bias[:])
                     nc.sync.dma_start(out=out[P * n : P * (n + 1), cols], in_=result)
 
         nc.vector.tensor_scalar(phase_turns[:], phase_t[:], 1.0 / TWO_PI, None, ALU.mult)
+        quantise_stress(0, False)
+        quantise_w1(0, 0, 64)
+        quantise_w1(0, 1, 80, pieces=2)
+        argument(0)
         gain_wide = held("gain_wide", [P, 2, SPREAD, PACK], F32)
         nc.scalar.copy(out=gain_wide[:], in_=gain_t[:].unsqueeze(2).to_broadcast([P, 2, SPREAD, PACK]))
-        quantise_stress(0, False)
-        quantise_w1(0, 0, 0)
-        quantise_w1(0, 1, 80)
-        argument(0)
         quantise_stress(1, False)
         quantise_w1(1, 0, 128)
         reduce_turns(0)
-        quantise_w1(1, 1, 128)
+        quantise_w1(1, 1, 80)
         argument(1)
 
         places = {}
         place = 0
         for c in range(CHUNKS - 1):
-            place = max(place, 3 * (UNITS.index((c, 1)) + 1) + 1, 11 if c < CHUNKS - 2 else 21)
+            place = max(place, 3 * (UNITS.index((c, 1)) + 1) + 1, 11 if c < CHUNKS - 2 else 22)
             for n in own_tiles(c):
                 places[place] = (c, n)
                 place = place + 1

@@ -186,15 +186,15 @@ def tile_list_morton_grain_corrections_kernel(
                 )
 
         def quantise_stress(c, on_vector):
-            woven = next_woven()
+            woven = next_woven()[:] if c != -1 else w1_woven[1][:, PACK * W :]
             cast(
                 on_vector,
-                woven[:].rearrange("p (j e i) -> p j i e", e=4, i=PACK),
+                woven.rearrange("p (j e i) -> p j i e", e=4, i=PACK),
                 st_raw[c][:].rearrange("p i (j e) -> p j i e", e=4),
             )
             st_c[c] = held("st_c%d" % c, [P, W], U32)
             st_s[c] = held("st_s%d" % c, [P, W], U8)
-            nc.vector.quantize_mx(out=st_c[c][:].bitcast(FP8X4), scales=st_s[c][:], in_=woven[:])
+            nc.vector.quantize_mx(out=st_c[c][:].bitcast(FP8X4), scales=st_s[c][:], in_=woven)
 
         v_c = [held("v_c%d" % g, [P, S], U32) for g in range(2)]
         for g in range(2):
@@ -242,17 +242,22 @@ def tile_list_morton_grain_corrections_kernel(
                         bias=phase_turns[:, a, t : t + 1], scale=1.0 / TWO_PI,
                     )
 
+        def gain_on_vector(i):
+            return not GAIN_ON_VECTOR <= i < 8
+
         def reduce_turns(i):
-            flat = turns[i][:].rearrange("p t j -> p (t j)")
-            whole = whole_bufs[i % 2]
-            if 2 <= i < TURNS_ON_VECTOR:
-                nc.vector.tensor_scalar(whole[:], flat, -0.25, None, ALU.add)
-            else:
-                nc.scalar.activation(whole[:].bitcast(U32), flat, ACT.Copy, bias=-0.25)
-            nc.vector.tensor_tensor(flat, flat, whole[:], ALU.subtract)
+            width = BANK if i < 0 else PACK * W
+            for lo in range(0, PACK * W, width):
+                flat = turns[i][:].rearrange("p t j -> p (t j)")[:, lo : lo + width]
+                whole = whole_bufs[i % 2][:, lo : lo + width]
+                if i in ():
+                    nc.vector.tensor_scalar(whole, flat, -0.25, None, ALU.add)
+                else:
+                    nc.scalar.activation(whole.bitcast(U32), flat, ACT.Copy, bias=-0.25)
+                nc.vector.tensor_tensor(flat, flat, whole, ALU.subtract)
 
         def sine(i):
-            if i < GAIN_ON_VECTOR:
+            if gain_on_vector(i):
                 cosine[i] = cosine_bufs[i % 2]
                 dst = cosine[i][:].rearrange("p (j e t) -> p j t e", e=4, t=PACK)
                 src = turns[i][:].rearrange("p t (j e) -> p j t e", e=4)
@@ -279,7 +284,7 @@ def tile_list_morton_grain_corrections_kernel(
             return list(range(TILES if c < CHUNKS - 2 else MERGED_FROM))
 
         def apply_gain(i):
-            if i >= GAIN_ON_VECTOR:
+            if not gain_on_vector(i):
                 a = UNITS[i][1]
                 for t in range(PACK):
                     nc.scalar.activation(
@@ -289,7 +294,7 @@ def tile_list_morton_grain_corrections_kernel(
         def quantise_h(i):
             c, a = UNITS[i]
             woven = next_woven()
-            if i < GAIN_ON_VECTOR:
+            if gain_on_vector(i):
                 nc.vector.tensor_tensor(
                     woven[:].rearrange("p (u x) -> p u x", x=SPREAD * PACK),
                     cosine[i][:].rearrange("p (u x) -> p u x", x=SPREAD * PACK),
@@ -313,10 +318,11 @@ def tile_list_morton_grain_corrections_kernel(
                     for n in range(MERGED_FROM, TILES):
                         second_product([(c - 1, n), (c, n)])
 
-        def scatter(c, n, chunks=1):
+        def scatter(c, n, chunks=1, rows=None):
             bank, at = y_place[c, n]
             lo, hi = W * c, W * (c + chunks)
-            rows = y_neg[:, S * n + lo : S * n + hi]
+            if rows is None:
+                rows = y_neg[:, S * n + lo : S * n + hi]
             nc.scalar.activation(rows, bank[:, at : at + hi - lo], ACT.Copy, scale=-1.0)
             nc.vector.tensor_tensor(
                 page_neg[n][:].indirect(offs2_t[:, lo // LIST : hi // LIST]), rows, wgo_t[:, lo:hi], ALU.mult
@@ -383,11 +389,12 @@ def tile_list_morton_grain_corrections_kernel(
         places = {}
         place = 0
         for c in range(CHUNKS - 1):
-            place = max(place, 3 * (UNITS.index((c, 1)) + 1) + 1, 11 if c < CHUNKS - 2 else 22)
+            place = max(place, 3 * (UNITS.index((c, 1)) + 1) + 1, 11 if c < CHUNKS - 2 else 20)
             for n in own_tiles(c):
                 places[place] = (c, n)
                 place = place + 1
         last = len(UNITS) - 1
+        kept = places.pop(max(places))
 
         def use_place(place):
             if place in places:
@@ -407,10 +414,10 @@ def tile_list_morton_grain_corrections_kernel(
             apply_gain(i)
             use_place(3 * i + 2)
             quantise_h(i)
-            if i in (0, 2):
-                quantise_stress(2 if i == 0 else 3, True)
-        for place in range(3 * len(UNITS), max(places) + 1):
-            use_place(place)
+            if i in (1, 2):
+                quantise_stress(2 if i == 1 else 3, True)
+        spent = slices_bufs[last % 2][:].rearrange("p t j -> p (t j)").bitcast(F32)
+        scatter(*kept, rows=spent[:, 0:W])
 
         for n in range(TILES):
             if n < MERGED_FROM:

@@ -32,10 +32,12 @@ TWO_PI = 2.0 * math.pi
 TURNS_ON_VECTOR = 2
 GAIN_ON_VECTOR = 4
 WEAVE_ON_SCALAR_FROM = 4
+GATE = 0
 SPREAD = 32
 FIRST_SCATTER_PLACE = 11
-MERGED_FROM = 3
-TENSOR_TILES = 2
+MERGED_FROM = 4
+TENSOR_HALVES = 2
+LAST_PIECES = (0, 512, 768, 1024)
 
 
 def tile_list_morton_grain_corrections_kernel(
@@ -50,8 +52,11 @@ def tile_list_morton_grain_corrections_kernel(
         def held(name, shape, dtype):
             return keep.tile(shape, dtype, name=name, align_bytes=64)
 
+        taken = []
+
         def arg_bank(shape):
-            return psum.tile(shape, F32, name="arg_bank", bufs=6)
+            taken.append(shape)
+            return psum.tile(shape, F32, name="arg_bank%d" % ((len(taken) - 1) % 6))
 
         def cast(on_vector, dst, src):
             if on_vector:
@@ -113,6 +118,7 @@ def tile_list_morton_grain_corrections_kernel(
         load_tab(1)
         nc.sync.dma_start(out=w2_raw[:].bitcast(I32), in_=w2_words[0].bitcast(I32))
         nc.sync.dma_start(out=phase_t[:], in_=phase.rearrange("(a p t) -> p a t", a=2, t=PACK))
+        nc.sync.dma_start(out=gain_t[:], in_=gain.rearrange("(a p t) -> p a t", a=2, t=PACK))
         load_stress(0)
         load_w1(0, 0)
         nc.vector.tensor_copy(picked_rows[:], tab_s[:].indirect(offs_t[:]))
@@ -122,7 +128,6 @@ def tile_list_morton_grain_corrections_kernel(
                 in_=picked_rows[8 * quad : 8 * quad + 8, :].bitcast(I32),
             )
         load_w1(0, 1)
-        nc.sync.dma_start(out=gain_t[:], in_=gain.rearrange("(a p t) -> p a t", a=2, t=PACK))
         load_stress(1)
         load_w1(1, 0)
         load_w1(1, 1)
@@ -157,8 +162,9 @@ def tile_list_morton_grain_corrections_kernel(
         whole_bufs = buffers("whole", 2, [P, PACK * W], I32)
         cosine_bufs = buffers("cosine", 2, [P, PACK * W], F32)
         slices_bufs = buffers("h_slices", 2, [P, PACK, W], BF16)
-        turned_bufs = buffers("turned", 2 * TENSOR_TILES, [P, 4, P], F32)
+        turned_bufs = buffers("turned", TENSOR_HALVES, [P, 4, P], F32)
         late_diff = held("late_diff", [P, 4, BANK], F32)
+        halves = [(n, half) for n in range(TILES - 1) for half in range(2)]
         woven_uses = []
 
         def next_woven():
@@ -200,9 +206,11 @@ def tile_list_morton_grain_corrections_kernel(
         for g in range(2):
             nc.vector.tensor_copy(v_c[g][:], tab_w[g][:].indirect(offs_t[:]))
 
-        x0_t = held("tab_w0", [P, TILES, S], F32)
-        nc.sync.dma_start(out=x0_t[:, 0:2, :], in_=x0[0 : 2 * P, :].rearrange("(n p) j -> p n j", n=2))
-        nc.sync.dma_start(out=x0_t[:, 2:4, :], in_=x0[2 * P : 4 * P, :].rearrange("(n p) j -> p n j", n=2))
+        x0_flat = held("tab_w0", [P, TILES * S + W], F32)
+        x0_rows = {n: x0_flat[:, S * e : S * (e + 1)] for e, n in enumerate((0, 2, 3, 1))}
+        for n in range(TILES):
+            nc.sync.dma_start(out=x0_rows[n], in_=x0[P * n : P * (n + 1), :])
+        last_out = [x0_flat[:, 3 * S + W : 3 * S + W + BANK], x0_flat[:, 3 * S + W + BANK : 4 * S + W], x0_rows[2][:, :BANK], x0_rows[2][:, BANK:]]
         y_neg = held("tab_w1", [P, TILES * S], F32)
         page_neg = [held("page_neg%d" % n, [P, S], F32) for n in range(TILES)]
 
@@ -265,8 +273,8 @@ def tile_list_morton_grain_corrections_kernel(
                 dst = src = turns[i][:].rearrange("p t j -> p (t j)")
             nc.scalar.activation(dst, src, ACT.Sin, bias=math.pi / 2, scale=-TWO_PI)
 
-        def second_product(parts):
-            bank = psum.tile([P, BANK], F32, name="y_bank", bufs=2)
+        def second_product(parts, spare=False):
+            bank = arg_bank([P, BANK]) if spare else psum.tile([P, BANK], F32, name="y_bank", bufs=2)
             for e, (c, n) in enumerate(parts):
                 y_place[c, n] = (bank, W * e)
                 for a in range(2):
@@ -312,11 +320,20 @@ def tile_list_morton_grain_corrections_kernel(
             nc.vector.quantize_mx(out=h_c[c, a][:].bitcast(FP8X4), scales=h_s[c, a][:], in_=woven[:])
             if (c, 0) in h_c and (c, 1) in h_c:
                 tiles = own_tiles(c)
-                for lo in range(0, len(tiles), 2):
-                    second_product([(c, n) for n in tiles[lo : lo + 2]])
                 if c == CHUNKS - 1:
-                    for n in range(MERGED_FROM, TILES):
-                        second_product([(c - 1, n), (c, n)])
+                    second_product([(c, 0)])
+                    second_product([(c, 1)])
+                    second_product([(c, 2)], spare=True)
+                    second_product([(c, 3)], spare=True)
+                else:
+                    for lo in range(0, len(tiles), 2):
+                        second_product([(c, n) for n in tiles[lo : lo + 2]])
+
+        def rows_of(c, n, chunks=1):
+            return y_neg[:, S * n + W * c : S * n + W * (c + chunks)]
+
+        def places_of(c, n, chunks=1):
+            return page_neg[n][:].indirect(offs2_t[:, W * c // LIST : W * (c + chunks) // LIST])
 
         def scatter(c, n, chunks=1, rows=None):
             bank, at = y_place[c, n]
@@ -331,55 +348,42 @@ def tile_list_morton_grain_corrections_kernel(
         def blocks_of(half):
             return [(b, slice(BANK * half + P * b, BANK * half + P * (b + 1))) for b in range(4)]
 
-        def turn_x0(n):
-            for half in range(2):
-                x0_bank[n, half] = arg_bank([P, 4, P])
-                for b, blk in blocks_of(half):
-                    nc.tensor.matmul(
-                        x0_bank[n, half][:, b, :], x0_t[:, n, blk], ident[:],
-                        start=(b == 0), stop=False, is_transpose=True,
-                    )
+        def turn_x0(n, half):
+            x0_bank[n, half] = arg_bank([P, 4, P])
+            for b, blk in blocks_of(half):
+                nc.tensor.matmul(
+                    x0_bank[n, half][:, b, :], x0_rows[n][:, blk], ident[:],
+                    start=(b == 0), stop=False, is_transpose=True,
+                )
 
-        def finish(n):
-            if n < TENSOR_TILES:
-                turned = {}
-                for half in range(2):
-                    bank = x0_bank[n, half]
-                    for b, blk in blocks_of(half):
-                        nc.tensor.matmul(
-                            bank[:, b, :], page_neg[n][:, blk], ident[:], start=False, stop=(b == 3), is_transpose=True
-                        )
-                    if 2 * n + half != 3:
-                        turned[half] = turned_bufs[2 * n + half][:]
-                    else:
-                        turned[half] = late_diff[:, :, 0:P]
-                    nc.scalar.activation(turned[half], bank[:], ACT.Abs, bias=zero_bias[:])
-                for half in range(2):
-                    bank = x0_bank[n, half]
-                    cols = slice(BANK * half, BANK * (half + 1))
-                    for b, blk in blocks_of(half):
-                        nc.tensor.transpose(bank[:, b, :], turned[half][:, b, :], ident[:])
-                    nc.scalar.copy(out=x0_t[:, n, cols], in_=bank[:].rearrange("p b j -> p (b j)"))
-                    nc.sync.dma_start(out=out[P * n : P * (n + 1), cols], in_=x0_t[:, n, cols])
-            else:
-                for half in range(2):
-                    cols = slice(BANK * half, BANK * (half + 1))
-                    result = late_diff[:, 2 * (n - TENSOR_TILES) + half, :]
-                    nc.vector.tensor_tensor(result, page_neg[n][:, cols], x0_t[:, n, cols], ALU.add)
-                    if 2 * n + half >= 8:
-                        nc.vector.scalar_tensor_tensor(x0_t[:, n, cols], result, -1.0, result, ALU.mult, ALU.max)
-                        result = x0_t[:, n, cols]
-                    else:
-                        nc.scalar.activation(result, result, ACT.Abs, bias=zero_bias[:])
-                    nc.sync.dma_start(out=out[P * n : P * (n + 1), cols], in_=result)
+        def turn_page(n, half, turned):
+            bank = x0_bank[n, half]
+            for b, blk in blocks_of(half):
+                nc.tensor.matmul(
+                    bank[:, b, :], page_neg[n][:, blk], ident[:], start=False, stop=(b == 3), is_transpose=True
+                )
+            nc.scalar.activation(turned, bank[:], ACT.Abs, bias=zero_bias[:])
+
+        def turn_back(n, half, turned):
+            bank = x0_bank[n, half]
+            cols = slice(BANK * half, BANK * (half + 1))
+            for b, blk in blocks_of(half):
+                nc.tensor.transpose(bank[:, b, :], turned[:, b, :], ident[:])
+            nc.scalar.copy(out=x0_rows[n][:, cols], in_=bank[:].rearrange("p b j -> p (b j)"))
+            nc.sync.dma_start(out=out[P * n : P * (n + 1), cols], in_=x0_rows[n][:, cols])
+
+        def finish(engine, n, cols, result):
+            engine.tensor_tensor(result, page_neg[n][:, cols], x0_rows[n][:, cols], ALU.add)
+            nc.scalar.activation(result, result, ACT.Abs, bias=zero_bias[:])
+            nc.sync.dma_start(out=out[P * n : P * (n + 1), cols], in_=result)
 
         nc.vector.tensor_scalar(phase_turns[:], phase_t[:], 1.0 / TWO_PI, None, ALU.mult)
+        gain_wide = held("gain_wide", [P, 2, SPREAD, PACK], F32)
+        nc.scalar.copy(out=gain_wide[:], in_=gain_t[:].unsqueeze(2).to_broadcast([P, 2, SPREAD, PACK]))
         quantise_stress(0, False)
         quantise_w1(0, 0, 64)
         quantise_w1(0, 1, 80, pieces=2)
         argument(0)
-        gain_wide = held("gain_wide", [P, 2, SPREAD, PACK], F32)
-        nc.scalar.copy(out=gain_wide[:], in_=gain_t[:].unsqueeze(2).to_broadcast([P, 2, SPREAD, PACK]))
         quantise_stress(1, False)
         quantise_w1(1, 0, 128)
         reduce_turns(0)
@@ -404,8 +408,8 @@ def tile_list_morton_grain_corrections_kernel(
             if 0 < i < last:
                 argument(i + 1)
             if i == last - 1:
-                for n in range(TENSOR_TILES):
-                    turn_x0(n)
+                for n, half in halves[:TENSOR_HALVES]:
+                    turn_x0(n, half)
             use_place(3 * i)
             sine(i)
             use_place(3 * i + 1)
@@ -419,9 +423,30 @@ def tile_list_morton_grain_corrections_kernel(
         spent = slices_bufs[last % 2][:].rearrange("p t j -> p (t j)").bitcast(F32)
         scatter(*kept, rows=spent[:, 0:W])
 
-        for n in range(TILES):
-            if n < MERGED_FROM:
-                scatter(CHUNKS - 1, n)
-            else:
-                scatter(CHUNKS - 2, n, chunks=2)
-            finish(n)
+        c = CHUNKS - 1
+        bank, at = y_place[c, 1]
+        nc.vector.scalar_tensor_tensor(
+            rows_of(c, 1), bank[:, at : at + W], -1.0, wgo_t[:, W * c : W * (c + 1)], ALU.mult, ALU.mult
+        )
+        scatter(c, 0)
+        nc.vector.tensor_copy(places_of(c, 1), rows_of(c, 1))
+        for first, n, chunks, weighed in ((c, 2, 1, y_neg[:, S - 3 * P : S - P]), (c, 3, 1, y_neg[:, S - P : S + P])):
+            bank, at = y_place[first, n]
+            rows = rows_of(first, n, chunks)
+            nc.scalar.activation(rows, bank[:, at : at + W * chunks], ACT.Copy, scale=-1.0)
+            nc.gpsimd.tensor_tensor(weighed, rows, wgo_t[:, W * first : W * (first + chunks)], ALU.mult)
+            nc.vector.tensor_copy(places_of(first, n, chunks), weighed)
+        turned = [buf[:] for buf in turned_bufs]
+        turned[GATE] = late_diff[:, :, 0:P]
+        for e in (0, 1):
+            turn_page(*halves[e], turned[e])
+        for e in (0, 1):
+            turn_back(*halves[e], turned[e])
+        for e in range(2, TENSOR_HALVES):
+            turn_page(*halves[e], turned[e])
+        for e in range(2, TENSOR_HALVES):
+            turn_back(*halves[e], turned[e])
+        for half in range(2):
+            finish(nc.gpsimd, 1, slice(BANK * half, BANK * (half + 1)), late_diff[:, half, :])
+        for e, (n, half) in enumerate([(2, 0), (2, 1), (3, 0), (3, 1)]):
+            finish(nc.vector, n, slice(BANK * half, BANK * (half + 1)), last_out[e])

@@ -162,8 +162,8 @@ def tile_list_morton_grain_corrections_kernel(
         whole_bufs = buffers("whole", 2, [P, PACK * W], I32)
         cosine_bufs = buffers("cosine", 2, [P, PACK * W], F32)
         slices_bufs = buffers("h_slices", 2, [P, PACK, W], BF16)
-        turned_bufs = buffers("turned", TENSOR_HALVES, [P, 4, P], F32)
-        late_diff = held("late_diff", [P, 4, BANK], F32)
+        turned_first = held("turned_first", [P, 4, P], F32)
+        late = held("late", [P, 5 * BANK], F32)
         halves = [(n, half) for n in range(TILES - 1) for half in range(2)]
         woven_uses = []
 
@@ -206,11 +206,10 @@ def tile_list_morton_grain_corrections_kernel(
         for g in range(2):
             nc.vector.tensor_copy(v_c[g][:], tab_w[g][:].indirect(offs_t[:]))
 
-        x0_flat = held("tab_w0", [P, TILES * S + W], F32)
-        x0_rows = {n: x0_flat[:, S * e : S * (e + 1)] for e, n in enumerate((0, 2, 3, 1))}
+        x0_flat = held("tab_w0", [P, TILES * S], F32)
+        x0_rows = {n: x0_flat[:, S * e : S * (e + 1)] for e, n in enumerate(range(TILES))}
         for n in range(TILES):
             nc.sync.dma_start(out=x0_rows[n], in_=x0[P * n : P * (n + 1), :])
-        last_out = [x0_flat[:, 3 * S + W : 3 * S + W + BANK], x0_flat[:, 3 * S + W + BANK : 4 * S + W], x0_rows[2][:, :BANK], x0_rows[2][:, BANK:]]
         y_neg = held("tab_w1", [P, TILES * S], F32)
         page_neg = [held("page_neg%d" % n, [P, S], F32) for n in range(TILES)]
 
@@ -372,9 +371,9 @@ def tile_list_morton_grain_corrections_kernel(
             nc.scalar.copy(out=x0_rows[n][:, cols], in_=bank[:].rearrange("p b j -> p (b j)"))
             nc.sync.dma_start(out=out[P * n : P * (n + 1), cols], in_=x0_rows[n][:, cols])
 
-        def finish(engine, n, cols, result):
-            engine.tensor_tensor(result, page_neg[n][:, cols], x0_rows[n][:, cols], ALU.add)
-            nc.scalar.activation(result, result, ACT.Abs, bias=zero_bias[:])
+        def finish(engine, n, cols, diff, result):
+            engine.tensor_tensor(diff, page_neg[n][:, cols], x0_rows[n][:, cols], ALU.add)
+            nc.scalar.activation(result, diff, ACT.Abs, bias=zero_bias[:])
             nc.sync.dma_start(out=out[P * n : P * (n + 1), cols], in_=result)
 
         nc.vector.tensor_scalar(phase_turns[:], phase_t[:], 1.0 / TWO_PI, None, ALU.mult)
@@ -436,17 +435,15 @@ def tile_list_morton_grain_corrections_kernel(
             nc.scalar.activation(rows, bank[:, at : at + W * chunks], ACT.Copy, scale=-1.0)
             nc.gpsimd.tensor_tensor(weighed, rows, wgo_t[:, W * first : W * (first + chunks)], ALU.mult)
             nc.vector.tensor_copy(places_of(first, n, chunks), weighed)
-        turned = [buf[:] for buf in turned_bufs]
-        turned[GATE] = late_diff[:, :, 0:P]
-        for e in (0, 1):
-            turn_page(*halves[e], turned[e])
-        for e in (0, 1):
-            turn_back(*halves[e], turned[e])
-        for e in range(2, TENSOR_HALVES):
-            turn_page(*halves[e], turned[e])
-        for e in range(2, TENSOR_HALVES):
-            turn_back(*halves[e], turned[e])
+        turned = [turned_first[:], late[:, BANK - P // 2 : 5 * BANK - P // 2].rearrange("p (b j) -> p b j", b=4)[:, :, 0:P]]
+        rows = [late[:, BANK * e : BANK * (e + 1)] for e in range(5)]
         for half in range(2):
-            finish(nc.gpsimd, 1, slice(BANK * half, BANK * (half + 1)), late_diff[:, half, :])
+            turn_page(0, half, turned[half])
+        for half in range(2):
+            turn_back(0, half, turned[half])
+        results = [turned_first[:].rearrange("p b j -> p (b j)"), rows[0]]
+        for half in range(2):
+            cols = slice(BANK * half, BANK * (half + 1))
+            finish(nc.gpsimd, 1, cols, x0_rows[1][:, cols], results[half])
         for e, (n, half) in enumerate([(2, 0), (2, 1), (3, 0), (3, 1)]):
-            finish(nc.vector, n, slice(BANK * half, BANK * (half + 1)), last_out[e])
+            finish(nc.vector, n, slice(BANK * half, BANK * (half + 1)), rows[1 + e], rows[1 + e])

@@ -115,8 +115,8 @@ def tile_list_morton_grain_corrections_kernel(
                 out=w2s_raw[32 * quad : 32 * quad + 4, :].bitcast(I32),
                 in_=w2_scales[0, 4 * quad : 4 * quad + 4, :].bitcast(I32),
             )
-        load_tab(1)
         nc.sync.dma_start(out=w2_raw[:].bitcast(I32), in_=w2_words[0].bitcast(I32))
+        load_tab(1)
         nc.sync.dma_start(out=phase_t[:], in_=phase.rearrange("(a p t) -> p a t", a=2, t=PACK))
         nc.sync.dma_start(out=gain_t[:], in_=gain.rearrange("(a p t) -> p a t", a=2, t=PACK))
         load_stress(0)

@@ -174,14 +174,17 @@ def tile_list_morton_grain_corrections_kernel(
         w1_c, w1_s, st_c, st_s, h_c, h_s = {}, {}, {}, {}, {}, {}
         turns, cosine, y_place, y_rows, x0_bank = {}, {}, {}, {}, {}
 
-        def quantise_w1(a, g, vector_columns, pieces=1):
-            woven = w1_woven[max(a, g)]
+        def round_w1(a, g, vector_columns):
+            woven = w1_woven[g]
             dst = woven[:].rearrange("p (t m i) -> p m i t", t=PACK, i=PACK)
             src = w1_raw[a, g][:].rearrange("p i (m t) -> p m i t", t=PACK)
             if vector_columns > 0:
                 cast(True, dst[:, :vector_columns], src[:, :vector_columns])
             if vector_columns < P:
                 cast(False, dst[:, vector_columns:], src[:, vector_columns:])
+
+        def quantise_w1(a, g, pieces=1):
+            woven = w1_woven[g]
             w1_c[a, g] = held("w1_c%d%d" % (a, g), [P, PASS], U32)
             w1_s[a, g] = held("w1_s%d%d" % (a, g), [P, PASS], U8)
             for lo in range(0, PASS, PASS // pieces):
@@ -191,13 +194,18 @@ def tile_list_morton_grain_corrections_kernel(
                     in_=woven[:, PACK * lo : PACK * hi],
                 )
 
-        def quantise_stress(c, on_vector):
-            woven = next_woven()[:] if c != -1 else w1_woven[1][:, PACK * W :]
+        st_woven = {}
+
+        def round_stress(c, on_vector, woven):
+            st_woven[c] = woven
             cast(
                 on_vector,
                 woven.rearrange("p (j e i) -> p j i e", e=4, i=PACK),
                 st_raw[c][:].rearrange("p i (j e) -> p j i e", e=4),
             )
+
+        def quantise_stress(c):
+            woven = st_woven[c]
             st_c[c] = held("st_c%d" % c, [P, W], U32)
             st_s[c] = held("st_s%d" % c, [P, W], U8)
             nc.vector.quantize_mx(out=st_c[c][:].bitcast(FP8X4), scales=st_s[c][:], in_=woven)
@@ -222,16 +230,15 @@ def tile_list_morton_grain_corrections_kernel(
                 slices = [(e, 2 * pair + e) for e in range(2)]
                 for e, t in slices:
                     first = PASS * a + P * t
-                    for lo in range(0, W, P):
-                        nc.tensor.matmul_mx(
-                            out=bank[:, e, lo : lo + P],
-                            lhsT=w2_c[:, 2 * first : 2 * (first + P)].bitcast(FP4X4),
-                            lhsT_scale=w2_s[:, first : first + P],
-                            rhs=st_c[c][:, lo : lo + P].bitcast(FP8X4),
-                            rhs_scale=st_s[c][:, lo : lo + P],
-                            start=(e == 0 and lo == 0),
-                            stop=False,
-                        )
+                    nc.tensor.matmul_mx(
+                        out=bank[:, e, :],
+                        lhsT=w2_c[:, 2 * first : 2 * (first + P)].bitcast(FP4X4),
+                        lhsT_scale=w2_s[:, first : first + P],
+                        rhs=st_c[c][:].bitcast(FP8X4),
+                        rhs_scale=st_s[c][:],
+                        start=(e == 0),
+                        stop=False,
+                    )
                 for g in range(2):
                     for e, t in slices:
                         nc.tensor.matmul_mx(
@@ -298,9 +305,9 @@ def tile_list_morton_grain_corrections_kernel(
                         slices_bufs[i % 2][:, t, :], turns[i][:, t, :], ACT.Copy, scale=gain_t[:, a, t : t + 1]
                     )
 
-        def quantise_h(i):
+        def weave_h(i):
             c, a = UNITS[i]
-            woven = next_woven()
+            woven = woven_bufs[i % 2]
             if gain_on_vector(i):
                 nc.vector.tensor_tensor(
                     woven[:].rearrange("p (u x) -> p u x", x=SPREAD * PACK),
@@ -314,6 +321,10 @@ def tile_list_morton_grain_corrections_kernel(
                     woven[:].rearrange("p (j e t) -> p j t e", e=4, t=PACK),
                     slices_bufs[i % 2][:].rearrange("p t (j e) -> p j t e", e=4),
                 )
+
+        def quantise_h(i):
+            c, a = UNITS[i]
+            woven = woven_bufs[i % 2]
             h_c[c, a] = held("h_c%d%d" % (c, a), [P, W], U32)
             h_s[c, a] = held("h_s%d%d" % (c, a), [P, W], U8)
             nc.vector.quantize_mx(out=h_c[c, a][:].bitcast(FP8X4), scales=h_s[c, a][:], in_=woven[:])
@@ -379,14 +390,20 @@ def tile_list_morton_grain_corrections_kernel(
         nc.vector.tensor_scalar(phase_turns[:], phase_t[:], 1.0 / TWO_PI, None, ALU.mult)
         gain_wide = held("gain_wide", [P, 2, SPREAD, PACK], F32)
         nc.scalar.copy(out=gain_wide[:], in_=gain_t[:].unsqueeze(2).to_broadcast([P, 2, SPREAD, PACK]))
-        quantise_stress(0, False)
-        quantise_w1(0, 0, 64)
-        quantise_w1(0, 1, 80, pieces=2)
+        round_stress(0, False, woven_bufs[0][:])
+        quantise_stress(0)
+        round_w1(0, 0, 64)
+        quantise_w1(0, 0)
+        round_w1(0, 1, 80)
+        quantise_w1(0, 1, pieces=2)
         argument(0)
-        quantise_stress(1, False)
-        quantise_w1(1, 0, 128)
+        round_stress(1, False, woven_bufs[1][:])
+        quantise_stress(1)
+        round_w1(1, 0, 128)
         reduce_turns(0)
-        quantise_w1(1, 1, 80)
+        round_w1(1, 1, 80)
+        quantise_w1(1, 0)
+        quantise_w1(1, 1)
         argument(1)
 
         places = {}
@@ -415,10 +432,16 @@ def tile_list_morton_grain_corrections_kernel(
             if i < last:
                 reduce_turns(i + 1)
             apply_gain(i)
+            if gain_on_vector(i):
+                weave_h(i)
+            if i in (1, 2):
+                round_stress(i + 1, True, woven_bufs[(i + 1) % 2][:])
             use_place(3 * i + 2)
+            if not gain_on_vector(i):
+                weave_h(i)
             quantise_h(i)
             if i in (1, 2):
-                quantise_stress(2 if i == 1 else 3, True)
+                quantise_stress(i + 1)
         spent = slices_bufs[last % 2][:].rearrange("p t j -> p (t j)").bitcast(F32)
         scatter(*kept, rows=spent[:, 0:W])
 

@@ -26,18 +26,12 @@ LIST = 16
 W = 256
 CHUNKS = S // W
 TILES = N // P
-UNITS = [(0, 0), (1, 0), (0, 1), (1, 1)] + [(c, a) for c in range(2, CHUNKS) for a in range(H // PASS)]
+UNITS = [(c, a) for c in range(CHUNKS) for a in range(H // PASS)]
 TWO_PI = 2.0 * math.pi
 
-TURNS_ON_VECTOR = 2
-GAIN_ON_VECTOR = 4
-WEAVE_ON_SCALAR_FROM = 4
-GATE = 0
 SPREAD = 32
-FIRST_SCATTER_PLACE = 11
-MERGED_FROM = 4
-TENSOR_HALVES = 2
-LAST_PIECES = (0, 512, 768, 1024)
+UNIT = PACK * W
+ROUND_ON_VECTOR = 3
 
 
 def tile_list_morton_grain_corrections_kernel(
@@ -78,6 +72,8 @@ def tile_list_morton_grain_corrections_kernel(
         w3_s = held("w3_s", [P, N], U8)
         phase_t = held("phase_t", [P, 2, PACK], F32)
         phase_turns = held("phase_turns", [P, 2, PACK], F32)
+        phase_folded = held("phase_folded", [P, 2, PACK], F32)
+        phase_sine = held("phase_sine", [P, 2, PACK], F32)
         gain_t = held("gain_t", [P, 2, PACK], F32)
         wgo_t = held("wgo_t", [P, S], F32)
         w1_raw = {(a, g): held("w1_raw%d%d" % (a, g), [P, PACK, PASS], F32) for a in range(2) for g in range(2)}
@@ -128,9 +124,9 @@ def tile_list_morton_grain_corrections_kernel(
                 in_=picked_rows[8 * quad : 8 * quad + 8, :].bitcast(I32),
             )
         load_w1(0, 1)
-        load_stress(1)
         load_w1(1, 0)
         load_w1(1, 1)
+        load_stress(1)
         nc.sync.dma_start(out=w3_c[:].bitcast(I32), in_=w3_words.rearrange("a p n i -> p a (n i)").bitcast(I32))
         for quad in range(4):
             nc.sync.dma_start(
@@ -156,27 +152,37 @@ def tile_list_morton_grain_corrections_kernel(
         def buffers(name, count, shape, dtype):
             return [held("%s%d" % (name, e), shape, dtype) for e in range(count)]
 
-        w1_woven = buffers("w1_woven", 2, [P, PACK * PASS], BF16)
-        woven_bufs = buffers("woven", 2, [P, PACK * W], BF16)
-        turns_bufs = buffers("turns", 3, [P, PACK, W], F32)
-        whole_bufs = buffers("whole", 2, [P, PACK * W], I32)
-        cosine_bufs = buffers("cosine", 2, [P, PACK * W], F32)
-        slices_bufs = buffers("h_slices", 2, [P, PACK, W], BF16)
-        turned_first = held("turned_first", [P, 4, P], F32)
-        late = held("late", [P, 5 * BANK], F32)
-        halves = [(n, half) for n in range(TILES - 1) for half in range(2)]
-        woven_uses = []
+        first_woven = held("first_woven", [P, 2 * UNIT], BF16)
+        chain = held("chain", [P, 3 * UNIT], BF16)
+        w1_woven = {
+            (0, 0): first_woven[:], (0, 1): chain[:, 0 : 2 * UNIT],
+            (1, 0): chain[:, 0 : 2 * UNIT], (1, 1): chain[:, UNIT : 3 * UNIT],
+        }
+        first_rest = chain[:, UNIT : 3 * UNIT].bitcast(F32)
+        st_first = held("st_first", [P, UNIT], BF16)
+        turns_bufs = buffers("turns", 2, [P, PACK, W], F32)
+        cosine_bufs = buffers("cosine", 2, [P, PACK, W], F32)
+        slices = held("h_slices", [P, PACK, W], BF16)
+        shared = held("shared", [P, 9 * W], F32)
 
-        def next_woven():
-            woven_uses.append(woven_bufs[len(woven_uses) % 2])
-            return woven_uses[-1]
+        def slots(lo, hi):
+            return shared[:, W * lo : W * hi]
+
+        woven = slots(1, 5).bitcast(BF16)
+        kept_rows = slots(3, 4)
+        whole_bufs = [held("whole_even", [P, UNIT], I32)[:], slots(4, 8).bitcast(I32)]
+        first_whole = held("first_whole", [P, UNIT], I32)[:]
+        rest_odd = held("rest_odd", [P, PACK, W], F32)
+        by_slot = shared[:].rearrange("p (s j) -> p s j", j=W)
+        rest_bufs = [[by_slot[:, 0:2], by_slot[:, 2:9:6]], [rest_odd[:, 0:2], rest_odd[:, 2:4]]]
+        turned_first = held("turned_first", [P, 4, P], F32)
+        turned_second = held("turned_second", [P, 4, P], F32)
 
         w1_c, w1_s, st_c, st_s, h_c, h_s = {}, {}, {}, {}, {}, {}
-        turns, cosine, y_place, y_rows, x0_bank = {}, {}, {}, {}, {}
+        banks, y_place, x0_bank = {}, {}, {}
 
         def round_w1(a, g, vector_columns):
-            woven = w1_woven[g]
-            dst = woven[:].rearrange("p (t m i) -> p m i t", t=PACK, i=PACK)
+            dst = w1_woven[a, g].rearrange("p (t m i) -> p m i t", t=PACK, i=PACK)
             src = w1_raw[a, g][:].rearrange("p i (m t) -> p m i t", t=PACK)
             if vector_columns > 0:
                 cast(True, dst[:, :vector_columns], src[:, :vector_columns])
@@ -184,176 +190,250 @@ def tile_list_morton_grain_corrections_kernel(
                 cast(False, dst[:, vector_columns:], src[:, vector_columns:])
 
         def quantise_w1(a, g, pieces=1):
-            woven = w1_woven[g]
             w1_c[a, g] = held("w1_c%d%d" % (a, g), [P, PASS], U32)
             w1_s[a, g] = held("w1_s%d%d" % (a, g), [P, PASS], U8)
             for lo in range(0, PASS, PASS // pieces):
                 hi = lo + PASS // pieces
                 nc.vector.quantize_mx(
                     out=w1_c[a, g][:, lo:hi].bitcast(FP8X4), scales=w1_s[a, g][:, lo:hi],
-                    in_=woven[:, PACK * lo : PACK * hi],
+                    in_=w1_woven[a, g][:, PACK * lo : PACK * hi],
                 )
 
-        st_woven = {}
+        st_place = {}
 
-        def round_stress(c, on_vector, woven):
-            st_woven[c] = woven
+        def round_stress(c, on_vector, place):
+            st_place[c] = place
             cast(
                 on_vector,
-                woven.rearrange("p (j e i) -> p j i e", e=4, i=PACK),
+                place.rearrange("p (j e i) -> p j i e", e=4, i=PACK),
                 st_raw[c][:].rearrange("p i (j e) -> p j i e", e=4),
             )
 
         def quantise_stress(c):
-            woven = st_woven[c]
             st_c[c] = held("st_c%d" % c, [P, W], U32)
             st_s[c] = held("st_s%d" % c, [P, W], U8)
-            nc.vector.quantize_mx(out=st_c[c][:].bitcast(FP8X4), scales=st_s[c][:], in_=woven)
+            nc.vector.quantize_mx(out=st_c[c][:].bitcast(FP8X4), scales=st_s[c][:], in_=st_place[c])
 
         v_c = [held("v_c%d" % g, [P, S], U32) for g in range(2)]
         for g in range(2):
             nc.vector.tensor_copy(v_c[g][:], tab_w[g][:].indirect(offs_t[:]))
 
-        x0_flat = held("tab_w0", [P, TILES * S], F32)
-        x0_rows = {n: x0_flat[:, S * e : S * (e + 1)] for e, n in enumerate(range(TILES))}
+        x0_flat = held("tab_w0", [P, (TILES + 1) * S], F32)
+        x0_rows = {n: x0_flat[:, S * e : S * (e + 1)] for n, e in enumerate((0, 1, 3, 4))}
         for n in range(TILES):
             nc.sync.dma_start(out=x0_rows[n], in_=x0[P * n : P * (n + 1), :])
-        y_neg = held("tab_w1", [P, TILES * S], F32)
+        y_flat = held("tab_w1", [P, 4 * S], F32)
         page_neg = [held("page_neg%d" % n, [P, S], F32) for n in range(TILES)]
 
         def argument(i):
             c, a = UNITS[i]
             cols = slice(W * c, W * (c + 1))
-            turns[i] = turns_bufs[i % len(turns_bufs)]
             for pair in range(2):
-                bank = arg_bank([P, 2, W])
-                slices = [(e, 2 * pair + e) for e in range(2)]
-                for e, t in slices:
-                    first = PASS * a + P * t
-                    nc.tensor.matmul_mx(
-                        out=bank[:, e, :],
-                        lhsT=w2_c[:, 2 * first : 2 * (first + P)].bitcast(FP4X4),
-                        lhsT_scale=w2_s[:, first : first + P],
-                        rhs=st_c[c][:].bitcast(FP8X4),
-                        rhs_scale=st_s[c][:],
-                        start=(e == 0),
-                        stop=False,
-                    )
-                for g in range(2):
-                    for e, t in slices:
+                bank = banks[i, pair] = arg_bank([P, 2, W])
+                passes = [0, 1, "stress"] if i in (2, 3, 4, 6) else ["stress", 0, 1]
+                for place, g in enumerate(passes):
+                    for e in range(2):
+                        t = 2 * pair + e
+                        first = PASS * a + P * t
+                        if g == "stress":
+                            operands = dict(
+                                lhsT=w2_c[:, 2 * first : 2 * (first + P)].bitcast(FP4X4),
+                                lhsT_scale=w2_s[:, first : first + P],
+                                rhs=st_c[c][:].bitcast(FP8X4),
+                                rhs_scale=st_s[c][:],
+                            )
+                        else:
+                            operands = dict(
+                                lhsT=w1_c[a, g][:, P * t : P * (t + 1)].bitcast(FP8X4),
+                                lhsT_scale=w1_s[a, g][:, P * t : P * (t + 1)],
+                                rhs=v_c[g][:, cols].bitcast(FP8X4),
+                                rhs_scale=v_s[:, S * g + W * c : S * g + W * (c + 1)],
+                            )
                         nc.tensor.matmul_mx(
-                            out=bank[:, e, :],
-                            lhsT=w1_c[a, g][:, P * t : P * (t + 1)].bitcast(FP8X4),
-                            lhsT_scale=w1_s[a, g][:, P * t : P * (t + 1)],
-                            rhs=v_c[g][:, cols].bitcast(FP8X4),
-                            rhs_scale=v_s[:, S * g + W * c : S * g + W * (c + 1)],
-                            start=False,
-                            stop=(g == 1 and e == 1),
+                            out=bank[:, e, :], start=(place == 0 and e == 0), stop=(place == 2 and e == 1), **operands
                         )
-                for e, t in slices:
-                    nc.scalar.activation(
-                        turns[i][:, t, :], bank[:, e, :], ACT.Abs,
-                        bias=phase_turns[:, a, t : t + 1], scale=1.0 / TWO_PI,
-                    )
 
-        def gain_on_vector(i):
-            return not GAIN_ON_VECTOR <= i < 8
+        def whole_of(i):
+            return first_whole if i == 1 else whole_bufs[i % 2]
 
-        def reduce_turns(i):
-            width = BANK if i < 0 else PACK * W
-            for lo in range(0, PACK * W, width):
-                flat = turns[i][:].rearrange("p t j -> p (t j)")[:, lo : lo + width]
-                whole = whole_bufs[i % 2][:, lo : lo + width]
-                if i in ():
-                    nc.vector.tensor_scalar(whole, flat, -0.25, None, ALU.add)
-                else:
-                    nc.scalar.activation(whole.bitcast(U32), flat, ACT.Copy, bias=-0.25)
-                nc.vector.tensor_tensor(flat, flat, whole, ALU.subtract)
+        def turns_out(i):
+            a = UNITS[i][1]
+            for t in range(PACK):
+                nc.scalar.activation(
+                    turns_bufs[i % 2][:, t, :], banks[i, t // 2][:, t % 2, :], ACT.Identity,
+                    bias=phase_turns[:, a, t : t + 1], scale=1.0 / TWO_PI,
+                )
+
+        def folded_turns_out(i):
+            a = UNITS[i][1]
+            for t in range(PACK):
+                nc.scalar.activation(
+                    turns_bufs[i % 2][:, t, :], banks[i, t // 2][:, t % 2, :], ACT.Abs,
+                    bias=phase_folded[:, a, t : t + 1], scale=1.0 / TWO_PI,
+                )
+
+        def folded_round(i):
+            flat = turns_bufs[i % 2][:].rearrange("p t j -> p (t j)")
+            nc.scalar.activation(whole_of(i).bitcast(U32), flat, ACT.Copy, bias=-0.25)
+
+        def folded_rest_of(i):
+            return first_rest if i == 0 else turns_bufs[i % 2][:].rearrange("p t j -> p (t j)")
+
+        def folded_rest(i):
+            flat = turns_bufs[i % 2][:].rearrange("p t j -> p (t j)")
+            nc.vector.tensor_tensor(folded_rest_of(i), flat, whole_of(i), ALU.subtract)
+
+        def folded_sine(i):
+            nc.scalar.activation(
+                cosine_bufs[i % 2][:].rearrange("p t j -> p (t j)").rearrange("p (j e t) -> p j t e", e=4, t=PACK),
+                folded_rest_of(i).rearrange("p (t j e) -> p j t e", t=PACK, e=4),
+                ACT.Sin, bias=math.pi / 2, scale=-TWO_PI,
+            )
+
+        def folded_gain(i, engine):
+            a = UNITS[i][1]
+            engine.tensor_tensor(
+                woven_of(i).rearrange("p (u x) -> p u x", x=SPREAD * PACK),
+                cosine_bufs[i % 2][:].rearrange("p t j -> p (t j)").rearrange("p (u x) -> p u x", x=SPREAD * PACK),
+                gain_wide[:, a].rearrange("p j t -> p (j t)").unsqueeze(1).to_broadcast([P, W // SPREAD, SPREAD * PACK]),
+                ALU.mult,
+            )
+
+        def round_turns(i):
+            nc.gpsimd.tensor_scalar(
+                whole_of(i), turns_bufs[i % 2][:].rearrange("p t j -> p (t j)"), 1.0, 0.0, ALU.mult, ALU.add
+            )
+
+        def round_bank(i, pair):
+            a = UNITS[i][1]
+            for t in (2 * pair, 2 * pair + 1):
+                nc.vector.tensor_scalar(
+                    whole_of(i)[:, W * t : W * (t + 1)], banks[i, pair][:, t % 2, :], 1.0 / TWO_PI,
+                    phase_turns[:, a, t : t + 1], ALU.mult, ALU.add,
+                )
+
+        def take_rest(i, pair):
+            cols = slice(BANK * pair, BANK * (pair + 1))
+            nc.vector.scalar_tensor_tensor(
+                rest_bufs[i % 2][pair], banks[i, pair][:], 1.0 / TWO_PI,
+                whole_of(i)[:, cols].rearrange("p (e j) -> p e j", e=2), ALU.mult, ALU.subtract,
+            )
+
+        def reduce_on_vector(i):
+            for pair in range(2):
+                round_bank(i, pair)
+            rests(i)
+
+        def rests(i):
+            for pair in range(2):
+                take_rest(i, pair)
 
         def sine(i):
-            if gain_on_vector(i):
-                cosine[i] = cosine_bufs[i % 2]
-                dst = cosine[i][:].rearrange("p (j e t) -> p j t e", e=4, t=PACK)
-                src = turns[i][:].rearrange("p t (j e) -> p j t e", e=4)
-            else:
-                dst = src = turns[i][:].rearrange("p t j -> p (t j)")
-            nc.scalar.activation(dst, src, ACT.Sin, bias=math.pi / 2, scale=-TWO_PI)
+            a = UNITS[i][1]
+            for t in range(PACK):
+                nc.scalar.activation(
+                    cosine_bufs[i % 2][:, t, :], rest_bufs[i % 2][t // 2][:, t % 2, :], ACT.Sin,
+                    bias=phase_sine[:, a, t : t + 1], scale=TWO_PI,
+                )
 
-        def second_product(parts, spare=False):
-            bank = arg_bank([P, BANK]) if spare else psum.tile([P, BANK], F32, name="y_bank", bufs=2)
+        def woven_of(i):
+            a = UNITS[i][1]
+            return woven[:, UNIT * a : UNIT * (a + 1)]
+
+        def gain_on_vector(i):
+            a = UNITS[i][1]
+            nc.vector.tensor_tensor(
+                woven_of(i).rearrange("p (j e t) -> p j t e", e=4, t=PACK),
+                cosine_bufs[i % 2][:].rearrange("p t (j e) -> p j t e", e=4),
+                gain_t[:, a].unsqueeze(1).unsqueeze(3).to_broadcast([P, W // 4, PACK, 4]),
+                ALU.mult,
+            )
+
+        def gain_on_gpsimd(i):
+            a = UNITS[i][1]
+            nc.gpsimd.tensor_tensor(
+                woven_of(i).rearrange("p (j t) -> p j t", t=PACK),
+                cosine_bufs[i % 2][:].rearrange("p t j -> p j t"),
+                gain_t[:, a].unsqueeze(1).to_broadcast([P, W, PACK]),
+                ALU.mult,
+            )
+
+        def gain_on_scalar(i):
+            a = UNITS[i][1]
+            for t in range(PACK):
+                nc.scalar.activation(
+                    slices[:, t, :], cosine_bufs[i % 2][:, t, :], ACT.Copy, scale=gain_t[:, a, t : t + 1]
+                )
+
+        def weave_on_scalar(i):
+            nc.scalar.copy(
+                out=woven_of(i).rearrange("p (j e t) -> p j t e", e=4, t=PACK),
+                in_=slices[:].rearrange("p t (j e) -> p j t e", e=4),
+            )
+
+        def second_product(parts, bank):
+            y_banks[parts[0]] = bank
             for e, (c, n) in enumerate(parts):
-                y_place[c, n] = (bank, W * e)
+                y_place[c, n] = bank[:, W * e : W * (e + 1)]
                 for a in range(2):
                     nc.tensor.matmul_mx(
-                        out=bank[:, W * e : W * (e + 1)],
+                        out=y_place[c, n],
                         lhsT=w3_c[:, a, P * n : P * (n + 1)].bitcast(FP8X4),
                         lhsT_scale=w3_s[4 * a : P, P * n : P * (n + 1)],
-                        rhs=h_c[c, a][:].bitcast(FP8X4),
-                        rhs_scale=h_s[c, a][:],
+                        rhs=h_c[c][:, W * a : W * (a + 1)].bitcast(FP8X4),
+                        rhs_scale=h_s[c][:, W * a : W * (a + 1)],
                         start=(a == 0),
                         stop=(a == 1),
                     )
 
-        def own_tiles(c):
-            return list(range(TILES if c < CHUNKS - 2 else MERGED_FROM))
+        y_banks = {}
 
-        def apply_gain(i):
-            if not gain_on_vector(i):
-                a = UNITS[i][1]
-                for t in range(PACK):
-                    nc.scalar.activation(
-                        slices_bufs[i % 2][:, t, :], turns[i][:, t, :], ACT.Copy, scale=gain_t[:, a, t : t + 1]
-                    )
+        def y_bank(e):
+            return psum.tile([P, BANK], F32, name="y_bank%d" % e)
 
-        def weave_h(i):
-            c, a = UNITS[i]
-            woven = woven_bufs[i % 2]
-            if gain_on_vector(i):
-                nc.vector.tensor_tensor(
-                    woven[:].rearrange("p (u x) -> p u x", x=SPREAD * PACK),
-                    cosine[i][:].rearrange("p (u x) -> p u x", x=SPREAD * PACK),
-                    gain_wide[:, a].rearrange("p j t -> p (j t)").unsqueeze(1).to_broadcast([P, W // SPREAD, SPREAD * PACK]),
-                    ALU.mult,
-                )
-            else:
-                cast(
-                    i < WEAVE_ON_SCALAR_FROM,
-                    woven[:].rearrange("p (j e t) -> p j t e", e=4, t=PACK),
-                    slices_bufs[i % 2][:].rearrange("p t (j e) -> p j t e", e=4),
-                )
+        def quantise_h(c):
+            h_c[c] = held("h_c%d" % c, [P, 2 * W], U32)
+            h_s[c] = held("h_s%d" % c, [P, 2 * W], U8)
+            nc.vector.quantize_mx(out=h_c[c][:].bitcast(FP8X4), scales=h_s[c][:], in_=woven)
 
-        def quantise_h(i):
-            c, a = UNITS[i]
-            woven = woven_bufs[i % 2]
-            h_c[c, a] = held("h_c%d%d" % (c, a), [P, W], U32)
-            h_s[c, a] = held("h_s%d%d" % (c, a), [P, W], U8)
-            nc.vector.quantize_mx(out=h_c[c, a][:].bitcast(FP8X4), scales=h_s[c, a][:], in_=woven[:])
-            if (c, 0) in h_c and (c, 1) in h_c:
-                tiles = own_tiles(c)
-                if c == CHUNKS - 1:
-                    second_product([(c, 0)])
-                    second_product([(c, 1)])
-                    second_product([(c, 2)], spare=True)
-                    second_product([(c, 3)], spare=True)
-                else:
-                    for lo in range(0, len(tiles), 2):
-                        second_product([(c, n) for n in tiles[lo : lo + 2]])
+        ahead_of_codes = held("st_c3", [P, W], F32)
 
-        def rows_of(c, n, chunks=1):
-            return y_neg[:, S * n + W * c : S * n + W * (c + chunks)]
+        def wgo_of(c):
+            return wgo_t[:, W * c : W * (c + 1)]
 
-        def places_of(c, n, chunks=1):
-            return page_neg[n][:].indirect(offs2_t[:, W * c // LIST : W * (c + chunks) // LIST])
+        def places_of(c, n):
+            return page_neg[n][:].indirect(offs2_t[:, W * c // LIST : W * (c + 1) // LIST])
 
-        def scatter(c, n, chunks=1, rows=None):
-            bank, at = y_place[c, n]
-            lo, hi = W * c, W * (c + chunks)
-            if rows is None:
-                rows = y_neg[:, S * n + lo : S * n + hi]
-            nc.scalar.activation(rows, bank[:, at : at + hi - lo], ACT.Copy, scale=-1.0)
-            nc.vector.tensor_tensor(
-                page_neg[n][:].indirect(offs2_t[:, lo // LIST : hi // LIST]), rows, wgo_t[:, lo:hi], ALU.mult
+        def rows_of(n):
+            return y_flat[:, W * n : W * (n + 1)]
+
+        def weighed_of(c, n):
+            if n == TILES - 1 and c < CHUNKS - 1:
+                return kept_rows if c < CHUNKS - 2 else None
+            if (c, n) == (0, 2):
+                return ahead_of_codes[:]
+            return y_flat[:, S + W * (4 * (c % 2) + n) : S + W * (4 * (c % 2) + n + 1)]
+
+        def weigh_on_vector(c, n):
+            nc.vector.scalar_tensor_tensor(weighed_of(c, n), y_place[c, n], -1.0, wgo_of(c), ALU.mult, ALU.mult)
+
+        def y_out(c, n, rows=None):
+            nc.scalar.activation(rows_of(n) if rows is None else rows, y_place[c, n], ACT.Copy, scale=-1.0)
+
+        def pair_out(c, n):
+            nc.scalar.activation(y_flat[:, W * n : W * (n + 2)], y_banks[c, n][:], ACT.Copy, scale=-1.0)
+
+        def weigh_on_gpsimd(c, n, count=1):
+            rows = y_flat[:, W * n : W * (n + count)].rearrange("p (e j) -> p e j", e=count)
+            first = S + W * (4 * (c % 2) + n)
+            weighed = weighed_of(c, n) if count == 1 else y_flat[:, first : first + W * count]
+            nc.gpsimd.tensor_tensor(
+                weighed.rearrange("p (e j) -> p e j", e=count), rows,
+                wgo_of(c).unsqueeze(1).to_broadcast([P, count, W]), ALU.mult,
             )
+
+        def scatter(c, n):
+            nc.vector.tensor_copy(places_of(c, n), weighed_of(c, n))
 
         def blocks_of(half):
             return [(b, slice(BANK * half + P * b, BANK * half + P * (b + 1))) for b in range(4)]
@@ -387,86 +467,118 @@ def tile_list_morton_grain_corrections_kernel(
             nc.scalar.activation(result, diff, ACT.Abs, bias=zero_bias[:])
             nc.sync.dma_start(out=out[P * n : P * (n + 1), cols], in_=result)
 
-        nc.vector.tensor_scalar(phase_turns[:], phase_t[:], 1.0 / TWO_PI, None, ALU.mult)
+        nc.vector.tensor_scalar(phase_turns[:], phase_t[:], 1.0 / TWO_PI, 0.25, ALU.mult, ALU.add)
+        nc.vector.tensor_scalar(phase_folded[:], phase_t[:], 1.0 / TWO_PI, None, ALU.mult)
+        nc.vector.tensor_scalar(phase_sine[:], phase_t[:], math.pi / 2, None, ALU.add)
         gain_wide = held("gain_wide", [P, 2, SPREAD, PACK], F32)
         nc.scalar.copy(out=gain_wide[:], in_=gain_t[:].unsqueeze(2).to_broadcast([P, 2, SPREAD, PACK]))
-        round_stress(0, False, woven_bufs[0][:])
+        round_stress(0, False, st_first[:])
         quantise_stress(0)
         round_w1(0, 0, 64)
         quantise_w1(0, 0)
         round_w1(0, 1, 80)
         quantise_w1(0, 1, pieces=2)
         argument(0)
-        round_stress(1, False, woven_bufs[1][:])
-        quantise_stress(1)
+        folded_turns_out(0)
         round_w1(1, 0, 128)
-        reduce_turns(0)
-        round_w1(1, 1, 80)
         quantise_w1(1, 0)
-        quantise_w1(1, 1)
+        folded_round(0)
+        round_w1(1, 1, 128)
+        quantise_w1(1, 1, pieces=2)
         argument(1)
+        folded_rest(0)
+        round_stress(1, False, chain[:, 0:UNIT])
+        quantise_stress(1)
+        folded_sine(0)
+        reduce_on_vector(1)
+        argument(2)
+        argument(3)
+        sine(1)
+        folded_gain(0, nc.vector)
+        gain_on_vector(1)
+        folded_turns_out(2)
+        folded_round(2)
+        turns_out(3)
 
-        places = {}
-        place = 0
-        for c in range(CHUNKS - 1):
-            place = max(place, 3 * (UNITS.index((c, 1)) + 1) + 1, 11 if c < CHUNKS - 2 else 20)
-            for n in own_tiles(c):
-                places[place] = (c, n)
-                place = place + 1
-        last = len(UNITS) - 1
-        kept = places.pop(max(places))
+        last = CHUNKS - 1
+        for c in range(last):
+            even, odd = 2 * c + 2, 2 * c + 3
+            quantise_h(c)
+            second_product([(c, 0), (c, 1)], y_bank(0))
+            second_product([(c, 2), (c, 3)], y_bank(1))
+            if c == 0:
+                folded_rest(even)
+                round_stress(2, True, shared[:, 5 * W // 2 : 9 * W // 2].bitcast(BF16))
+                quantise_stress(2)
+                round_turns(odd)
+                weigh_on_vector(c, 0)
+                scatter(c, 0)
+                y_out(c, 1)
+                folded_sine(even)
+                weigh_on_gpsimd(c, 1)
+                rests(odd)
+                scatter(c, 1)
+            else:
+                rests(even)
+                weigh_on_gpsimd(c - 1, 3)
+                scatter(c - 1, 3)
+                round_turns(odd)
+                pair_out(c, 0)
+                sine(even)
+                weigh_on_gpsimd(c, 0, 2)
+                rests(odd)
+                scatter(c, 0)
+                scatter(c, 1)
+            if c < last - 1:
+                pair_out(c, 2)
+            else:
+                y_out(c, 2)
+            weigh_on_gpsimd(c, 2)
+            scatter(c, 2)
+            if c == 0:
+                round_stress(3, False, first_whole.bitcast(BF16)[:, 0:UNIT])
+                quantise_stress(3)
+            if c < last - 1:
+                argument(even + 2)
+                turns_out(even + 2)
+                round_turns(even + 2)
+            else:
+                for half in range(2):
+                    turn_x0(0, half)
+            if c == 0:
+                folded_gain(even, nc.gpsimd)
+            else:
+                gain_on_gpsimd(even)
+            sine(odd)
+            gain_on_scalar(odd)
+            weave_on_scalar(odd)
+            if c < last - 1:
+                argument(odd + 2)
+                turns_out(odd + 2)
 
-        def use_place(place):
-            if place in places:
-                scatter(*places[place])
-
-        for i, (c, a) in enumerate(UNITS):
-            if 0 < i < last:
-                argument(i + 1)
-            if i == last - 1:
-                for n, half in halves[:TENSOR_HALVES]:
-                    turn_x0(n, half)
-            use_place(3 * i)
-            sine(i)
-            use_place(3 * i + 1)
-            if i < last:
-                reduce_turns(i + 1)
-            apply_gain(i)
-            if gain_on_vector(i):
-                weave_h(i)
-            if i in (1, 2):
-                round_stress(i + 1, True, woven_bufs[(i + 1) % 2][:])
-            use_place(3 * i + 2)
-            if not gain_on_vector(i):
-                weave_h(i)
-            quantise_h(i)
-            if i in (1, 2):
-                quantise_stress(i + 1)
-        spent = slices_bufs[last % 2][:].rearrange("p t j -> p (t j)").bitcast(F32)
-        scatter(*kept, rows=spent[:, 0:W])
-
-        c = CHUNKS - 1
-        bank, at = y_place[c, 1]
-        nc.vector.scalar_tensor_tensor(
-            rows_of(c, 1), bank[:, at : at + W], -1.0, wgo_t[:, W * c : W * (c + 1)], ALU.mult, ALU.mult
-        )
-        scatter(c, 0)
-        nc.vector.tensor_copy(places_of(c, 1), rows_of(c, 1))
-        for first, n, chunks, weighed in ((c, 2, 1, y_neg[:, S - 3 * P : S - P]), (c, 3, 1, y_neg[:, S - P : S + P])):
-            bank, at = y_place[first, n]
-            rows = rows_of(first, n, chunks)
-            nc.scalar.activation(rows, bank[:, at : at + W * chunks], ACT.Copy, scale=-1.0)
-            nc.gpsimd.tensor_tensor(weighed, rows, wgo_t[:, W * first : W * (first + chunks)], ALU.mult)
-            nc.vector.tensor_copy(places_of(first, n, chunks), weighed)
-        turned = [turned_first[:], late[:, BANK - P // 2 : 5 * BANK - P // 2].rearrange("p (b j) -> p b j", b=4)[:, :, 0:P]]
-        rows = [late[:, BANK * e : BANK * (e + 1)] for e in range(5)]
+        quantise_h(last)
+        spent = slices[:].rearrange("p t j -> p (t j)").bitcast(F32)[:, 0:W]
+        y_out(last - 1, 3, rows=spent)
+        nc.vector.tensor_tensor(places_of(last - 1, 3), spent, wgo_of(last - 1), ALU.mult)
+        second_product([(last, 0)], y_bank(0))
+        second_product([(last, 1)], arg_bank([P, BANK]))
+        second_product([(last, 2)], arg_bank([P, BANK]))
+        second_product([(last, 3)], y_bank(1))
+        weigh_on_vector(last, 0)
+        scatter(last, 0)
+        for n in range(1, TILES):
+            y_out(last, n, rows=rest_odd[:, n])
+            nc.gpsimd.tensor_tensor(weighed_of(last, n), rest_odd[:, n], wgo_of(last), ALU.mult)
+            scatter(last, n)
+        turned = [turned_first[:], turned_second[:]]
         for half in range(2):
             turn_page(0, half, turned[half])
         for half in range(2):
             turn_back(0, half, turned[half])
-        results = [turned_first[:].rearrange("p b j -> p (b j)"), rows[0]]
         for half in range(2):
             cols = slice(BANK * half, BANK * (half + 1))
-            finish(nc.gpsimd, 1, cols, x0_rows[1][:, cols], results[half])
+            finish(nc.gpsimd, 1, cols, x0_rows[1][:, cols], turned[half].rearrange("p b j -> p (b j)"))
+        start = S + W
+        late = [x0_flat[:, start + BANK * e : start + BANK * (e + 1)] for e in range(4)]
         for e, (n, half) in enumerate([(2, 0), (2, 1), (3, 0), (3, 1)]):
-            finish(nc.vector, n, slice(BANK * half, BANK * (half + 1)), rows[1 + e], rows[1 + e])
+            finish(nc.vector, n, slice(BANK * half, BANK * (half + 1)), late[e], late[e])

@@ -30,8 +30,9 @@ UNITS = [(c, a) for c in range(CHUNKS) for a in range(H // PASS)]
 TWO_PI = 2.0 * math.pi
 
 SPREAD = 32
+BANK_PAIRS = (0, 1, 2, 1, 0, 2, 1, 0)
 UNIT = PACK * W
-ROUND_ON_VECTOR = 3
+GPSIMD_ENTRIES = 128
 
 
 def tile_list_morton_grain_corrections_kernel(
@@ -46,11 +47,8 @@ def tile_list_morton_grain_corrections_kernel(
         def held(name, shape, dtype):
             return keep.tile(shape, dtype, name=name, align_bytes=64)
 
-        taken = []
-
-        def arg_bank(shape):
-            taken.append(shape)
-            return psum.tile(shape, F32, name="arg_bank%d" % ((len(taken) - 1) % 6))
+        def arg_bank(pair_of_banks, e, shape):
+            return psum.tile(shape, F32, name="arg_bank%d" % (2 * pair_of_banks + e))
 
         def cast(on_vector, dst, src):
             if on_vector:
@@ -153,28 +151,26 @@ def tile_list_morton_grain_corrections_kernel(
             return [held("%s%d" % (name, e), shape, dtype) for e in range(count)]
 
         first_woven = held("first_woven", [P, 2 * UNIT], BF16)
-        chain = held("chain", [P, 3 * UNIT], BF16)
+        second_woven = held("second_woven", [P, 2 * UNIT], BF16)
+        first_turns = held("whole_even", [P, UNIT], I32)
         w1_woven = {
-            (0, 0): first_woven[:], (0, 1): chain[:, 0 : 2 * UNIT],
-            (1, 0): chain[:, 0 : 2 * UNIT], (1, 1): chain[:, UNIT : 3 * UNIT],
+            (0, 0): first_woven[:], (0, 1): second_woven[:], (1, 0): second_woven[:], (1, 1): first_turns[:, 0:UNIT].bitcast(BF16),
         }
-        first_rest = chain[:, UNIT : 3 * UNIT].bitcast(F32)
         st_first = held("st_first", [P, UNIT], BF16)
         turns_bufs = buffers("turns", 2, [P, PACK, W], F32)
         cosine_bufs = buffers("cosine", 2, [P, PACK, W], F32)
-        slices = held("h_slices", [P, PACK, W], BF16)
-        shared = held("shared", [P, 9 * W], F32)
-
-        def slots(lo, hi):
-            return shared[:, W * lo : W * hi]
-
-        woven = slots(1, 5).bitcast(BF16)
-        kept_rows = slots(3, 4)
-        whole_bufs = [held("whole_even", [P, UNIT], I32)[:], slots(4, 8).bitcast(I32)]
-        first_whole = held("first_whole", [P, UNIT], I32)[:]
+        shared = held("shared", [P, 3456], F32)
+        woven = shared[:, 448:1472].bitcast(BF16)
+        kept_rows = shared[:, 1024:1280]
+        wholes = {i: shared[:, 1280:2304].bitcast(I32) for i in (1, 3, 5, 7)}
+        wholes[0] = first_turns[:]
+        wholes[2] = shared[:, 2240:3264].bitcast(I32)
+        st_second = shared[:, 1728:2240].bitcast(BF16)
+        first_rest = shared[:, 2432:3456].rearrange("p (t j) -> p t j", t=PACK)
         rest_odd = held("rest_odd", [P, PACK, W], F32)
-        by_slot = shared[:].rearrange("p (s j) -> p s j", j=W)
-        rest_bufs = [[by_slot[:, 0:2], by_slot[:, 2:9:6]], [rest_odd[:, 0:2], rest_odd[:, 2:4]]]
+        rest_even = shared[:, 0:UNIT].rearrange("p (t j) -> p t j", t=PACK)
+        rest_bufs = [[rest_even[:, 0:2], rest_even[:, 2:4]], [rest_odd[:, 0:2], rest_odd[:, 2:4]]]
+        first_cosine = held("first_cosine", [P, PACK, W], F32)
         turned_first = held("turned_first", [P, 4, P], F32)
         turned_second = held("turned_second", [P, 4, P], F32)
 
@@ -210,7 +206,7 @@ def tile_list_morton_grain_corrections_kernel(
             )
 
         def quantise_stress(c):
-            st_c[c] = held("st_c%d" % c, [P, W], U32)
+            st_c[c] = held("whole_even" if c == 1 else "st_c%d" % c, [P, W], U32)
             st_s[c] = held("st_s%d" % c, [P, W], U8)
             nc.vector.quantize_mx(out=st_c[c][:].bitcast(FP8X4), scales=st_s[c][:], in_=st_place[c])
 
@@ -218,19 +214,22 @@ def tile_list_morton_grain_corrections_kernel(
         for g in range(2):
             nc.vector.tensor_copy(v_c[g][:], tab_w[g][:].indirect(offs_t[:]))
 
-        x0_flat = held("tab_w0", [P, (TILES + 1) * S], F32)
-        x0_rows = {n: x0_flat[:, S * e : S * (e + 1)] for n, e in enumerate((0, 1, 3, 4))}
+        x0_flat = held("tab_w0", [P, TILES * S + 2 * W], F32)
+        x0_rows = {n: x0_flat[:, S * n + W * e : S * (n + 1) + W * e] for n, e in enumerate((0, 1, 1, 2))}
         for n in range(TILES):
             nc.sync.dma_start(out=x0_rows[n], in_=x0[P * n : P * (n + 1), :])
-        y_flat = held("tab_w1", [P, 4 * S], F32)
+        y_all = held("tab_w1", [P, 4 * S], F32)
+        y_flat = y_all[:, BANK:]
+        first_kept = y_all[:, W // 2 : 3 * W // 2]
+        last_turns = y_all[:, 0:UNIT].rearrange("p (t j) -> p t j", t=PACK)
         page_neg = [held("page_neg%d" % n, [P, S], F32) for n in range(TILES)]
 
         def argument(i):
             c, a = UNITS[i]
             cols = slice(W * c, W * (c + 1))
             for pair in range(2):
-                bank = banks[i, pair] = arg_bank([P, 2, W])
-                passes = [0, 1, "stress"] if i in (2, 3, 4, 6) else ["stress", 0, 1]
+                bank = banks[i, pair] = arg_bank(BANK_PAIRS[i], pair, [P, 2, W])
+                passes = [0, 1, "stress"] if 2 <= i < 7 else ["stress", 0, 1]
                 for place, g in enumerate(passes):
                     for e in range(2):
                         t = 2 * pair + e
@@ -253,14 +252,25 @@ def tile_list_morton_grain_corrections_kernel(
                             out=bank[:, e, :], start=(place == 0 and e == 0), stop=(place == 2 and e == 1), **operands
                         )
 
+        def cosine_of(i):
+            return first_cosine if i == 1 else cosine_bufs[i % 2]
+
+        def turns_of(i):
+            return last_turns if i == 6 else turns_bufs[i % 2]
+
         def whole_of(i):
-            return first_whole if i == 1 else whole_bufs[i % 2]
+            if i not in wholes:
+                wholes[i] = held("whole_even", [P, UNIT], I32)[:]
+            return wholes[i]
+
+        def rest_of(i, pair):
+            return first_rest[:, 2 * pair : 2 * pair + 2] if i == 1 else rest_bufs[i % 2][pair]
 
         def turns_out(i):
             a = UNITS[i][1]
             for t in range(PACK):
                 nc.scalar.activation(
-                    turns_bufs[i % 2][:, t, :], banks[i, t // 2][:, t % 2, :], ACT.Identity,
+                    turns_of(i)[:, t, :], banks[i, t // 2][:, t % 2, :], ACT.Identity,
                     bias=phase_turns[:, a, t : t + 1], scale=1.0 / TWO_PI,
                 )
 
@@ -268,24 +278,24 @@ def tile_list_morton_grain_corrections_kernel(
             a = UNITS[i][1]
             for t in range(PACK):
                 nc.scalar.activation(
-                    turns_bufs[i % 2][:, t, :], banks[i, t // 2][:, t % 2, :], ACT.Abs,
+                    turns_of(i)[:, t, :], banks[i, t // 2][:, t % 2, :], ACT.Abs,
                     bias=phase_folded[:, a, t : t + 1], scale=1.0 / TWO_PI,
                 )
 
         def folded_round(i):
-            flat = turns_bufs[i % 2][:].rearrange("p t j -> p (t j)")
+            flat = turns_of(i)[:].rearrange("p t j -> p (t j)")
             nc.scalar.activation(whole_of(i).bitcast(U32), flat, ACT.Copy, bias=-0.25)
 
         def folded_rest_of(i):
-            return first_rest if i == 0 else turns_bufs[i % 2][:].rearrange("p t j -> p (t j)")
+            return shared[:, 0:UNIT]
 
         def folded_rest(i):
-            flat = turns_bufs[i % 2][:].rearrange("p t j -> p (t j)")
+            flat = turns_of(i)[:].rearrange("p t j -> p (t j)")
             nc.vector.tensor_tensor(folded_rest_of(i), flat, whole_of(i), ALU.subtract)
 
         def folded_sine(i):
             nc.scalar.activation(
-                cosine_bufs[i % 2][:].rearrange("p t j -> p (t j)").rearrange("p (j e t) -> p j t e", e=4, t=PACK),
+                cosine_of(i)[:].rearrange("p t j -> p (t j)").rearrange("p (j e t) -> p j t e", e=4, t=PACK),
                 folded_rest_of(i).rearrange("p (t j e) -> p j t e", t=PACK, e=4),
                 ACT.Sin, bias=math.pi / 2, scale=-TWO_PI,
             )
@@ -294,14 +304,14 @@ def tile_list_morton_grain_corrections_kernel(
             a = UNITS[i][1]
             engine.tensor_tensor(
                 woven_of(i).rearrange("p (u x) -> p u x", x=SPREAD * PACK),
-                cosine_bufs[i % 2][:].rearrange("p t j -> p (t j)").rearrange("p (u x) -> p u x", x=SPREAD * PACK),
+                cosine_of(i)[:].rearrange("p t j -> p (t j)").rearrange("p (u x) -> p u x", x=SPREAD * PACK),
                 gain_wide[:, a].rearrange("p j t -> p (j t)").unsqueeze(1).to_broadcast([P, W // SPREAD, SPREAD * PACK]),
                 ALU.mult,
             )
 
         def round_turns(i):
             nc.gpsimd.tensor_scalar(
-                whole_of(i), turns_bufs[i % 2][:].rearrange("p t j -> p (t j)"), 1.0, 0.0, ALU.mult, ALU.add
+                whole_of(i), turns_of(i)[:].rearrange("p t j -> p (t j)"), 1.0, 0.0, ALU.mult, ALU.add
             )
 
         def round_bank(i, pair):
@@ -315,7 +325,7 @@ def tile_list_morton_grain_corrections_kernel(
         def take_rest(i, pair):
             cols = slice(BANK * pair, BANK * (pair + 1))
             nc.vector.scalar_tensor_tensor(
-                rest_bufs[i % 2][pair], banks[i, pair][:], 1.0 / TWO_PI,
+                rest_of(i, pair), banks[i, pair][:], 1.0 / TWO_PI,
                 whole_of(i)[:, cols].rearrange("p (e j) -> p e j", e=2), ALU.mult, ALU.subtract,
             )
 
@@ -332,7 +342,7 @@ def tile_list_morton_grain_corrections_kernel(
             a = UNITS[i][1]
             for t in range(PACK):
                 nc.scalar.activation(
-                    cosine_bufs[i % 2][:, t, :], rest_bufs[i % 2][t // 2][:, t % 2, :], ACT.Sin,
+                    cosine_of(i)[:, t, :], rest_of(i, t // 2)[:, t % 2, :], ACT.Sin,
                     bias=phase_sine[:, a, t : t + 1], scale=TWO_PI,
                 )
 
@@ -344,31 +354,35 @@ def tile_list_morton_grain_corrections_kernel(
             a = UNITS[i][1]
             nc.vector.tensor_tensor(
                 woven_of(i).rearrange("p (j e t) -> p j t e", e=4, t=PACK),
-                cosine_bufs[i % 2][:].rearrange("p t (j e) -> p j t e", e=4),
+                cosine_of(i)[:].rearrange("p t (j e) -> p j t e", e=4),
                 gain_t[:, a].unsqueeze(1).unsqueeze(3).to_broadcast([P, W // 4, PACK, 4]),
                 ALU.mult,
             )
 
-        def gain_on_gpsimd(i):
+        def gain_on_gpsimd(i, entries):
             a = UNITS[i][1]
             nc.gpsimd.tensor_tensor(
-                woven_of(i).rearrange("p (j t) -> p j t", t=PACK),
-                cosine_bufs[i % 2][:].rearrange("p t j -> p j t"),
-                gain_t[:, a].unsqueeze(1).to_broadcast([P, W, PACK]),
+                woven_of(i).rearrange("p (j t) -> p j t", t=PACK)[:, :entries],
+                cosine_of(i)[:].rearrange("p t j -> p j t")[:, :entries],
+                gain_t[:, a].unsqueeze(1).to_broadcast([P, entries, PACK]),
                 ALU.mult,
             )
 
-        def gain_on_scalar(i):
+        def slices_of(i):
+            return turns_of(i)[:].bitcast(BF16)[:, :, 0:W]
+
+        def gain_on_scalar(i, first=0):
             a = UNITS[i][1]
+            slices = slices_of(i)
             for t in range(PACK):
                 nc.scalar.activation(
-                    slices[:, t, :], cosine_bufs[i % 2][:, t, :], ACT.Copy, scale=gain_t[:, a, t : t + 1]
+                    slices[:, t, first:], cosine_of(i)[:, t, first:], ACT.Copy, scale=gain_t[:, a, t : t + 1]
                 )
 
-        def weave_on_scalar(i):
+        def weave_on_scalar(i, first=0):
             nc.scalar.copy(
-                out=woven_of(i).rearrange("p (j e t) -> p j t e", e=4, t=PACK),
-                in_=slices[:].rearrange("p t (j e) -> p j t e", e=4),
+                out=woven_of(i).rearrange("p (j e t) -> p j t e", e=4, t=PACK)[:, first // 4 :],
+                in_=slices_of(i).rearrange("p t (j e) -> p j t e", e=4)[:, first // 4 :],
             )
 
         def second_product(parts, bank):
@@ -424,7 +438,8 @@ def tile_list_morton_grain_corrections_kernel(
             nc.scalar.activation(y_flat[:, W * n : W * (n + 2)], y_banks[c, n][:], ACT.Copy, scale=-1.0)
 
         def weigh_on_gpsimd(c, n, count=1):
-            rows = y_flat[:, W * n : W * (n + count)].rearrange("p (e j) -> p e j", e=count)
+            rows = first_kept if (c, n) == (0, 3) else y_flat[:, W * n : W * (n + count)]
+            rows = rows.rearrange("p (e j) -> p e j", e=count)
             first = S + W * (4 * (c % 2) + n)
             weighed = weighed_of(c, n) if count == 1 else y_flat[:, first : first + W * count]
             nc.gpsimd.tensor_tensor(
@@ -439,7 +454,7 @@ def tile_list_morton_grain_corrections_kernel(
             return [(b, slice(BANK * half + P * b, BANK * half + P * (b + 1))) for b in range(4)]
 
         def turn_x0(n, half):
-            x0_bank[n, half] = arg_bank([P, 4, P])
+            x0_bank[n, half] = arg_bank(2, half, [P, 4, P])
             for b, blk in blocks_of(half):
                 nc.tensor.matmul(
                     x0_bank[n, half][:, b, :], x0_rows[n][:, blk], ident[:],
@@ -479,46 +494,61 @@ def tile_list_morton_grain_corrections_kernel(
         round_w1(0, 1, 80)
         quantise_w1(0, 1, pieces=2)
         argument(0)
-        folded_turns_out(0)
-        round_w1(1, 0, 128)
+        round_w1(1, 0, 0)
+        reduce_on_vector(0)
         quantise_w1(1, 0)
-        folded_round(0)
         round_w1(1, 1, 128)
         quantise_w1(1, 1, pieces=2)
         argument(1)
-        folded_rest(0)
-        round_stress(1, False, chain[:, 0:UNIT])
+        sine(0)
+        round_stress(1, False, woven_of(0))
         quantise_stress(1)
-        folded_sine(0)
+        gain_on_gpsimd(0, W)
         reduce_on_vector(1)
         argument(2)
         argument(3)
         sine(1)
-        folded_gain(0, nc.vector)
+        round_stress(2, True, st_second)
         gain_on_vector(1)
+        quantise_stress(2)
         folded_turns_out(2)
         folded_round(2)
         turns_out(3)
+
+        round_stress(3, False, first_cosine[:].rearrange("p t j -> p (t j)")[:, 0:BANK].bitcast(BF16))
+
+        def next_even(i):
+            argument(i)
+            turns_out(i)
+            round_turns(i)
 
         last = CHUNKS - 1
         for c in range(last):
             even, odd = 2 * c + 2, 2 * c + 3
             quantise_h(c)
-            second_product([(c, 0), (c, 1)], y_bank(0))
-            second_product([(c, 2), (c, 3)], y_bank(1))
             if c == 0:
+                first_bank = y_bank(0)
+                second_product([(c, 0)], first_bank)
+                second_product([(c, 1), (c, 2)], y_bank(1))
                 folded_rest(even)
-                round_stress(2, True, shared[:, 5 * W // 2 : 9 * W // 2].bitcast(BF16))
-                quantise_stress(2)
                 round_turns(odd)
                 weigh_on_vector(c, 0)
                 scatter(c, 0)
-                y_out(c, 1)
-                folded_sine(even)
+                second_product([(c, 3)], first_bank)
+                pair_out(c, 1)
                 weigh_on_gpsimd(c, 1)
+                weigh_on_gpsimd(c, 2)
+                next_even(even + 2)
+                folded_sine(even)
+                folded_gain(even, nc.gpsimd)
                 rests(odd)
+                y_out(c, 3, rows=first_kept)
                 scatter(c, 1)
+                scatter(c, 2)
+                quantise_stress(3)
             else:
+                second_product([(c, 0), (c, 1)], y_bank(0))
+                second_product([(c, 2), (c, 3)], y_bank(1))
                 rests(even)
                 weigh_on_gpsimd(c - 1, 3)
                 scatter(c - 1, 3)
@@ -529,26 +559,18 @@ def tile_list_morton_grain_corrections_kernel(
                 rests(odd)
                 scatter(c, 0)
                 scatter(c, 1)
-            if c < last - 1:
-                pair_out(c, 2)
-            else:
-                y_out(c, 2)
-            weigh_on_gpsimd(c, 2)
-            scatter(c, 2)
-            if c == 0:
-                round_stress(3, False, first_whole.bitcast(BF16)[:, 0:UNIT])
-                quantise_stress(3)
-            if c < last - 1:
-                argument(even + 2)
-                turns_out(even + 2)
-                round_turns(even + 2)
-            else:
-                for half in range(2):
-                    turn_x0(0, half)
-            if c == 0:
-                folded_gain(even, nc.gpsimd)
-            else:
-                gain_on_gpsimd(even)
+                if c < last - 1:
+                    pair_out(c, 2)
+                    weigh_on_gpsimd(c, 2)
+                    gain_on_gpsimd(even, GPSIMD_ENTRIES)
+                    scatter(c, 2)
+                    gain_on_scalar(even, GPSIMD_ENTRIES)
+                    weave_on_scalar(even, GPSIMD_ENTRIES)
+                    next_even(even + 2)
+                else:
+                    gain_on_gpsimd(even, W)
+                    for half in range(2):
+                        turn_x0(1, half)
             sine(odd)
             gain_on_scalar(odd)
             weave_on_scalar(odd)
@@ -557,28 +579,38 @@ def tile_list_morton_grain_corrections_kernel(
                 turns_out(odd + 2)
 
         quantise_h(last)
-        spent = slices[:].rearrange("p t j -> p (t j)").bitcast(F32)[:, 0:W]
-        y_out(last - 1, 3, rows=spent)
-        nc.vector.tensor_tensor(places_of(last - 1, 3), spent, wgo_of(last - 1), ALU.mult)
+        spent = turns_bufs[1][:].rearrange("p t j -> p (t j)")[:, 0:BANK]
+        nc.scalar.activation(spent, y_banks[last - 1, 2][:], ACT.Copy, scale=-1.0)
+        nc.vector.tensor_tensor(places_of(last - 1, 2), spent[:, 0:W], wgo_of(last - 1), ALU.mult)
         second_product([(last, 0)], y_bank(0))
-        second_product([(last, 1)], arg_bank([P, BANK]))
-        second_product([(last, 2)], arg_bank([P, BANK]))
+        second_product([(last, 1)], arg_bank(1, 0, [P, BANK]))
+        second_product([(last, 2)], arg_bank(1, 1, [P, BANK]))
         second_product([(last, 3)], y_bank(1))
         weigh_on_vector(last, 0)
         scatter(last, 0)
+        nc.gpsimd.tensor_tensor(spent[:, 0:W], spent[:, W:BANK], wgo_of(last - 1), ALU.mult)
+        last_rows = {1: shared[:, 0:W], 2: shared[:, W:BANK], 3: shared[:, 3 * W : UNIT]}
         for n in range(1, TILES):
-            y_out(last, n, rows=rest_odd[:, n])
-            nc.gpsimd.tensor_tensor(weighed_of(last, n), rest_odd[:, n], wgo_of(last), ALU.mult)
-            scatter(last, n)
+            y_out(last, n, rows=last_rows[n])
+            weighed = weighed_of(last, n) if n < TILES - 1 else spent[:, W:BANK]
+            nc.gpsimd.tensor_tensor(weighed, last_rows[n], wgo_of(last), ALU.mult)
+            if n < TILES - 1:
+                scatter(last, n)
+        nc.vector.tensor_copy(page_neg[TILES - 1][:].indirect(offs2_t[:, W * (last - 1) // LIST :]), spent)
+        halves = [slice(0, BANK), slice(BANK, S)]
+        start = 3 * W // 2
+        diffs = [shared[:, start + BANK * e : start + BANK * (e + 1)] for e in range(2)]
+        diffs = diffs + [x0_flat[:, W + BANK * e : W + BANK * (e + 1)] for e in range(2)]
+        for half in range(2):
+            finish(nc.gpsimd, 0, halves[half], diffs[half], diffs[half])
         turned = [turned_first[:], turned_second[:]]
         for half in range(2):
-            turn_page(0, half, turned[half])
+            turn_page(1, half, turned[half])
         for half in range(2):
-            turn_back(0, half, turned[half])
+            turn_back(1, half, turned[half])
         for half in range(2):
-            cols = slice(BANK * half, BANK * (half + 1))
-            finish(nc.gpsimd, 1, cols, x0_rows[1][:, cols], turned[half].rearrange("p b j -> p (b j)"))
-        start = S + W
-        late = [x0_flat[:, start + BANK * e : start + BANK * (e + 1)] for e in range(4)]
-        for e, (n, half) in enumerate([(2, 0), (2, 1), (3, 0), (3, 1)]):
-            finish(nc.vector, n, slice(BANK * half, BANK * (half + 1)), late[e], late[e])
+            finish(nc.gpsimd, 2, halves[half], diffs[2 + half], diffs[2 + half])
+        start = 2 * S + 2 * W
+        for half in range(2):
+            late = x0_flat[:, start + BANK * half : start + BANK * (half + 1)]
+            finish(nc.vector, 3, halves[half], late, late)

@@ -32,6 +32,7 @@ TWO_PI = 2.0 * math.pi
 SPREAD = 32
 BANK_PAIRS = (0, 1, 2, 1, 0, 2, 1, 0)
 UNIT = PACK * W
+LATER_ENTRIES = 192
 GPSIMD_ENTRIES = 128
 
 
@@ -316,11 +317,11 @@ def tile_list_morton_grain_corrections_kernel(
 
         def round_bank(i, pair):
             a = UNITS[i][1]
-            for t in (2 * pair, 2 * pair + 1):
-                nc.vector.tensor_scalar(
-                    whole_of(i)[:, W * t : W * (t + 1)], banks[i, pair][:, t % 2, :], 1.0 / TWO_PI,
-                    phase_turns[:, a, t : t + 1], ALU.mult, ALU.add,
-                )
+            nc.vector.scalar_tensor_tensor(
+                whole_of(i)[:, BANK * pair : BANK * (pair + 1)].rearrange("p (e j) -> p e j", e=2),
+                banks[i, pair][:], 1.0 / TWO_PI,
+                phase_turns[:, a, 2 * pair : 2 * pair + 2].unsqueeze(2).to_broadcast([P, 2, W]), ALU.mult, ALU.add,
+            )
 
         def take_rest(i, pair):
             cols = slice(BANK * pair, BANK * (pair + 1))
@@ -410,7 +411,7 @@ def tile_list_morton_grain_corrections_kernel(
             h_s[c] = held("h_s%d" % c, [P, 2 * W], U8)
             nc.vector.quantize_mx(out=h_c[c][:].bitcast(FP8X4), scales=h_s[c][:], in_=woven)
 
-        ahead_of_codes = held("st_c3", [P, W], F32)
+        ahead_of_codes = held("st_c3", [P, 2 * W], F32)
 
         def wgo_of(c):
             return wgo_t[:, W * c : W * (c + 1)]
@@ -424,8 +425,8 @@ def tile_list_morton_grain_corrections_kernel(
         def weighed_of(c, n):
             if n == TILES - 1 and c < CHUNKS - 1:
                 return kept_rows if c < CHUNKS - 2 else None
-            if (c, n) == (0, 2):
-                return ahead_of_codes[:]
+            if c == 0 and n > 0:
+                return ahead_of_codes[:, W * (n - 1) : W * n]
             return y_flat[:, S + W * (4 * (c % 2) + n) : S + W * (4 * (c % 2) + n + 1)]
 
         def weigh_on_vector(c, n):
@@ -442,6 +443,8 @@ def tile_list_morton_grain_corrections_kernel(
             rows = rows.rearrange("p (e j) -> p e j", e=count)
             first = S + W * (4 * (c % 2) + n)
             weighed = weighed_of(c, n) if count == 1 else y_flat[:, first : first + W * count]
+            if c == 0 and count == 2:
+                weighed = ahead_of_codes[:]
             nc.gpsimd.tensor_tensor(
                 weighed.rearrange("p (e j) -> p e j", e=count), rows,
                 wgo_of(c).unsqueeze(1).to_broadcast([P, count, W]), ALU.mult,
@@ -503,7 +506,9 @@ def tile_list_morton_grain_corrections_kernel(
         sine(0)
         round_stress(1, False, woven_of(0))
         quantise_stress(1)
-        gain_on_gpsimd(0, W)
+        gain_on_gpsimd(0, GPSIMD_ENTRIES)
+        gain_on_scalar(0, GPSIMD_ENTRIES)
+        weave_on_scalar(0, GPSIMD_ENTRIES)
         reduce_on_vector(1)
         argument(2)
         argument(3)
@@ -536,8 +541,7 @@ def tile_list_morton_grain_corrections_kernel(
                 scatter(c, 0)
                 second_product([(c, 3)], first_bank)
                 pair_out(c, 1)
-                weigh_on_gpsimd(c, 1)
-                weigh_on_gpsimd(c, 2)
+                weigh_on_gpsimd(c, 1, 2)
                 next_even(even + 2)
                 folded_sine(even)
                 folded_gain(even, nc.gpsimd)
@@ -562,10 +566,10 @@ def tile_list_morton_grain_corrections_kernel(
                 if c < last - 1:
                     pair_out(c, 2)
                     weigh_on_gpsimd(c, 2)
-                    gain_on_gpsimd(even, GPSIMD_ENTRIES)
+                    gain_on_gpsimd(even, LATER_ENTRIES)
                     scatter(c, 2)
-                    gain_on_scalar(even, GPSIMD_ENTRIES)
-                    weave_on_scalar(even, GPSIMD_ENTRIES)
+                    gain_on_scalar(even, LATER_ENTRIES)
+                    weave_on_scalar(even, LATER_ENTRIES)
                     next_even(even + 2)
                 else:
                     gain_on_gpsimd(even, W)
@@ -579,7 +583,8 @@ def tile_list_morton_grain_corrections_kernel(
                 turns_out(odd + 2)
 
         quantise_h(last)
-        spent = turns_bufs[1][:].rearrange("p t j -> p (t j)")[:, 0:BANK]
+        spent_turns = turns_bufs[1][:].rearrange("p t j -> p (t j)")
+        spent = spent_turns[:, 0:BANK]
         nc.scalar.activation(spent, y_banks[last - 1, 2][:], ACT.Copy, scale=-1.0)
         nc.vector.tensor_tensor(places_of(last - 1, 2), spent[:, 0:W], wgo_of(last - 1), ALU.mult)
         second_product([(last, 0)], y_bank(0))
@@ -589,17 +594,20 @@ def tile_list_morton_grain_corrections_kernel(
         weigh_on_vector(last, 0)
         scatter(last, 0)
         nc.gpsimd.tensor_tensor(spent[:, 0:W], spent[:, W:BANK], wgo_of(last - 1), ALU.mult)
-        last_rows = {1: shared[:, 0:W], 2: shared[:, W:BANK], 3: shared[:, 3 * W : UNIT]}
-        for n in range(1, TILES):
-            y_out(last, n, rows=last_rows[n])
-            weighed = weighed_of(last, n) if n < TILES - 1 else spent[:, W:BANK]
-            nc.gpsimd.tensor_tensor(weighed, last_rows[n], wgo_of(last), ALU.mult)
-            if n < TILES - 1:
-                scatter(last, n)
+        y_out(last, 1, rows=shared[:, 0:W])
+        nc.gpsimd.tensor_tensor(weighed_of(last, 1), shared[:, 0:W], wgo_of(last), ALU.mult)
+        scatter(last, 1)
+        y_out(last, 2, rows=shared[:, 2 * W : 3 * W])
+        y_out(last, 3, rows=shared[:, W : 2 * W])
+        nc.gpsimd.tensor_tensor(
+            spent_turns[:, W : 3 * W].rearrange("p (e j) -> p e j", e=2),
+            shared[:, W : 3 * W].rearrange("p (e j) -> p e j", e=2),
+            wgo_of(last).unsqueeze(1).to_broadcast([P, 2, W]), ALU.mult,
+        )
+        nc.vector.tensor_copy(places_of(last, 2), spent_turns[:, 2 * W : 3 * W])
         nc.vector.tensor_copy(page_neg[TILES - 1][:].indirect(offs2_t[:, W * (last - 1) // LIST :]), spent)
         halves = [slice(0, BANK), slice(BANK, S)]
-        start = 3 * W // 2
-        diffs = [shared[:, start + BANK * e : start + BANK * (e + 1)] for e in range(2)]
+        diffs = [shared[:, P + BANK * e : P + BANK * (e + 1)] for e in range(2)]
         diffs = diffs + [x0_flat[:, W + BANK * e : W + BANK * (e + 1)] for e in range(2)]
         for half in range(2):
             finish(nc.gpsimd, 0, halves[half], diffs[half], diffs[half])

@@ -30,10 +30,10 @@ UNITS = [(c, a) for c in range(CHUNKS) for a in range(H // PASS)]
 TWO_PI = 2.0 * math.pi
 
 SPREAD = 32
-BANK_PAIRS = (0, 1, 2, 1, 0, 2, 1, 0)
+BANK_PAIRS = (0, 1, 2, 1, 0, 1, 2, 0)
 UNIT = PACK * W
 LATER_ENTRIES = 192
-GPSIMD_ENTRIES = 128
+GPSIMD_ENTRIES = 176
 
 
 def tile_list_morton_grain_corrections_kernel(
@@ -126,6 +126,8 @@ def tile_list_morton_grain_corrections_kernel(
         load_w1(1, 0)
         load_w1(1, 1)
         load_stress(1)
+        load_stress(2)
+        load_stress(3)
         nc.sync.dma_start(out=w3_c[:].bitcast(I32), in_=w3_words.rearrange("a p n i -> p a (n i)").bitcast(I32))
         for quad in range(4):
             nc.sync.dma_start(
@@ -133,9 +135,7 @@ def tile_list_morton_grain_corrections_kernel(
                 in_=w3_scales[:, 4 * quad : 4 * quad + 4, :].bitcast(I32),
             )
         nc.sync.dma_start(offs2_t[:], offs2)
-        load_stress(2)
         nc.sync.dma_start(out=wgo_t[:], in_=wgo)
-        load_stress(3)
 
         make_identity(nc, ident[:])
 
@@ -153,25 +153,31 @@ def tile_list_morton_grain_corrections_kernel(
 
         first_woven = held("first_woven", [P, 2 * UNIT], BF16)
         second_woven = held("second_woven", [P, 2 * UNIT], BF16)
-        first_turns = held("whole_even", [P, UNIT], I32)
+        first_turns = held("whole_even", [P, UNIT + BANK], I32)
         w1_woven = {
             (0, 0): first_woven[:], (0, 1): second_woven[:], (1, 0): second_woven[:], (1, 1): first_turns[:, 0:UNIT].bitcast(BF16),
         }
         st_first = held("st_first", [P, UNIT], BF16)
-        turns_bufs = buffers("turns", 2, [P, PACK, W], F32)
+        even_slices = held("even_slices", [P, PACK, W], BF16)
+        odd_room = held("odd_room", [P, 2 * UNIT], F32)
+        turns_odd = odd_room[:, BANK : BANK + UNIT].rearrange("p (t j) -> p t j", t=PACK)
+        odd_slices = odd_room[:].bitcast(BF16)[:, 896:3584].rearrange("p (t x) -> p t x", t=PACK)[:, :, 0:W]
         cosine_bufs = buffers("cosine", 2, [P, PACK, W], F32)
-        shared = held("shared", [P, 3456], F32)
-        woven = shared[:, 448:1472].bitcast(BF16)
-        kept_rows = shared[:, 1024:1280]
-        wholes = {i: shared[:, 1280:2304].bitcast(I32) for i in (1, 3, 5, 7)}
-        wholes[0] = first_turns[:]
-        wholes[2] = shared[:, 2240:3264].bitcast(I32)
-        st_second = shared[:, 1728:2240].bitcast(BF16)
-        first_rest = shared[:, 2432:3456].rearrange("p (t j) -> p t j", t=PACK)
+        shared = held("shared", [P, 5248], F32)
+        woven = shared[:, 0:UNIT].bitcast(BF16)
+        kept_rows = shared[:, 576:832]
+        wholes = {i: shared[:, 832:1856].bitcast(I32) for i in (3, 5, 7)}
+        wholes[0] = first_turns[:, BANK:]
+        wholes[2] = first_woven[:].bitcast(I32)
+        fourth_turns = first_woven[:].bitcast(F32).rearrange("p (t j) -> p t j", t=PACK)
+        folded_turns = shared[:, 1792:2816].rearrange("p (t j) -> p t j", t=PACK)
+        second_wholes = [shared[:, 3264:3776].bitcast(I32), shared[:, 2752:3264].bitcast(I32)]
+        st_third = shared[:, 3712:4224].bitcast(BF16)
+        st_second = shared[:, 4224:4736].bitcast(BF16)
+        first_rest = held("st_c2", [P, PACK, W], F32)
         rest_odd = held("rest_odd", [P, PACK, W], F32)
-        rest_even = shared[:, 0:UNIT].rearrange("p (t j) -> p t j", t=PACK)
-        rest_bufs = [[rest_even[:, 0:2], rest_even[:, 2:4]], [rest_odd[:, 0:2], rest_odd[:, 2:4]]]
-        first_cosine = held("first_cosine", [P, PACK, W], F32)
+        rest_even = [odd_room[:, lo : lo + BANK].rearrange("p (e j) -> p e j", e=2) for lo in (0, BANK + UNIT)]
+        rest_bufs = [rest_even, [rest_odd[:, 0:2], rest_odd[:, 2:4]]]
         turned_first = held("turned_first", [P, 4, P], F32)
         turned_second = held("turned_second", [P, 4, P], F32)
 
@@ -207,7 +213,7 @@ def tile_list_morton_grain_corrections_kernel(
             )
 
         def quantise_stress(c):
-            st_c[c] = held("whole_even" if c == 1 else "st_c%d" % c, [P, W], U32)
+            st_c[c] = held("st_c%d" % c, [P, W], U32)
             st_s[c] = held("st_s%d" % c, [P, W], U8)
             nc.vector.quantize_mx(out=st_c[c][:].bitcast(FP8X4), scales=st_s[c][:], in_=st_place[c])
 
@@ -254,15 +260,19 @@ def tile_list_morton_grain_corrections_kernel(
                         )
 
         def cosine_of(i):
-            return first_cosine if i == 1 else cosine_bufs[i % 2]
+            return cosine_bufs[i % 2]
 
         def turns_of(i):
-            return last_turns if i == 6 else turns_bufs[i % 2]
+            return {2: folded_turns, 4: fourth_turns, 6: last_turns}.get(i, turns_odd)
 
         def whole_of(i):
             if i not in wholes:
                 wholes[i] = held("whole_even", [P, UNIT], I32)[:]
             return wholes[i]
+
+        def whole_bank(i, pair):
+            bank = second_wholes[pair] if i == 1 else whole_of(i)[:, BANK * pair : BANK * (pair + 1)]
+            return bank.rearrange("p (e j) -> p e j", e=2)
 
         def rest_of(i, pair):
             return first_rest[:, 2 * pair : 2 * pair + 2] if i == 1 else rest_bufs[i % 2][pair]
@@ -284,14 +294,14 @@ def tile_list_morton_grain_corrections_kernel(
                 )
 
         def folded_round(i):
-            flat = turns_of(i)[:].rearrange("p t j -> p (t j)")
+            flat = turns_of(i).rearrange("p t j -> p (t j)")
             nc.scalar.activation(whole_of(i).bitcast(U32), flat, ACT.Copy, bias=-0.25)
 
         def folded_rest_of(i):
-            return shared[:, 0:UNIT]
+            return shared[:, 4224:5248]
 
         def folded_rest(i):
-            flat = turns_of(i)[:].rearrange("p t j -> p (t j)")
+            flat = turns_of(i).rearrange("p t j -> p (t j)")
             nc.vector.tensor_tensor(folded_rest_of(i), flat, whole_of(i), ALU.subtract)
 
         def folded_sine(i):
@@ -312,22 +322,19 @@ def tile_list_morton_grain_corrections_kernel(
 
         def round_turns(i):
             nc.gpsimd.tensor_scalar(
-                whole_of(i), turns_of(i)[:].rearrange("p t j -> p (t j)"), 1.0, 0.0, ALU.mult, ALU.add
+                whole_of(i), turns_of(i).rearrange("p t j -> p (t j)"), 1.0, 0.0, ALU.mult, ALU.add
             )
 
         def round_bank(i, pair):
             a = UNITS[i][1]
             nc.vector.scalar_tensor_tensor(
-                whole_of(i)[:, BANK * pair : BANK * (pair + 1)].rearrange("p (e j) -> p e j", e=2),
-                banks[i, pair][:], 1.0 / TWO_PI,
+                whole_bank(i, pair), banks[i, pair][:], 1.0 / TWO_PI,
                 phase_turns[:, a, 2 * pair : 2 * pair + 2].unsqueeze(2).to_broadcast([P, 2, W]), ALU.mult, ALU.add,
             )
 
         def take_rest(i, pair):
-            cols = slice(BANK * pair, BANK * (pair + 1))
             nc.vector.scalar_tensor_tensor(
-                rest_of(i, pair), banks[i, pair][:], 1.0 / TWO_PI,
-                whole_of(i)[:, cols].rearrange("p (e j) -> p e j", e=2), ALU.mult, ALU.subtract,
+                rest_of(i, pair), banks[i, pair][:], 1.0 / TWO_PI, whole_bank(i, pair), ALU.mult, ALU.subtract,
             )
 
         def reduce_on_vector(i):
@@ -370,7 +377,7 @@ def tile_list_morton_grain_corrections_kernel(
             )
 
         def slices_of(i):
-            return turns_of(i)[:].bitcast(BF16)[:, :, 0:W]
+            return odd_slices if i % 2 else even_slices[:]
 
         def gain_on_scalar(i, first=0):
             a = UNITS[i][1]
@@ -406,12 +413,16 @@ def tile_list_morton_grain_corrections_kernel(
         def y_bank(e):
             return psum.tile([P, BANK], F32, name="y_bank%d" % e)
 
-        def quantise_h(c):
+        def quantise_h(c, pieces=1):
             h_c[c] = held("h_c%d" % c, [P, 2 * W], U32)
             h_s[c] = held("h_s%d" % c, [P, 2 * W], U8)
-            nc.vector.quantize_mx(out=h_c[c][:].bitcast(FP8X4), scales=h_s[c][:], in_=woven)
+            for lo in range(0, 2 * W, 2 * W // pieces):
+                hi = lo + 2 * W // pieces
+                nc.vector.quantize_mx(
+                    out=h_c[c][:, lo:hi].bitcast(FP8X4), scales=h_s[c][:, lo:hi], in_=woven[:, PACK * lo : PACK * hi]
+                )
 
-        ahead_of_codes = held("st_c3", [P, 2 * W], F32)
+        ahead_of_codes = held("st_c3", [P, W], F32)
 
         def wgo_of(c):
             return wgo_t[:, W * c : W * (c + 1)]
@@ -425,8 +436,10 @@ def tile_list_morton_grain_corrections_kernel(
         def weighed_of(c, n):
             if n == TILES - 1 and c < CHUNKS - 1:
                 return kept_rows if c < CHUNKS - 2 else None
-            if c == 0 and n > 0:
-                return ahead_of_codes[:, W * (n - 1) : W * n]
+            if (c, n) == (0, 1):
+                return shared[:, UNIT : UNIT + W]
+            if (c, n) == (0, 2):
+                return ahead_of_codes[:]
             return y_flat[:, S + W * (4 * (c % 2) + n) : S + W * (4 * (c % 2) + n + 1)]
 
         def weigh_on_vector(c, n):
@@ -443,8 +456,6 @@ def tile_list_morton_grain_corrections_kernel(
             rows = rows.rearrange("p (e j) -> p e j", e=count)
             first = S + W * (4 * (c % 2) + n)
             weighed = weighed_of(c, n) if count == 1 else y_flat[:, first : first + W * count]
-            if c == 0 and count == 2:
-                weighed = ahead_of_codes[:]
             nc.gpsimd.tensor_tensor(
                 weighed.rearrange("p (e j) -> p e j", e=count), rows,
                 wgo_of(c).unsqueeze(1).to_broadcast([P, count, W]), ALU.mult,
@@ -457,7 +468,7 @@ def tile_list_morton_grain_corrections_kernel(
             return [(b, slice(BANK * half + P * b, BANK * half + P * (b + 1))) for b in range(4)]
 
         def turn_x0(n, half):
-            x0_bank[n, half] = arg_bank(2, half, [P, 4, P])
+            x0_bank[n, half] = arg_bank(1, half, [P, 4, P])
             for b, blk in blocks_of(half):
                 nc.tensor.matmul(
                     x0_bank[n, half][:, b, :], x0_rows[n][:, blk], ident[:],
@@ -499,13 +510,14 @@ def tile_list_morton_grain_corrections_kernel(
         argument(0)
         round_w1(1, 0, 0)
         reduce_on_vector(0)
-        quantise_w1(1, 0)
         round_w1(1, 1, 128)
+        quantise_w1(1, 0)
         quantise_w1(1, 1, pieces=2)
         argument(1)
         sine(0)
         round_stress(1, False, woven_of(0))
         quantise_stress(1)
+        round_stress(2, False, st_second)
         gain_on_gpsimd(0, GPSIMD_ENTRIES)
         gain_on_scalar(0, GPSIMD_ENTRIES)
         weave_on_scalar(0, GPSIMD_ENTRIES)
@@ -513,14 +525,12 @@ def tile_list_morton_grain_corrections_kernel(
         argument(2)
         argument(3)
         sine(1)
-        round_stress(2, True, st_second)
+        round_stress(3, True, st_third)
         gain_on_vector(1)
         quantise_stress(2)
         folded_turns_out(2)
         folded_round(2)
         turns_out(3)
-
-        round_stress(3, False, first_cosine[:].rearrange("p t j -> p (t j)")[:, 0:BANK].bitcast(BF16))
 
         def next_even(i):
             argument(i)
@@ -540,13 +550,14 @@ def tile_list_morton_grain_corrections_kernel(
                 weigh_on_vector(c, 0)
                 scatter(c, 0)
                 second_product([(c, 3)], first_bank)
-                pair_out(c, 1)
-                weigh_on_gpsimd(c, 1, 2)
+                y_out(c, 2)
+                weigh_on_gpsimd(c, 2)
                 next_even(even + 2)
                 folded_sine(even)
                 folded_gain(even, nc.gpsimd)
                 rests(odd)
                 y_out(c, 3, rows=first_kept)
+                weigh_on_vector(c, 1)
                 scatter(c, 1)
                 scatter(c, 2)
                 quantise_stress(3)
@@ -582,14 +593,15 @@ def tile_list_morton_grain_corrections_kernel(
                 argument(odd + 2)
                 turns_out(odd + 2)
 
-        quantise_h(last)
-        spent_turns = turns_bufs[1][:].rearrange("p t j -> p (t j)")
+        quantise_h(last, pieces=2)
+        spent_turns = odd_room[:, BANK : BANK + UNIT]
         spent = spent_turns[:, 0:BANK]
-        nc.scalar.activation(spent, y_banks[last - 1, 2][:], ACT.Copy, scale=-1.0)
+        y_out(last - 1, 2, rows=spent[:, 0:W])
+        y_out(last - 1, 3, rows=spent[:, W:BANK])
         nc.vector.tensor_tensor(places_of(last - 1, 2), spent[:, 0:W], wgo_of(last - 1), ALU.mult)
         second_product([(last, 0)], y_bank(0))
-        second_product([(last, 1)], arg_bank(1, 0, [P, BANK]))
-        second_product([(last, 2)], arg_bank(1, 1, [P, BANK]))
+        second_product([(last, 1)], arg_bank(2, 0, [P, BANK]))
+        second_product([(last, 2)], arg_bank(2, 1, [P, BANK]))
         second_product([(last, 3)], y_bank(1))
         weigh_on_vector(last, 0)
         scatter(last, 0)

@@ -169,7 +169,9 @@ def tile_list_morton_grain_corrections_kernel(
         wholes = {i: shared[:, 832:1856].bitcast(I32) for i in (3, 5, 7)}
         wholes[0] = first_turns[:, BANK:]
         wholes[2] = first_woven[:].bitcast(I32)
-        fourth_turns = first_woven[:].bitcast(F32).rearrange("p (t j) -> p t j", t=PACK)
+        fourth_whole = held("fourth_whole", [P, UNIT], F32)
+        wholes[6] = wholes[4] = fourth_whole[:].bitcast(I32)
+        fourth_turns = second_woven[:].bitcast(F32).rearrange("p (t j) -> p t j", t=PACK)
         folded_turns = shared[:, 1792:2816].rearrange("p (t j) -> p t j", t=PACK)
         second_wholes = [shared[:, 3264:3776].bitcast(I32), shared[:, 2752:3264].bitcast(I32)]
         st_third = shared[:, 3712:4224].bitcast(BF16)
@@ -266,8 +268,6 @@ def tile_list_morton_grain_corrections_kernel(
             return {2: folded_turns, 4: fourth_turns, 6: last_turns}.get(i, turns_odd)
 
         def whole_of(i):
-            if i not in wholes:
-                wholes[i] = held("whole_even", [P, UNIT], I32)[:]
             return wholes[i]
 
         def whole_bank(i, pair):
@@ -422,8 +422,6 @@ def tile_list_morton_grain_corrections_kernel(
                     out=h_c[c][:, lo:hi].bitcast(FP8X4), scales=h_s[c][:, lo:hi], in_=woven[:, PACK * lo : PACK * hi]
                 )
 
-        ahead_of_codes = held("st_c3", [P, W], F32)
-
         def wgo_of(c):
             return wgo_t[:, W * c : W * (c + 1)]
 
@@ -438,8 +436,6 @@ def tile_list_morton_grain_corrections_kernel(
                 return kept_rows if c < CHUNKS - 2 else None
             if (c, n) == (0, 1):
                 return shared[:, UNIT : UNIT + W]
-            if (c, n) == (0, 2):
-                return ahead_of_codes[:]
             return y_flat[:, S + W * (4 * (c % 2) + n) : S + W * (4 * (c % 2) + n + 1)]
 
         def weigh_on_vector(c, n):
@@ -526,6 +522,7 @@ def tile_list_morton_grain_corrections_kernel(
         argument(3)
         sine(1)
         round_stress(3, True, st_third)
+        quantise_stress(3)
         gain_on_vector(1)
         quantise_stress(2)
         folded_turns_out(2)
@@ -550,8 +547,8 @@ def tile_list_morton_grain_corrections_kernel(
                 weigh_on_vector(c, 0)
                 scatter(c, 0)
                 second_product([(c, 3)], first_bank)
-                y_out(c, 2)
-                weigh_on_gpsimd(c, 2)
+                y_out(c, 2, rows=fourth_whole[:, 0:W])
+                nc.gpsimd.tensor_tensor(weighed_of(c, 2), fourth_whole[:, 0:W], wgo_of(c), ALU.mult)
                 next_even(even + 2)
                 folded_sine(even)
                 folded_gain(even, nc.gpsimd)
@@ -560,15 +557,14 @@ def tile_list_morton_grain_corrections_kernel(
                 weigh_on_vector(c, 1)
                 scatter(c, 1)
                 scatter(c, 2)
-                quantise_stress(3)
             else:
                 second_product([(c, 0), (c, 1)], y_bank(0))
-                second_product([(c, 2), (c, 3)], y_bank(1))
                 rests(even)
                 weigh_on_gpsimd(c - 1, 3)
                 scatter(c - 1, 3)
                 round_turns(odd)
                 pair_out(c, 0)
+                second_product([(c, 2), (c, 3)], y_bank(0))
                 sine(even)
                 weigh_on_gpsimd(c, 0, 2)
                 rests(odd)
@@ -599,10 +595,10 @@ def tile_list_morton_grain_corrections_kernel(
         y_out(last - 1, 2, rows=spent[:, 0:W])
         y_out(last - 1, 3, rows=spent[:, W:BANK])
         nc.vector.tensor_tensor(places_of(last - 1, 2), spent[:, 0:W], wgo_of(last - 1), ALU.mult)
-        second_product([(last, 0)], y_bank(0))
+        second_product([(last, 0)], y_bank(1))
         second_product([(last, 1)], arg_bank(2, 0, [P, BANK]))
         second_product([(last, 2)], arg_bank(2, 1, [P, BANK]))
-        second_product([(last, 3)], y_bank(1))
+        second_product([(last, 3)], y_bank(0))
         weigh_on_vector(last, 0)
         scatter(last, 0)
         nc.gpsimd.tensor_tensor(spent[:, 0:W], spent[:, W:BANK], wgo_of(last - 1), ALU.mult)

@@ -29,11 +29,10 @@ TILES = N // P
 UNITS = [(c, a) for c in range(CHUNKS) for a in range(H // PASS)]
 TWO_PI = 2.0 * math.pi
 
+UNIT = PACK * W
 SPREAD = 32
 BANK_PAIRS = (0, 1, 2, 1, 0, 1, 2, 0)
-UNIT = PACK * W
-LATER_ENTRIES = 192
-GPSIMD_ENTRIES = 176
+GPSIMD_ENTRIES = {0: 176, 4: 192, 6: W}
 
 
 def tile_list_morton_grain_corrections_kernel(
@@ -148,43 +147,46 @@ def tile_list_morton_grain_corrections_kernel(
             in_=w2s_raw[:].rearrange("p (a m t) -> p a t m", a=2, t=PACK),
         )
 
-        def buffers(name, count, shape, dtype):
-            return [held("%s%d" % (name, e), shape, dtype) for e in range(count)]
-
         first_woven = held("first_woven", [P, 2 * UNIT], BF16)
         second_woven = held("second_woven", [P, 2 * UNIT], BF16)
-        first_turns = held("whole_even", [P, UNIT + BANK], I32)
+        first_wholes = held("first_wholes", [P, UNIT + BANK], I32)
         w1_woven = {
-            (0, 0): first_woven[:], (0, 1): second_woven[:], (1, 0): second_woven[:], (1, 1): first_turns[:, 0:UNIT].bitcast(BF16),
+            (0, 0): first_woven[:],
+            (0, 1): second_woven[:],
+            (1, 0): second_woven[:],
+            (1, 1): first_wholes[:, 0:UNIT].bitcast(BF16),
         }
         st_first = held("st_first", [P, UNIT], BF16)
         even_slices = held("even_slices", [P, PACK, W], BF16)
+
         odd_room = held("odd_room", [P, 2 * UNIT], F32)
         turns_odd = odd_room[:, BANK : BANK + UNIT].rearrange("p (t j) -> p t j", t=PACK)
         odd_slices = odd_room[:].bitcast(BF16)[:, 896:3584].rearrange("p (t x) -> p t x", t=PACK)[:, :, 0:W]
-        cosine_bufs = buffers("cosine", 2, [P, PACK, W], F32)
+        cosine_bufs = [held("cosine%d" % e, [P, PACK, W], F32) for e in range(2)]
+
         shared = held("shared", [P, 5248], F32)
         woven = shared[:, 0:UNIT].bitcast(BF16)
         kept_rows = shared[:, 576:832]
         wholes = {i: shared[:, 832:1856].bitcast(I32) for i in (3, 5, 7)}
-        wholes[0] = first_turns[:, BANK:]
+        wholes[0] = first_wholes[:, BANK:]
         wholes[2] = first_woven[:].bitcast(I32)
-        fourth_whole = held("fourth_whole", [P, UNIT], F32)
-        wholes[6] = wholes[4] = fourth_whole[:].bitcast(I32)
+        even_room = held("even_room", [P, UNIT], F32)
+        wholes[4] = wholes[6] = even_room[:].bitcast(I32)
         fourth_turns = second_woven[:].bitcast(F32).rearrange("p (t j) -> p t j", t=PACK)
         folded_turns = shared[:, 1792:2816].rearrange("p (t j) -> p t j", t=PACK)
         second_wholes = [shared[:, 3264:3776].bitcast(I32), shared[:, 2752:3264].bitcast(I32)]
         st_third = shared[:, 3712:4224].bitcast(BF16)
         st_second = shared[:, 4224:4736].bitcast(BF16)
+        folded_rest_rows = shared[:, 4224:5248]
+
         first_rest = held("st_c2", [P, PACK, W], F32)
         rest_odd = held("rest_odd", [P, PACK, W], F32)
         rest_even = [odd_room[:, lo : lo + BANK].rearrange("p (e j) -> p e j", e=2) for lo in (0, BANK + UNIT)]
         rest_bufs = [rest_even, [rest_odd[:, 0:2], rest_odd[:, 2:4]]]
-        turned_first = held("turned_first", [P, 4, P], F32)
-        turned_second = held("turned_second", [P, 4, P], F32)
+        turned = [held("turned%d" % half, [P, 4, P], F32) for half in range(2)]
 
         w1_c, w1_s, st_c, st_s, h_c, h_s = {}, {}, {}, {}, {}, {}
-        banks, y_place, x0_bank = {}, {}, {}
+        st_place, banks, y_banks, y_place, x0_bank = {}, {}, {}, {}, {}
 
         def round_w1(a, g, vector_columns):
             dst = w1_woven[a, g].rearrange("p (t m i) -> p m i t", t=PACK, i=PACK)
@@ -203,8 +205,6 @@ def tile_list_morton_grain_corrections_kernel(
                     out=w1_c[a, g][:, lo:hi].bitcast(FP8X4), scales=w1_s[a, g][:, lo:hi],
                     in_=w1_woven[a, g][:, PACK * lo : PACK * hi],
                 )
-
-        st_place = {}
 
         def round_stress(c, on_vector, place):
             st_place[c] = place
@@ -267,11 +267,8 @@ def tile_list_morton_grain_corrections_kernel(
         def turns_of(i):
             return {2: folded_turns, 4: fourth_turns, 6: last_turns}.get(i, turns_odd)
 
-        def whole_of(i):
-            return wholes[i]
-
         def whole_bank(i, pair):
-            bank = second_wholes[pair] if i == 1 else whole_of(i)[:, BANK * pair : BANK * (pair + 1)]
+            bank = second_wholes[pair] if i == 1 else wholes[i][:, BANK * pair : BANK * (pair + 1)]
             return bank.rearrange("p (e j) -> p e j", e=2)
 
         def rest_of(i, pair):
@@ -295,34 +292,31 @@ def tile_list_morton_grain_corrections_kernel(
 
         def folded_round(i):
             flat = turns_of(i).rearrange("p t j -> p (t j)")
-            nc.scalar.activation(whole_of(i).bitcast(U32), flat, ACT.Copy, bias=-0.25)
-
-        def folded_rest_of(i):
-            return shared[:, 4224:5248]
+            nc.scalar.activation(wholes[i].bitcast(U32), flat, ACT.Copy, bias=-0.25)
 
         def folded_rest(i):
             flat = turns_of(i).rearrange("p t j -> p (t j)")
-            nc.vector.tensor_tensor(folded_rest_of(i), flat, whole_of(i), ALU.subtract)
+            nc.vector.tensor_tensor(folded_rest_rows, flat, wholes[i], ALU.subtract)
 
         def folded_sine(i):
             nc.scalar.activation(
                 cosine_of(i)[:].rearrange("p t j -> p (t j)").rearrange("p (j e t) -> p j t e", e=4, t=PACK),
-                folded_rest_of(i).rearrange("p (t j e) -> p j t e", t=PACK, e=4),
+                folded_rest_rows.rearrange("p (t j e) -> p j t e", t=PACK, e=4),
                 ACT.Sin, bias=math.pi / 2, scale=-TWO_PI,
             )
 
-        def folded_gain(i, engine):
+        def folded_gain(i):
             a = UNITS[i][1]
-            engine.tensor_tensor(
+            nc.gpsimd.tensor_tensor(
                 woven_of(i).rearrange("p (u x) -> p u x", x=SPREAD * PACK),
                 cosine_of(i)[:].rearrange("p t j -> p (t j)").rearrange("p (u x) -> p u x", x=SPREAD * PACK),
-                gain_wide[:, a].rearrange("p j t -> p (j t)").unsqueeze(1).to_broadcast([P, W // SPREAD, SPREAD * PACK]),
+                gain_wide[:, a].rearrange("p j t -> p (j t)").unsqueeze(1).to_broadcast([P, W // SPREAD, P]),
                 ALU.mult,
             )
 
         def round_turns(i):
             nc.gpsimd.tensor_scalar(
-                whole_of(i), turns_of(i).rearrange("p t j -> p (t j)"), 1.0, 0.0, ALU.mult, ALU.add
+                wholes[i], turns_of(i).rearrange("p t j -> p (t j)"), 1.0, 0.0, ALU.mult, ALU.add
             )
 
         def round_bank(i, pair):
@@ -332,19 +326,16 @@ def tile_list_morton_grain_corrections_kernel(
                 phase_turns[:, a, 2 * pair : 2 * pair + 2].unsqueeze(2).to_broadcast([P, 2, W]), ALU.mult, ALU.add,
             )
 
-        def take_rest(i, pair):
-            nc.vector.scalar_tensor_tensor(
-                rest_of(i, pair), banks[i, pair][:], 1.0 / TWO_PI, whole_bank(i, pair), ALU.mult, ALU.subtract,
-            )
+        def rests(i):
+            for pair in range(2):
+                nc.vector.scalar_tensor_tensor(
+                    rest_of(i, pair), banks[i, pair][:], 1.0 / TWO_PI, whole_bank(i, pair), ALU.mult, ALU.subtract
+                )
 
         def reduce_on_vector(i):
             for pair in range(2):
                 round_bank(i, pair)
             rests(i)
-
-        def rests(i):
-            for pair in range(2):
-                take_rest(i, pair)
 
         def sine(i):
             a = UNITS[i][1]
@@ -367,8 +358,9 @@ def tile_list_morton_grain_corrections_kernel(
                 ALU.mult,
             )
 
-        def gain_on_gpsimd(i, entries):
+        def gain_on_gpsimd(i):
             a = UNITS[i][1]
+            entries = GPSIMD_ENTRIES[i]
             nc.gpsimd.tensor_tensor(
                 woven_of(i).rearrange("p (j t) -> p j t", t=PACK)[:, :entries],
                 cosine_of(i)[:].rearrange("p t j -> p j t")[:, :entries],
@@ -376,21 +368,17 @@ def tile_list_morton_grain_corrections_kernel(
                 ALU.mult,
             )
 
-        def slices_of(i):
-            return odd_slices if i % 2 else even_slices[:]
-
-        def gain_on_scalar(i, first=0):
+        def gain_on_scalar(i):
             a = UNITS[i][1]
-            slices = slices_of(i)
+            first = GPSIMD_ENTRIES.get(i, 0)
+            slices = odd_slices if i % 2 else even_slices[:]
             for t in range(PACK):
                 nc.scalar.activation(
                     slices[:, t, first:], cosine_of(i)[:, t, first:], ACT.Copy, scale=gain_t[:, a, t : t + 1]
                 )
-
-        def weave_on_scalar(i, first=0):
             nc.scalar.copy(
                 out=woven_of(i).rearrange("p (j e t) -> p j t e", e=4, t=PACK)[:, first // 4 :],
-                in_=slices_of(i).rearrange("p t (j e) -> p j t e", e=4)[:, first // 4 :],
+                in_=slices.rearrange("p t (j e) -> p j t e", e=4)[:, first // 4 :],
             )
 
         def second_product(parts, bank):
@@ -407,8 +395,6 @@ def tile_list_morton_grain_corrections_kernel(
                         start=(a == 0),
                         stop=(a == 1),
                     )
-
-        y_banks = {}
 
         def y_bank(e):
             return psum.tile([P, BANK], F32, name="y_bank%d" % e)
@@ -428,12 +414,9 @@ def tile_list_morton_grain_corrections_kernel(
         def places_of(c, n):
             return page_neg[n][:].indirect(offs2_t[:, W * c // LIST : W * (c + 1) // LIST])
 
-        def rows_of(n):
-            return y_flat[:, W * n : W * (n + 1)]
-
         def weighed_of(c, n):
-            if n == TILES - 1 and c < CHUNKS - 1:
-                return kept_rows if c < CHUNKS - 2 else None
+            if n == TILES - 1:
+                return kept_rows
             if (c, n) == (0, 1):
                 return shared[:, UNIT : UNIT + W]
             return y_flat[:, S + W * (4 * (c % 2) + n) : S + W * (4 * (c % 2) + n + 1)]
@@ -441,8 +424,8 @@ def tile_list_morton_grain_corrections_kernel(
         def weigh_on_vector(c, n):
             nc.vector.scalar_tensor_tensor(weighed_of(c, n), y_place[c, n], -1.0, wgo_of(c), ALU.mult, ALU.mult)
 
-        def y_out(c, n, rows=None):
-            nc.scalar.activation(rows_of(n) if rows is None else rows, y_place[c, n], ACT.Copy, scale=-1.0)
+        def y_out(c, n, rows):
+            nc.scalar.activation(rows, y_place[c, n], ACT.Copy, scale=-1.0)
 
         def pair_out(c, n):
             nc.scalar.activation(y_flat[:, W * n : W * (n + 2)], y_banks[c, n][:], ACT.Copy, scale=-1.0)
@@ -487,10 +470,15 @@ def tile_list_morton_grain_corrections_kernel(
             nc.scalar.copy(out=x0_rows[n][:, cols], in_=bank[:].rearrange("p b j -> p (b j)"))
             nc.sync.dma_start(out=out[P * n : P * (n + 1), cols], in_=x0_rows[n][:, cols])
 
-        def finish(engine, n, cols, diff, result):
+        def finish(engine, n, cols, diff):
             engine.tensor_tensor(diff, page_neg[n][:, cols], x0_rows[n][:, cols], ALU.add)
-            nc.scalar.activation(result, diff, ACT.Abs, bias=zero_bias[:])
-            nc.sync.dma_start(out=out[P * n : P * (n + 1), cols], in_=result)
+            nc.scalar.activation(diff, diff, ACT.Abs, bias=zero_bias[:])
+            nc.sync.dma_start(out=out[P * n : P * (n + 1), cols], in_=diff)
+
+        def next_even(i):
+            argument(i)
+            turns_out(i)
+            round_turns(i)
 
         nc.vector.tensor_scalar(phase_turns[:], phase_t[:], 1.0 / TWO_PI, 0.25, ALU.mult, ALU.add)
         nc.vector.tensor_scalar(phase_folded[:], phase_t[:], 1.0 / TWO_PI, None, ALU.mult)
@@ -514,9 +502,8 @@ def tile_list_morton_grain_corrections_kernel(
         round_stress(1, False, woven_of(0))
         quantise_stress(1)
         round_stress(2, False, st_second)
-        gain_on_gpsimd(0, GPSIMD_ENTRIES)
-        gain_on_scalar(0, GPSIMD_ENTRIES)
-        weave_on_scalar(0, GPSIMD_ENTRIES)
+        gain_on_gpsimd(0)
+        gain_on_scalar(0)
         reduce_on_vector(1)
         argument(2)
         argument(3)
@@ -528,11 +515,6 @@ def tile_list_morton_grain_corrections_kernel(
         folded_turns_out(2)
         folded_round(2)
         turns_out(3)
-
-        def next_even(i):
-            argument(i)
-            turns_out(i)
-            round_turns(i)
 
         last = CHUNKS - 1
         for c in range(last):
@@ -547,13 +529,13 @@ def tile_list_morton_grain_corrections_kernel(
                 weigh_on_vector(c, 0)
                 scatter(c, 0)
                 second_product([(c, 3)], first_bank)
-                y_out(c, 2, rows=fourth_whole[:, 0:W])
-                nc.gpsimd.tensor_tensor(weighed_of(c, 2), fourth_whole[:, 0:W], wgo_of(c), ALU.mult)
+                y_out(c, 2, even_room[:, 0:W])
+                nc.gpsimd.tensor_tensor(weighed_of(c, 2), even_room[:, 0:W], wgo_of(c), ALU.mult)
                 next_even(even + 2)
                 folded_sine(even)
-                folded_gain(even, nc.gpsimd)
+                folded_gain(even)
                 rests(odd)
-                y_out(c, 3, rows=first_kept)
+                y_out(c, 3, first_kept)
                 weigh_on_vector(c, 1)
                 scatter(c, 1)
                 scatter(c, 2)
@@ -573,18 +555,16 @@ def tile_list_morton_grain_corrections_kernel(
                 if c < last - 1:
                     pair_out(c, 2)
                     weigh_on_gpsimd(c, 2)
-                    gain_on_gpsimd(even, LATER_ENTRIES)
+                    gain_on_gpsimd(even)
                     scatter(c, 2)
-                    gain_on_scalar(even, LATER_ENTRIES)
-                    weave_on_scalar(even, LATER_ENTRIES)
+                    gain_on_scalar(even)
                     next_even(even + 2)
                 else:
-                    gain_on_gpsimd(even, W)
+                    gain_on_gpsimd(even)
                     for half in range(2):
                         turn_x0(1, half)
             sine(odd)
             gain_on_scalar(odd)
-            weave_on_scalar(odd)
             if c < last - 1:
                 argument(odd + 2)
                 turns_out(odd + 2)
@@ -592,8 +572,8 @@ def tile_list_morton_grain_corrections_kernel(
         quantise_h(last, pieces=2)
         spent_turns = odd_room[:, BANK : BANK + UNIT]
         spent = spent_turns[:, 0:BANK]
-        y_out(last - 1, 2, rows=spent[:, 0:W])
-        y_out(last - 1, 3, rows=spent[:, W:BANK])
+        y_out(last - 1, 2, spent[:, 0:W])
+        y_out(last - 1, 3, spent[:, W:BANK])
         nc.vector.tensor_tensor(places_of(last - 1, 2), spent[:, 0:W], wgo_of(last - 1), ALU.mult)
         second_product([(last, 0)], y_bank(1))
         second_product([(last, 1)], arg_bank(2, 0, [P, BANK]))
@@ -602,11 +582,11 @@ def tile_list_morton_grain_corrections_kernel(
         weigh_on_vector(last, 0)
         scatter(last, 0)
         nc.gpsimd.tensor_tensor(spent[:, 0:W], spent[:, W:BANK], wgo_of(last - 1), ALU.mult)
-        y_out(last, 1, rows=shared[:, 0:W])
+        y_out(last, 1, shared[:, 0:W])
         nc.gpsimd.tensor_tensor(weighed_of(last, 1), shared[:, 0:W], wgo_of(last), ALU.mult)
         scatter(last, 1)
-        y_out(last, 2, rows=shared[:, 2 * W : 3 * W])
-        y_out(last, 3, rows=shared[:, W : 2 * W])
+        y_out(last, 2, shared[:, 2 * W : 3 * W])
+        y_out(last, 3, shared[:, W : 2 * W])
         nc.gpsimd.tensor_tensor(
             spent_turns[:, W : 3 * W].rearrange("p (e j) -> p e j", e=2),
             shared[:, W : 3 * W].rearrange("p (e j) -> p e j", e=2),
@@ -614,19 +594,22 @@ def tile_list_morton_grain_corrections_kernel(
         )
         nc.vector.tensor_copy(places_of(last, 2), spent_turns[:, 2 * W : 3 * W])
         nc.vector.tensor_copy(page_neg[TILES - 1][:].indirect(offs2_t[:, W * (last - 1) // LIST :]), spent)
+
         halves = [slice(0, BANK), slice(BANK, S)]
         diffs = [shared[:, P + BANK * e : P + BANK * (e + 1)] for e in range(2)]
         diffs = diffs + [x0_flat[:, W + BANK * e : W + BANK * (e + 1)] for e in range(2)]
         for half in range(2):
-            finish(nc.gpsimd, 0, halves[half], diffs[half], diffs[half])
-        turned = [turned_first[:], turned_second[:]]
+            finish(nc.gpsimd, 0, halves[half], diffs[half])
         for half in range(2):
-            turn_page(1, half, turned[half])
+            turn_page(1, half, turned[half][:])
         for half in range(2):
-            turn_back(1, half, turned[half])
+            turn_back(1, half, turned[half][:])
         for half in range(2):
-            finish(nc.gpsimd, 2, halves[half], diffs[2 + half], diffs[2 + half])
+            finish(nc.gpsimd, 2, halves[half], diffs[2 + half])
         start = 2 * S + 2 * W
-        for half in range(2):
-            late = x0_flat[:, start + BANK * half : start + BANK * (half + 1)]
-            finish(nc.vector, 3, halves[half], late, late)
+        finish(nc.vector, 3, halves[0], x0_flat[:, start : start + BANK])
+        late = x0_flat[:, start + BANK : start + S]
+        nc.vector.tensor_tensor(late, page_neg[3][:, halves[1]], x0_rows[3][:, halves[1]], ALU.add)
+        nc.vector.scalar_tensor_tensor(late[:, 0:W], late[:, 0:W], -1.0, late[:, 0:W], ALU.mult, ALU.max)
+        nc.scalar.activation(late[:, W:], late[:, W:], ACT.Abs, bias=zero_bias[:])
+        nc.sync.dma_start(out=out[P * 3 :, halves[1]], in_=late)

import math
from contextlib import ExitStack

import concourse.mybir as mybir
from concourse.masks import make_identity

K, K2, H, N, T, S = 1024, 512, 1024, 512, 4096, 1024
FLOPS = 2 * (K + K2) * H * S + 2 * H * N * S

F32 = mybir.dt.float32
BF16 = mybir.dt.bfloat16
I32 = mybir.dt.int32
U32 = mybir.dt.uint32
U16 = mybir.dt.uint16
U8 = mybir.dt.uint8
FP8X4 = mybir.dt.float8_e4m3fn_x4
FP4X4 = mybir.dt.float4_e2m1fn_x4
ALU = mybir.AluOpType
ACT = mybir.ActivationFunctionType

P = 128
PACK = 4
PASS = P * PACK
BANK = 512
LIST = 16
W = 256
CHUNKS = S // W
TILES = N // P
UNITS = [(c, a) for c in range(CHUNKS) for a in range(H // PASS)]
TWO_PI = 2.0 * math.pi

UNIT = PACK * W
SPREAD = 32
BANK_PAIRS = (0, 1, 2, 1, 0, 1, 2, 0)
GPSIMD_ENTRIES = {0: 176, 4: 192, 6: W}


def tile_list_morton_grain_corrections_kernel(
    tc, tab_words, tab_scales, offs, w1, stress, w2_words, w2_scales, phase, gain,
    w3_words, w3_scales, offs2, wgo, x0, out,
):
    nc = tc.nc
    with ExitStack() as ctx:
        keep = ctx.enter_context(tc.tile_pool(name="keep", bufs=1))
        psum = ctx.enter_context(tc.psum_pool(name="psum", bufs=1))

        def held(name, shape, dtype):
            return keep.tile(shape, dtype, name=name, align_bytes=64)

        def arg_bank(pair_of_banks, e, shape):
            return psum.tile(shape, F32, name="arg_bank%d" % (2 * pair_of_banks + e))

        def cast(on_vector, dst, src):
            if on_vector:
                nc.vector.tensor_copy(out=dst, in_=src)
            else:
                nc.scalar.copy(out=dst, in_=src)

        offs_t = held("offs_t", [P, S // LIST], U16)
        offs2_t = held("offs2_t", [P, S // LIST], U16)
        tab_w = [held("tab_w%d" % g, [P, T], U32) for g in range(2)]
        tab_s = held("tab_s", [P, T], U8)
        picked_rows = held("picked_rows", [P, S], U8)
        v_s = held("v_s", [P, 2 * S], U8)
        w2_raw = held("w2_raw", [P, 2 * H], U8)
        w2s_raw = held("w2s_raw", [P, H], U8)
        w2_c = held("w2_c", [P, 2 * H], U8)
        w2_s = held("w2_s", [P, H], U8)
        w3_c = held("w3_c", [P, 2, N], U32)
        w3_s = held("w3_s", [P, N], U8)
        phase_t = held("phase_t", [P, 2, PACK], F32)
        phase_turns = held("phase_turns", [P, 2, PACK], F32)
        phase_folded = held("phase_folded", [P, 2, PACK], F32)
        phase_sine = held("phase_sine", [P, 2, PACK], F32)
        gain_t = held("gain_t", [P, 2, PACK], F32)
        wgo_t = held("wgo_t", [P, S], F32)
        w1_raw = {(a, g): held("w1_raw%d%d" % (a, g), [P, PACK, PASS], F32) for a in range(2) for g in range(2)}
        st_raw = [held("st_raw%d" % c, [P, PACK, W], F32) for c in range(CHUNKS)]
        zero = held("zero", [P, 1], F32)
        zero_bias = held("zero_bias", [P, 1], F32)
        ident = held("ident", [P, P], F32)

        nc.vector.memset(zero[:], 0.0)
        nc.scalar.activation(zero_bias[:], zero[:], ACT.Sin)

        nc.vector.memset(w2s_raw[:].bitcast(I32), 0)
        nc.sync.dma_start(out=tab_s[0:32, :].bitcast(I32), in_=tab_scales.rearrange("g q n -> q g n").bitcast(I32))
        nc.vector.memset(tab_s[32:64, :].bitcast(I32), 0)
        nc.vector.memset(tab_s[64:128, :].bitcast(I32), 0)
        nc.gpsimd.memset(v_s[:].bitcast(I32), 0)
        nc.gpsimd.memset(w3_s[:].bitcast(I32), 0)

        def load_w1(a, g):
            block = w1[PASS * g : PASS * (g + 1), PASS * a : PASS * (a + 1)]
            nc.sync.dma_start(out=w1_raw[a, g][:], in_=block.rearrange("(p i) r -> p i r", i=PACK))

        def load_tab(g):
            words = tab_words[g].rearrange("p n i -> p (n i)")
            nc.sync.dma_start(out=tab_w[g][:].bitcast(I32), in_=words.bitcast(I32))

        def load_stress(c):
            columns = stress[:, W * c : W * (c + 1)]
            nc.sync.dma_start(out=st_raw[c][:], in_=columns.rearrange("(p i) j -> p i j", i=PACK))

        nc.sync.dma_start(offs_t[:], offs)
        load_tab(0)
        for quad in range(4):
            nc.sync.dma_start(
                out=w2s_raw[32 * quad : 32 * quad + 4, :].bitcast(I32),
                in_=w2_scales[0, 4 * quad : 4 * quad + 4, :].bitcast(I32),
            )
        nc.sync.dma_start(out=w2_raw[:].bitcast(I32), in_=w2_words[0].bitcast(I32))
        load_tab(1)
        nc.sync.dma_start(out=phase_t[:], in_=phase.rearrange("(a p t) -> p a t", a=2, t=PACK))
        nc.sync.dma_start(out=gain_t[:], in_=gain.rearrange("(a p t) -> p a t", a=2, t=PACK))
        load_stress(0)
        load_w1(0, 0)
        nc.vector.tensor_copy(picked_rows[:], tab_s[:].indirect(offs_t[:]))
        for quad in range(4):
            nc.sync.dma_start(
                out=v_s[32 * quad : 32 * quad + 4, :].bitcast(I32),
                in_=picked_rows[8 * quad : 8 * quad + 8, :].bitcast(I32),
            )
        load_w1(0, 1)
        load_w1(1, 0)
        load_w1(1, 1)
        load_stress(1)
        load_stress(2)
        load_stress(3)
        nc.sync.dma_start(out=w3_c[:].bitcast(I32), in_=w3_words.rearrange("a p n i -> p a (n i)").bitcast(I32))
        for quad in range(4):
            nc.sync.dma_start(
                out=w3_s[32 * quad : 32 * quad + 8, :].bitcast(I32),
                in_=w3_scales[:, 4 * quad : 4 * quad + 4, :].bitcast(I32),
            )
        nc.sync.dma_start(offs2_t[:], offs2)
        nc.sync.dma_start(out=wgo_t[:], in_=wgo)

        make_identity(nc, ident[:])

        nc.vector.tensor_copy(
            out=w2_c[:].rearrange("p (a t m b) -> p a t m b", a=2, t=PACK, b=2),
            in_=w2_raw[:].rearrange("p (a m t b) -> p a t m b", a=2, t=PACK, b=2),
        )
        nc.vector.tensor_copy(
            out=w2_s[:].rearrange("p (a t m) -> p a t m", a=2, t=PACK),
            in_=w2s_raw[:].rearrange("p (a m t) -> p a t m", a=2, t=PACK),
        )

        first_woven = held("first_woven", [P, 2 * UNIT], BF16)
        second_woven = held("second_woven", [P, 2 * UNIT], BF16)
        first_wholes = held("first_wholes", [P, UNIT + BANK], I32)
        w1_woven = {
            (0, 0): first_woven[:],
            (0, 1): second_woven[:],
            (1, 0): second_woven[:],
            (1, 1): first_wholes[:, 0:UNIT].bitcast(BF16),
        }
        st_first = held("st_first", [P, UNIT], BF16)
        even_slices = held("even_slices", [P, PACK, W], BF16)

        odd_room = held("odd_room", [P, 2 * UNIT], F32)
        turns_odd = odd_room[:, BANK : BANK + UNIT].rearrange("p (t j) -> p t j", t=PACK)
        odd_slices = odd_room[:].bitcast(BF16)[:, 896:3584].rearrange("p (t x) -> p t x", t=PACK)[:, :, 0:W]
        cosine_bufs = [held("cosine%d" % e, [P, PACK, W], F32) for e in range(2)]

        shared = held("shared", [P, 5248], F32)
        woven = shared[:, 0:UNIT].bitcast(BF16)
        kept_rows = shared[:, 576:832]
        wholes = {i: shared[:, 832:1856].bitcast(I32) for i in (3, 5, 7)}
        wholes[0] = first_wholes[:, BANK:]
        wholes[2] = first_woven[:].bitcast(I32)
        even_room = held("even_room", [P, UNIT], F32)
        wholes[4] = wholes[6] = even_room[:].bitcast(I32)
        fourth_turns = second_woven[:].bitcast(F32).rearrange("p (t j) -> p t j", t=PACK)
        folded_turns = shared[:, 1792:2816].rearrange("p (t j) -> p t j", t=PACK)
        second_wholes = [shared[:, 3264:3776].bitcast(I32), shared[:, 2752:3264].bitcast(I32)]
        st_third = shared[:, 3712:4224].bitcast(BF16)
        st_second = shared[:, 4224:4736].bitcast(BF16)
        folded_rest_rows = shared[:, 4224:5248]

        first_rest = held("st_c2", [P, PACK, W], F32)
        rest_odd = held("rest_odd", [P, PACK, W], F32)
        rest_even = [odd_room[:, lo : lo + BANK].rearrange("p (e j) -> p e j", e=2) for lo in (0, BANK + UNIT)]
        rest_bufs = [rest_even, [rest_odd[:, 0:2], rest_odd[:, 2:4]]]
        turned = [held("turned%d" % half, [P, 4, P], F32) for half in range(2)]

        w1_c, w1_s, st_c, st_s, h_c, h_s = {}, {}, {}, {}, {}, {}
        st_place, banks, y_banks, y_place, x0_bank = {}, {}, {}, {}, {}

        def round_w1(a, g, vector_columns):
            dst = w1_woven[a, g].rearrange("p (t m i) -> p m i t", t=PACK, i=PACK)
            src = w1_raw[a, g][:].rearrange("p i (m t) -> p m i t", t=PACK)
            if vector_columns > 0:
                cast(True, dst[:, :vector_columns], src[:, :vector_columns])
            if vector_columns < P:
                cast(False, dst[:, vector_columns:], src[:, vector_columns:])

        def quantise_w1(a, g, pieces=1):
            w1_c[a, g] = held("w1_c%d%d" % (a, g), [P, PASS], U32)
            w1_s[a, g] = held("w1_s%d%d" % (a, g), [P, PASS], U8)
            for lo in range(0, PASS, PASS // pieces):
                hi = lo + PASS // pieces
                nc.vector.quantize_mx(
                    out=w1_c[a, g][:, lo:hi].bitcast(FP8X4), scales=w1_s[a, g][:, lo:hi],
                    in_=w1_woven[a, g][:, PACK * lo : PACK * hi],
                )

        def round_stress(c, on_vector, place):
            st_place[c] = place
            cast(
                on_vector,
                place.rearrange("p (j e i) -> p j i e", e=4, i=PACK),
                st_raw[c][:].rearrange("p i (j e) -> p j i e", e=4),
            )

        def quantise_stress(c):
            st_c[c] = held("st_c%d" % c, [P, W], U32)
            st_s[c] = held("st_s%d" % c, [P, W], U8)
            nc.vector.quantize_mx(out=st_c[c][:].bitcast(FP8X4), scales=st_s[c][:], in_=st_place[c])

        v_c = [held("v_c%d" % g, [P, S], U32) for g in range(2)]
        for g in range(2):
            nc.vector.tensor_copy(v_c[g][:], tab_w[g][:].indirect(offs_t[:]))

        x0_flat = held("tab_w0", [P, TILES * S + 2 * W], F32)
        x0_rows = {n: x0_flat[:, S * n + W * e : S * (n + 1) + W * e] for n, e in enumerate((0, 1, 1, 2))}
        for n in range(TILES):
            nc.sync.dma_start(out=x0_rows[n], in_=x0[P * n : P * (n + 1), :])
        y_all = held("tab_w1", [P, 4 * S], F32)
        y_flat = y_all[:, BANK:]
        first_kept = y_all[:, W // 2 : 3 * W // 2]
        last_turns = y_all[:, 0:UNIT].rearrange("p (t j) -> p t j", t=PACK)
        page_neg = [held("page_neg%d" % n, [P, S], F32) for n in range(TILES)]

        def argument(i):
            c, a = UNITS[i]
            cols = slice(W * c, W * (c + 1))
            for pair in range(2):
                bank = banks[i, pair] = arg_bank(BANK_PAIRS[i], pair, [P, 2, W])
                passes = [0, 1, "stress"] if 2 <= i < 7 else ["stress", 0, 1]
                for place, g in enumerate(passes):
                    for e in range(2):
                        t = 2 * pair + e
                        first = PASS * a + P * t
                        if g == "stress":
                            operands = dict(
                                lhsT=w2_c[:, 2 * first : 2 * (first + P)].bitcast(FP4X4),
                                lhsT_scale=w2_s[:, first : first + P],
                                rhs=st_c[c][:].bitcast(FP8X4),
                                rhs_scale=st_s[c][:],
                            )
                        else:
                            operands = dict(
                                lhsT=w1_c[a, g][:, P * t : P * (t + 1)].bitcast(FP8X4),
                                lhsT_scale=w1_s[a, g][:, P * t : P * (t + 1)],
                                rhs=v_c[g][:, cols].bitcast(FP8X4),
                                rhs_scale=v_s[:, S * g + W * c : S * g + W * (c + 1)],
                            )
                        nc.tensor.matmul_mx(
                            out=bank[:, e, :], start=(place == 0 and e == 0), stop=(place == 2 and e == 1), **operands
                        )

        def cosine_of(i):
            return cosine_bufs[i % 2]

        def turns_of(i):
            return {2: folded_turns, 4: fourth_turns, 6: last_turns}.get(i, turns_odd)

        def whole_bank(i, pair):
            bank = second_wholes[pair] if i == 1 else wholes[i][:, BANK * pair : BANK * (pair + 1)]
            return bank.rearrange("p (e j) -> p e j", e=2)

        def rest_of(i, pair):
            return first_rest[:, 2 * pair : 2 * pair + 2] if i == 1 else rest_bufs[i % 2][pair]

        def turns_out(i):
            a = UNITS[i][1]
            for t in range(PACK):
                nc.scalar.activation(
                    turns_of(i)[:, t, :], banks[i, t // 2][:, t % 2, :], ACT.Identity,
                    bias=phase_turns[:, a, t : t + 1], scale=1.0 / TWO_PI,
                )

        def folded_turns_out(i):
            a = UNITS[i][1]
            for t in range(PACK):
                nc.scalar.activation(
                    turns_of(i)[:, t, :], banks[i, t // 2][:, t % 2, :], ACT.Abs,
                    bias=phase_folded[:, a, t : t + 1], scale=1.0 / TWO_PI,
                )

        def folded_round(i):
            flat = turns_of(i).rearrange("p t j -> p (t j)")
            nc.scalar.activation(wholes[i].bitcast(U32), flat, ACT.Copy, bias=-0.25)

        def folded_rest(i):
            flat = turns_of(i).rearrange("p t j -> p (t j)")
            nc.vector.tensor_tensor(folded_rest_rows, flat, wholes[i], ALU.subtract)

        def folded_sine(i):
            nc.scalar.activation(
                cosine_of(i)[:].rearrange("p t j -> p (t j)").rearrange("p (j e t) -> p j t e", e=4, t=PACK),
                folded_rest_rows.rearrange("p (t j e) -> p j t e", t=PACK, e=4),
                ACT.Sin, bias=math.pi / 2, scale=-TWO_PI,
            )

        def folded_gain(i):
            a = UNITS[i][1]
            nc.gpsimd.tensor_tensor(
                woven_of(i).rearrange("p (u x) -> p u x", x=SPREAD * PACK),
                cosine_of(i)[:].rearrange("p t j -> p (t j)").rearrange("p (u x) -> p u x", x=SPREAD * PACK),
                gain_wide[:, a].rearrange("p j t -> p (j t)").unsqueeze(1).to_broadcast([P, W // SPREAD, P]),
                ALU.mult,
            )

        def round_turns(i):
            nc.gpsimd.tensor_scalar(
                wholes[i], turns_of(i).rearrange("p t j -> p (t j)"), 1.0, 0.0, ALU.mult, ALU.add
            )

        def round_bank(i, pair):
            a = UNITS[i][1]
            nc.vector.scalar_tensor_tensor(
                whole_bank(i, pair), banks[i, pair][:], 1.0 / TWO_PI,
                phase_turns[:, a, 2 * pair : 2 * pair + 2].unsqueeze(2).to_broadcast([P, 2, W]), ALU.mult, ALU.add,
            )

        def rests(i):
            for pair in range(2):
                nc.vector.scalar_tensor_tensor(
                    rest_of(i, pair), banks[i, pair][:], 1.0 / TWO_PI, whole_bank(i, pair), ALU.mult, ALU.subtract
                )

        def reduce_on_vector(i):
            for pair in range(2):
                round_bank(i, pair)
            rests(i)

        def sine(i):
            a = UNITS[i][1]
            for t in range(PACK):
                nc.scalar.activation(
                    cosine_of(i)[:, t, :], rest_of(i, t // 2)[:, t % 2, :], ACT.Sin,
                    bias=phase_sine[:, a, t : t + 1], scale=TWO_PI,
                )

        def woven_of(i):
            a = UNITS[i][1]
            return woven[:, UNIT * a : UNIT * (a + 1)]

        def gain_on_vector(i):
            a = UNITS[i][1]
            nc.vector.tensor_tensor(
                woven_of(i).rearrange("p (j e t) -> p j t e", e=4, t=PACK),
                cosine_of(i)[:].rearrange("p t (j e) -> p j t e", e=4),
                gain_t[:, a].unsqueeze(1).unsqueeze(3).to_broadcast([P, W // 4, PACK, 4]),
                ALU.mult,
            )

        def gain_on_gpsimd(i):
            a = UNITS[i][1]
            entries = GPSIMD_ENTRIES[i]
            nc.gpsimd.tensor_tensor(
                woven_of(i).rearrange("p (j t) -> p j t", t=PACK)[:, :entries],
                cosine_of(i)[:].rearrange("p t j -> p j t")[:, :entries],
                gain_t[:, a].unsqueeze(1).to_broadcast([P, entries, PACK]),
                ALU.mult,
            )

        def gain_on_scalar(i):
            a = UNITS[i][1]
            first = GPSIMD_ENTRIES.get(i, 0)
            slices = odd_slices if i % 2 else even_slices[:]
            for t in range(PACK):
                nc.scalar.activation(
                    slices[:, t, first:], cosine_of(i)[:, t, first:], ACT.Copy, scale=gain_t[:, a, t : t + 1]
                )
            nc.scalar.copy(
                out=woven_of(i).rearrange("p (j e t) -> p j t e", e=4, t=PACK)[:, first // 4 :],
                in_=slices.rearrange("p t (j e) -> p j t e", e=4)[:, first // 4 :],
            )

        def second_product(parts, bank):
            y_banks[parts[0]] = bank
            for e, (c, n) in enumerate(parts):
                y_place[c, n] = bank[:, W * e : W * (e + 1)]
                for a in range(2):
                    nc.tensor.matmul_mx(
                        out=y_place[c, n],
                        lhsT=w3_c[:, a, P * n : P * (n + 1)].bitcast(FP8X4),
                        lhsT_scale=w3_s[4 * a : P, P * n : P * (n + 1)],
                        rhs=h_c[c][:, W * a : W * (a + 1)].bitcast(FP8X4),
                        rhs_scale=h_s[c][:, W * a : W * (a + 1)],
                        start=(a == 0),
                        stop=(a == 1),
                    )

        def y_bank(e):
            return psum.tile([P, BANK], F32, name="y_bank%d" % e)

        def quantise_h(c, pieces=1):
            h_c[c] = held("h_c%d" % c, [P, 2 * W], U32)
            h_s[c] = held("h_s%d" % c, [P, 2 * W], U8)
            for lo in range(0, 2 * W, 2 * W // pieces):
                hi = lo + 2 * W // pieces
                nc.vector.quantize_mx(
                    out=h_c[c][:, lo:hi].bitcast(FP8X4), scales=h_s[c][:, lo:hi], in_=woven[:, PACK * lo : PACK * hi]
                )

        def wgo_of(c):
            return wgo_t[:, W * c : W * (c + 1)]

        def places_of(c, n):
            return page_neg[n][:].indirect(offs2_t[:, W * c // LIST : W * (c + 1) // LIST])

        def weighed_of(c, n):
            if n == TILES - 1:
                return kept_rows
            if (c, n) == (0, 1):
                return shared[:, UNIT : UNIT + W]
            return y_flat[:, S + W * (4 * (c % 2) + n) : S + W * (4 * (c % 2) + n + 1)]

        def weigh_on_vector(c, n):
            nc.vector.scalar_tensor_tensor(weighed_of(c, n), y_place[c, n], -1.0, wgo_of(c), ALU.mult, ALU.mult)

        def y_out(c, n, rows):
            nc.scalar.activation(rows, y_place[c, n], ACT.Copy, scale=-1.0)

        def pair_out(c, n):
            nc.scalar.activation(y_flat[:, W * n : W * (n + 2)], y_banks[c, n][:], ACT.Copy, scale=-1.0)

        def weigh_on_gpsimd(c, n, count=1):
            rows = first_kept if (c, n) == (0, 3) else y_flat[:, W * n : W * (n + count)]
            rows = rows.rearrange("p (e j) -> p e j", e=count)
            first = S + W * (4 * (c % 2) + n)
            weighed = weighed_of(c, n) if count == 1 else y_flat[:, first : first + W * count]
            nc.gpsimd.tensor_tensor(
                weighed.rearrange("p (e j) -> p e j", e=count), rows,
                wgo_of(c).unsqueeze(1).to_broadcast([P, count, W]), ALU.mult,
            )

        def scatter(c, n):
            nc.vector.tensor_copy(places_of(c, n), weighed_of(c, n))

        def blocks_of(half):
            return [(b, slice(BANK * half + P * b, BANK * half + P * (b + 1))) for b in range(4)]

        def turn_x0(n, half):
            x0_bank[n, half] = arg_bank(1, half, [P, 4, P])
            for b, blk in blocks_of(half):
                nc.tensor.matmul(
                    x0_bank[n, half][:, b, :], x0_rows[n][:, blk], ident[:],
                    start=(b == 0), stop=False, is_transpose=True,
                )

        def turn_page(n, half, turned):
            bank = x0_bank[n, half]
            for b, blk in blocks_of(half):
                nc.tensor.matmul(
                    bank[:, b, :], page_neg[n][:, blk], ident[:], start=False, stop=(b == 3), is_transpose=True
                )
            nc.scalar.activation(turned, bank[:], ACT.Abs, bias=zero_bias[:])

        def turn_back(n, half, turned):
            bank = x0_bank[n, half]
            cols = slice(BANK * half, BANK * (half + 1))
            for b, blk in blocks_of(half):
                nc.tensor.transpose(bank[:, b, :], turned[:, b, :], ident[:])
            nc.scalar.copy(out=x0_rows[n][:, cols], in_=bank[:].rearrange("p b j -> p (b j)"))
            nc.sync.dma_start(out=out[P * n : P * (n + 1), cols], in_=x0_rows[n][:, cols])

        def finish(engine, n, cols, diff):
            engine.tensor_tensor(diff, page_neg[n][:, cols], x0_rows[n][:, cols], ALU.add)
            nc.scalar.activation(diff, diff, ACT.Abs, bias=zero_bias[:])
            nc.sync.dma_start(out=out[P * n : P * (n + 1), cols], in_=diff)

        def next_even(i):
            argument(i)
            turns_out(i)
            round_turns(i)

        nc.vector.tensor_scalar(phase_turns[:], phase_t[:], 1.0 / TWO_PI, 0.25, ALU.mult, ALU.add)
        nc.vector.tensor_scalar(phase_folded[:], phase_t[:], 1.0 / TWO_PI, None, ALU.mult)
        nc.vector.tensor_scalar(phase_sine[:], phase_t[:], math.pi / 2, None, ALU.add)
        gain_wide = held("gain_wide", [P, 2, SPREAD, PACK], F32)
        nc.scalar.copy(out=gain_wide[:], in_=gain_t[:].unsqueeze(2).to_broadcast([P, 2, SPREAD, PACK]))
        round_stress(0, False, st_first[:])
        quantise_stress(0)
        round_w1(0, 0, 64)
        quantise_w1(0, 0)
        round_w1(0, 1, 80)
        quantise_w1(0, 1, pieces=2)
        argument(0)
        round_w1(1, 0, 0)
        reduce_on_vector(0)
        round_w1(1, 1, 128)
        quantise_w1(1, 0)
        quantise_w1(1, 1, pieces=2)
        argument(1)
        sine(0)
        round_stress(1, False, woven_of(0))
        quantise_stress(1)
        round_stress(2, False, st_second)
        gain_on_gpsimd(0)
        gain_on_scalar(0)
        reduce_on_vector(1)
        argument(2)
        argument(3)
        sine(1)
        round_stress(3, True, st_third)
        quantise_stress(3)
        gain_on_vector(1)
        quantise_stress(2)
        folded_turns_out(2)
        folded_round(2)
        turns_out(3)

        last = CHUNKS - 1
        for c in range(last):
            even, odd = 2 * c + 2, 2 * c + 3
            quantise_h(c)
            if c == 0:
                first_bank = y_bank(0)
                second_product([(c, 0)], first_bank)
                second_product([(c, 1), (c, 2)], y_bank(1))
                folded_rest(even)
                round_turns(odd)
                weigh_on_vector(c, 0)
                scatter(c, 0)
                second_product([(c, 3)], first_bank)
                y_out(c, 2, even_room[:, 0:W])
                nc.gpsimd.tensor_tensor(weighed_of(c, 2), even_room[:, 0:W], wgo_of(c), ALU.mult)
                next_even(even + 2)
                folded_sine(even)
                folded_gain(even)
                rests(odd)
                y_out(c, 3, first_kept)
                weigh_on_vector(c, 1)
                scatter(c, 1)
                scatter(c, 2)
            else:
                second_product([(c, 0), (c, 1)], y_bank(0))
                rests(even)
                weigh_on_gpsimd(c - 1, 3)
                scatter(c - 1, 3)
                round_turns(odd)
                pair_out(c, 0)
                second_product([(c, 2), (c, 3)], y_bank(0))
                sine(even)
                weigh_on_gpsimd(c, 0, 2)
                rests(odd)
                scatter(c, 0)
                scatter(c, 1)
                if c < last - 1:
                    pair_out(c, 2)
                    weigh_on_gpsimd(c, 2)
                    gain_on_gpsimd(even)
                    scatter(c, 2)
                    gain_on_scalar(even)
                    next_even(even + 2)
                else:
                    gain_on_gpsimd(even)
                    for half in range(2):
                        turn_x0(1, half)
            sine(odd)
            gain_on_scalar(odd)
            if c < last - 1:
                argument(odd + 2)
                turns_out(odd + 2)

        quantise_h(last, pieces=2)
        spent_turns = odd_room[:, BANK : BANK + UNIT]
        spent = spent_turns[:, 0:BANK]
        y_out(last - 1, 2, spent[:, 0:W])
        y_out(last - 1, 3, spent[:, W:BANK])
        nc.vector.tensor_tensor(places_of(last - 1, 2), spent[:, 0:W], wgo_of(last - 1), ALU.mult)
        second_product([(last, 0)], y_bank(1))
        second_product([(last, 1)], arg_bank(2, 0, [P, BANK]))
        second_product([(last, 2)], arg_bank(2, 1, [P, BANK]))
        second_product([(last, 3)], y_bank(0))
        weigh_on_vector(last, 0)
        scatter(last, 0)
        nc.gpsimd.tensor_tensor(spent[:, 0:W], spent[:, W:BANK], wgo_of(last - 1), ALU.mult)
        y_out(last, 1, shared[:, 0:W])
        nc.gpsimd.tensor_tensor(weighed_of(last, 1), shared[:, 0:W], wgo_of(last), ALU.mult)
        scatter(last, 1)
        y_out(last, 2, shared[:, 2 * W : 3 * W])
        y_out(last, 3, shared[:, W : 2 * W])
        nc.gpsimd.tensor_tensor(
            spent_turns[:, W : 3 * W].rearrange("p (e j) -> p e j", e=2),
            shared[:, W : 3 * W].rearrange("p (e j) -> p e j", e=2),
            wgo_of(last).unsqueeze(1).to_broadcast([P, 2, W]), ALU.mult,
        )
        nc.vector.tensor_copy(places_of(last, 2), spent_turns[:, 2 * W : 3 * W])
        nc.vector.tensor_copy(page_neg[TILES - 1][:].indirect(offs2_t[:, W * (last - 1) // LIST :]), spent)

        halves = [slice(0, BANK), slice(BANK, S)]
        diffs = [shared[:, P + BANK * e : P + BANK * (e + 1)] for e in range(2)]
        diffs = diffs + [x0_flat[:, W + BANK * e : W + BANK * (e + 1)] for e in range(2)]
        for half in range(2):
            finish(nc.gpsimd, 0, halves[half], diffs[half])
        for half in range(2):
            turn_page(1, half, turned[half][:])
        for half in range(2):
            turn_back(1, half, turned[half][:])
        for half in range(2):
            finish(nc.gpsimd, 2, halves[half], diffs[2 + half])
        start = 2 * S + 2 * W
        finish(nc.vector, 3, halves[0], x0_flat[:, start : start + BANK])
        late = x0_flat[:, start + BANK : start + S]
        nc.vector.tensor_tensor(late, page_neg[3][:, halves[1]], x0_rows[3][:, halves[1]], ALU.add)
        nc.vector.scalar_tensor_tensor(late[:, 0:W], late[:, 0:W], -1.0, late[:, 0:W], ALU.mult, ALU.max)
        nc.scalar.activation(late[:, W:], late[:, W:], ACT.Abs, bias=zero_bias[:])
        nc.sync.dma_start(out=out[P * 3 :, halves[1]], in_=late)
